import numpy as np
import ml_dtypes


def mxq(x, axis, fmt="e4m3"):
    dtype, down = {"e4m3": (ml_dtypes.float8_e4m3fn, 7), "e5m2": (ml_dtypes.float8_e5m2, 14)}[fmt]
    v = np.moveaxis(np.asarray(x, np.float32).astype(ml_dtypes.bfloat16).astype(np.float64), axis, -1)
    blocks = v.reshape(v.shape[:-1] + (-1, 32))
    amax = np.abs(blocks).max(-1, keepdims=True)
    byte = np.maximum(np.where(amax > 0, np.frexp(amax)[1] - 1 + 127, 0) - down, 1)
    scale = np.exp2(byte - 127.0)
    codes = (blocks / scale).astype(np.float32).astype(dtype).astype(np.float64)
    return np.moveaxis((codes * scale).reshape(v.shape), -1, axis)


WIDE = False


def mx_kscale(k):
    if not WIDE:
        return np.ones(k)
    levels = np.array([10, -10, 5, -5, 0])
    if k % 512:
        return np.exp2(np.random.permutation(np.resize(levels, k // 32))).repeat(32)
    a = np.empty((k // 512, 16))
    for p in range(k // 512):
        a[p, :8] = np.random.permutation(np.resize(levels, 8))
        for g in range(8):
            far = levels[np.abs(levels - a[p, g]) >= 10]
            a[p, g + 8] = far[np.random.randint(len(far))]
    return np.exp2(a.ravel()).repeat(32)


def f64(x):
    return np.asarray(x).astype(np.float64)


def striped(idx):
    return np.tile(idx.reshape(-1, 16).T, (8, 1)).astype(np.uint16)


def unstriped(offs):
    return offs[:16].T.reshape(-1).astype(np.int64)


def pack_weight(w):
    k, n = w.shape
    w = f64(np.asarray(w, np.float32).astype(ml_dtypes.bfloat16)).reshape(k // 32, 32, n)
    amax = np.abs(w).max(1)
    byte = np.clip(np.where(amax > 0, np.frexp(amax)[1] - 1 + 127 - 7, 1), 1, 254)
    scaled = (w * np.exp2(127.0 - byte)[:, None, :]).reshape(k, n).astype(np.float32)
    words = np.ascontiguousarray(scaled.reshape(k // 512, 128, 4, n).transpose(0, 1, 3, 2)).astype(ml_dtypes.float8_e4m3fn).view(np.uint8)
    return words, np.ascontiguousarray(byte.astype(np.uint8).reshape(k // 512, 16, n))


def unpack_weight(words, scales):
    g, p, n, _ = words.shape
    vals = np.ascontiguousarray(words).view(ml_dtypes.float8_e4m3fn).astype(np.float64) * np.repeat(np.exp2(scales.astype(np.float64) - 127.0), 8, axis=1)[..., None]
    return vals.transpose(0, 1, 3, 2).reshape(g * 512, n)


E2M1 = np.array([0.0, 0.5, 1.0, 1.5, 2.0, 3.0, 4.0, 6.0, -0.0, -0.5, -1.0, -1.5, -2.0, -3.0, -4.0, -6.0])


def pack_fp4(w):
    k, n = w.shape
    w = f64(np.asarray(w, np.float32).astype(ml_dtypes.bfloat16)).reshape(k // 32, 32, n)
    amax = np.abs(w).max(1)
    mant, ex = np.frexp(amax / 6.0)
    byte = np.clip(np.where(amax > 0, np.where(mant > 0.5, ex, ex - 1) + 127, 1), 1, 254)
    scaled = (w * np.exp2(127.0 - byte)[:, None, :]).reshape(k, n).astype(np.float32)
    c = np.ascontiguousarray(scaled.reshape(k // 512, 128, 4, n).transpose(0, 1, 3, 2)).astype(ml_dtypes.float4_e2m1fn).view(np.uint8) & 0xF
    words = (c[..., 0::2] | (c[..., 1::2] << 4)).reshape(k // 512, 128, 2 * n)
    return np.ascontiguousarray(words), np.ascontiguousarray(byte.astype(np.uint8).reshape(k // 512, 16, n))


def unpack_fp4(words, scales):
    g, _, n = scales.shape
    words = np.ascontiguousarray(words).reshape(g, 128, n, 2)
    nib = np.empty((g, 128, n, 4), np.uint8)
    nib[..., 0::2] = words & 0xF
    nib[..., 1::2] = words >> 4
    vals = E2M1[nib] * np.repeat(np.exp2(scales.astype(np.float64) - 127.0), 8, axis=1)[..., None]
    return vals.transpose(0, 1, 3, 2).reshape(g * 512, n)


def gelu(v):
    return 0.5 * v * (1.0 + np.tanh(np.sqrt(2.0 / np.pi) * (v + 0.044715 * v**3)))


K, T, S, D, V, H, N, U = 1024, 2048, 1024, 3, 512, 512, 128, 256
P = 2 ** 7


def setup_inputs():
    n = np.random.standard_normal
    s = mx_kscale(K)[:, None]
    u = mx_kscale(H)
    near = np.random.permutation(S)
    next_ = np.random.permutation(V)
    packed_xT = pack_weight(n((K, T)) * s)
    packed_w2 = pack_fp4(n((H, N)) / np.sqrt(H) / u[:, None])
    return {
        "x_words": packed_xT[0],
        "x_scales": packed_xT[1],
        "w1": (n((K, H)) / np.sqrt(K) / s * u).astype(np.float32),
        "w2_words": packed_w2[0],
        "w2_scales": packed_w2[1],
        "gate": (np.tile(np.random.uniform(0.2, 1.0, (D, 1, V)) / np.sqrt(D), (1, P, 1))).astype(np.float32),
        "gate2": (np.tile(np.random.uniform(0.2, 1.0, (D, 1, U)) / np.sqrt(D), (1, P, 1))).astype(np.float32),
        "offs": striped(np.random.permutation(T)[:S]),
        "cen": striped(np.random.permutation(S)[:V]),
        "pos1": striped(near[:V]),
        "pos2": striped(near[V:]),
        "pos3": striped(np.random.permutation(S)[:V]),
        "nxt1": striped(next_[:U]),
        "nxt2": striped(next_[U:]),
        "nxt3": striped(np.random.permutation(V)[:U]),
        "root": striped(np.random.permutation(S)[:U]),
    }


def reference(x_words, x_scales, w1, w2_words, w2_scales, gate, gate2, offs, cen, pos1, pos2, pos3, nxt1, nxt2, nxt3, root):
    xq = unpack_weight(x_words, x_scales)[:, unstriped(offs)]
    h = gelu(mxq(f64(w1), 0, "e4m3").T @ xq)
    y = unpack_fp4(w2_words, w2_scales).T @ mxq(h, 0, "e4m3")
    z = 0.8 * (y[:, unstriped(pos1)] * f64(gate)[0, :1] + y[:, unstriped(pos2)] * f64(gate)[1, :1] + y[:, unstriped(pos3)] * f64(gate)[2, :1]) + 0.2 * y[:, unstriped(cen)]
    return 0.8 * (z[:, unstriped(nxt1)] * f64(gate2)[0, :1] + z[:, unstriped(nxt2)] * f64(gate2)[1, :1] + z[:, unstriped(nxt3)] * f64(gate2)[2, :1]) + 0.2 * y[:, unstriped(root)]

@@ -1,0 +1,174 @@
+from contextlib import ExitStack
+
+import concourse.mybir as mybir
+
+K, T, S, D, V, H, N, U = 1024, 2048, 1024, 3, 512, 512, 128, 256
+FLOPS = 2 * K * H * S + 2 * H * N * S
+
+F32 = mybir.dt.float32
+BF16 = mybir.dt.bfloat16
+I32 = mybir.dt.int32
+U32 = mybir.dt.uint32
+U16 = mybir.dt.uint16
+U8 = mybir.dt.uint8
+FP8X4 = mybir.dt.float8_e4m3fn_x4
+FP4X4 = mybir.dt.float4_e2m1fn_x4
+MULT = mybir.AluOpType.mult
+ADD = mybir.AluOpType.add
+COPY = mybir.ActivationFunctionType.Copy
+GELU = mybir.ActivationFunctionType.Gelu_apprx_tanh
+
+P = 128
+PACK = 4
+PASSES = K // (P * PACK)
+BLK = 128
+SLICE = 256
+H_STRETCHES = [256,256,256,128,128]
+SCALAR_HALVES = [2,1]
+
+
+def tile_picked_zappnp_gelu_p_kernel(tc, x_words, x_scales, w1, w2_words, w2_scales, gate, gate2, offs, cen, pos1, pos2, pos3, nxt1, nxt2, nxt3, root, out):
+    nc = tc.nc
+    with ExitStack() as ctx:
+        keep = ctx.enter_context(tc.tile_pool(name="keep", bufs=1))
+        hps = ctx.enter_context(tc.psum_pool(name="hps", bufs=5))
+        yps = ctx.enter_context(tc.psum_pool(name="yps", bufs=3))
+
+        def load_list(name, src):
+            t = keep.tile([P, src.shape[1]], U16, name=name)
+            nc.sync.dma_start(t[:], src)
+            return t
+
+        xs_win = keep.tile([P, T], U8, name="xs_win", align_bytes=64)
+        nc.vector.memset(xs_win[:].bitcast(I32), 0)
+        w2s = keep.tile([P, N], U8, name="w2s", align_bytes=64)
+        nc.vector.memset(w2s[:].bitcast(I32), 0)
+        warm_in = keep.tile([P, 8], F32, name="warm_in")
+        nc.vector.memset(warm_in[:], 0.0)
+        warm_out = keep.tile([P, 8], F32, name="warm_out")
+        nc.scalar.activation(warm_out[:], warm_in[:], GELU)
+
+        def load_w1(g):
+            t = keep.tile([P, PACK, H], F32, name=f"w1raw{g}")
+            nc.sync.dma_start(t[:], w1[512 * g : 512 * (g + 1), :].rearrange("(p j) c -> p j c", j=PACK))
+            return t
+
+        def load_x(g):
+            t = keep.tile([P, T], I32, name=f"xwin{g}", align_bytes=64)
+            nc.sync.dma_start(t[:], x_words[g].rearrange("p n t -> p (n t)").bitcast(I32))
+            return t
+
+        offs_t = load_list("offs_t", offs)
+        w1first = keep.tile([P, PACK, H], F32, name="w1raw0")
+        w1rows = w1[0:512, :].rearrange("(p j) c -> p j c", j=PACK)
+        nc.sync.dma_start(w1first[:, 0, :], w1rows[:, 0, :])
+        for q in range(4):
+            nc.sync.dma_start(xs_win[32 * q : 32 * q + 8, :].bitcast(I32), x_scales[:, 4 * q : 4 * q + 4, :].bitcast(I32))
+        for j in range(1, PACK):
+            nc.sync.dma_start(w1first[:, j, :], w1rows[:, j, :])
+        w1raw = [w1first]
+        w1raw.append(load_w1(1))
+        xwin = [load_x(0), load_x(1)]
+
+        w2w = keep.tile([P, 2 * N], U8, name="w2w", align_bytes=64)
+        nc.sync.dma_start(w2w[:].bitcast(I32), w2_words[0].bitcast(I32))
+        for q in range(4):
+            nc.sync.dma_start(w2s[32 * q : 32 * q + 4, :].bitcast(I32), w2_scales[0, 4 * q : 4 * q + 4, :].bitcast(I32))
+        pos_t = [load_list(f"pos{d}", src) for d, src in enumerate((pos1, pos2, pos3))]
+        g1 = keep.tile([P, D, V], F32, name="g1")
+        nc.sync.dma_start(g1[:], gate.rearrange("d p v -> p d v"))
+        cen_t = load_list("cen_t", cen)
+        nxt_t = [load_list(f"nxt{d}", src) for d, src in enumerate((nxt1, nxt2, nxt3))]
+        root_t = load_list("root_t", root)
+        g2 = keep.tile([P, D, U], F32, name="g2")
+        nc.sync.dma_start(g2[:], gate2.rearrange("d p v -> p d v"))
+
+        xs = keep.tile([P, S], U8, name="xs", align_bytes=64)
+        nc.vector.tensor_copy(xs[:], xs_win[:].indirect(offs_t[:]))
+
+        w1c = {}
+        w1s = {}
+        for g in range(PASSES):
+            src = w1raw[g][:].rearrange("p j (m t) -> p m t j", t=PACK)
+            halves = []
+            for hf in range(2):
+                grp = keep.tile([P, 2, P, PACK], BF16, name=f"w1b{g}{hf}", align_bytes=64)
+                dst = grp[:].rearrange("p t m j -> p m t j")
+                if hf < SCALAR_HALVES[g]:
+                    nc.scalar.copy(dst, src[:, :, 2 * hf : 2 * hf + 2, :])
+                else:
+                    nc.vector.tensor_copy(dst, src[:, :, 2 * hf : 2 * hf + 2, :])
+                halves.append(grp)
+            for hf in range(2):
+                c = keep.tile([P, 2 * P], U32, name=f"w1c{g}{hf}", align_bytes=64)
+                s = keep.tile([P, 2 * P], U8, name=f"w1s{g}{hf}", align_bytes=64)
+                nc.vector.quantize_mx(out=c[:].bitcast(FP8X4), scales=s[:], in_=halves[hf][:].rearrange("p t m j -> p (t m j)"))
+                for tt in range(2):
+                    w1c[(g, 2 * hf + tt)] = c[:, tt * P : (tt + 1) * P]
+                    w1s[(g, 2 * hf + tt)] = s[:, tt * P : (tt + 1) * P]
+
+        x0 = []
+        warm_bank = yps.tile([P, SLICE], F32, name="ybank")
+        for sl in range(S // SLICE):
+            t = keep.tile([P, SLICE], U32, name=f"x0_{sl}", align_bytes=64)
+            nc.vector.tensor_copy(t[:], xwin[0][:].bitcast(U32).indirect(offs_t[:, sl * SLICE // 16 : (sl + 1) * SLICE // 16]))
+            x0.append(t)
+            nc.tensor.matmul_mx(out=warm_bank[:], lhsT=w1c[(0, 0)].bitcast(FP8X4), lhsT_scale=w1s[(0, 0)], rhs=t[:].bitcast(FP8X4), rhs_scale=xs[:, sl * SLICE : (sl + 1) * SLICE], start=True, stop=True)
+        ywin = keep.tile([P, S], F32, name="ywin")
+        x1 = []
+        for sl in range(S // SLICE):
+            t = keep.tile([P, SLICE], U32, name=f"x1_{sl}", align_bytes=64)
+            nc.vector.tensor_copy(t[:], xwin[1][:].bitcast(U32).indirect(offs_t[:, sl * SLICE // 16 : (sl + 1) * SLICE // 16]))
+            x1.append(t)
+
+        hbs = []
+        c0 = 0
+        for i, width in enumerate(H_STRETCHES):
+            hb = keep.tile([P, width, PACK], BF16, name=f"hb{i}", align_bytes=64)
+            hbs.append(hb)
+            for b0 in range(0, width, BLK):
+                n0 = c0 + b0
+                bank = hps.tile([P, PACK, BLK], F32, name="hbank")
+                for t in range(PACK):
+                    for g in range(PASSES):
+                        words = (x0, x1)[g][n0 // SLICE][:, n0 % SLICE : n0 % SLICE + BLK]
+                        nc.tensor.matmul_mx(
+                            out=bank[:, t, :],
+                            lhsT=w1c[(g, t)].bitcast(FP8X4),
+                            lhsT_scale=w1s[(g, t)],
+                            rhs=words.bitcast(FP8X4),
+                            rhs_scale=xs[4 * g : P, n0 : n0 + BLK],
+                            start=(g == 0),
+                            stop=(g == PASSES - 1),
+                        )
+                nc.scalar.activation(hb[:, b0 : b0 + BLK, :], bank[:].rearrange("p t n -> p n t"), GELU)
+            hc = keep.tile([P, width], U32, name=f"hc{i}", align_bytes=64)
+            hs = keep.tile([P, width], U8, name=f"hs{i}", align_bytes=64)
+            nc.vector.quantize_mx(out=hc[:].bitcast(FP8X4), scales=hs[:], in_=hb[:].rearrange("p n t -> p (n t)"))
+            ybank = yps.tile([P, width], F32, name="ybank")
+            nc.tensor.matmul_mx(out=ybank[:], lhsT=w2w[:].bitcast(FP4X4), lhsT_scale=w2s[:], rhs=hc[:].bitcast(FP8X4), rhs_scale=hs[:], start=True, stop=True)
+            nc.vector.tensor_scalar(ywin[:, c0 : c0 + width], ybank[:], 0.64, None, MULT)
+            c0 = c0 + width
+
+        ycen = keep.tile([P, S], F32, name="ycen")
+        nc.scalar.activation(ycen[:], ywin[:], COPY, scale=0.25)
+        yroot = keep.tile([P, S], F32, name="yroot")
+        nc.scalar.activation(yroot[:], ywin[:], COPY, scale=0.3125)
+
+        def step(tag, window, lists, gates, own_window, own_list, width):
+            a = []
+            for d in range(D):
+                t = keep.tile([P, width], F32, name=f"{tag}a{d}")
+                nc.vector.tensor_tensor(t[:], window[:].indirect(lists[d][:]), gates[:, d, :], MULT)
+                a.append(t)
+            s01 = keep.tile([P, width], F32, name=f"{tag}s01")
+            nc.vector.tensor_tensor(s01[:], a[0][:], a[1][:], ADD)
+            s2 = keep.tile([P, width], F32, name=f"{tag}s2")
+            nc.vector.tensor_tensor(s2[:], own_window[:].indirect(own_list[:]), a[2][:], ADD)
+            res = keep.tile([P, width], F32, name=f"{tag}res")
+            nc.vector.tensor_tensor(res[:], s01[:], s2[:], ADD)
+            return res
+
+        z = step("z", ywin, pos_t, g1, ycen, cen_t, V)
+        o = step("o", z, nxt_t, g2, yroot, root_t, U)
+        nc.sync.dma_start(out, o[:])

@@ -24,29 +24,20 @@ PASSES = K // (P * PACK)
 BLK = 128
 SLICE = 256
 H_STRETCHES = [256,256,256,128,128]
-SCALAR_HALVES = [2,1]
 
 
 def tile_picked_zappnp_gelu_p_kernel(tc, x_words, x_scales, w1, w2_words, w2_scales, gate, gate2, offs, cen, pos1, pos2, pos3, nxt1, nxt2, nxt3, root, out):
     nc = tc.nc
     with ExitStack() as ctx:
         keep = ctx.enter_context(tc.tile_pool(name="keep", bufs=1))
-        hps = ctx.enter_context(tc.psum_pool(name="hps", bufs=5))
-        yps = ctx.enter_context(tc.psum_pool(name="yps", bufs=3))
+        reuse = ctx.enter_context(tc.tile_pool(name="reuse", bufs=1))
+        hps = ctx.enter_context(tc.psum_pool(name="hps", bufs=6))
+        yps = ctx.enter_context(tc.psum_pool(name="yps", bufs=2))
 
         def load_list(name, src):
             t = keep.tile([P, src.shape[1]], U16, name=name)
             nc.sync.dma_start(t[:], src)
             return t
-
-        xs_win = keep.tile([P, T], U8, name="xs_win", align_bytes=64)
-        nc.vector.memset(xs_win[:].bitcast(I32), 0)
-        w2s = keep.tile([P, N], U8, name="w2s", align_bytes=64)
-        nc.vector.memset(w2s[:].bitcast(I32), 0)
-        warm_in = keep.tile([P, 8], F32, name="warm_in")
-        nc.vector.memset(warm_in[:], 0.0)
-        warm_out = keep.tile([P, 8], F32, name="warm_out")
-        nc.scalar.activation(warm_out[:], warm_in[:], GELU)
 
         def load_w1(g):
             t = keep.tile([P, PACK, H], F32, name=f"w1raw{g}")
@@ -58,17 +49,18 @@ def tile_picked_zappnp_gelu_p_kernel(tc, x_words, x_scales, w1, w2_words, w2_sca
             nc.sync.dma_start(t[:], x_words[g].rearrange("p n t -> p (n t)").bitcast(I32))
             return t
 
-        offs_t = load_list("offs_t", offs)
-        w1first = keep.tile([P, PACK, H], F32, name="w1raw0")
-        w1rows = w1[0:512, :].rearrange("(p j) c -> p j c", j=PACK)
-        nc.sync.dma_start(w1first[:, 0, :], w1rows[:, 0, :])
+        WIN = 4096
+        xs_win = reuse.tile([P, T], U8, name="xs_win", align_bytes=64, offset=WIN)
+        nc.gpsimd.memset(xs_win[:].bitcast(I32), 0)
         for q in range(4):
-            nc.sync.dma_start(xs_win[32 * q : 32 * q + 8, :].bitcast(I32), x_scales[:, 4 * q : 4 * q + 4, :].bitcast(I32))
-        for j in range(1, PACK):
-            nc.sync.dma_start(w1first[:, j, :], w1rows[:, j, :])
-        w1raw = [w1first]
-        w1raw.append(load_w1(1))
-        xwin = [load_x(0), load_x(1)]
+            nc.gpsimd.dma_start(xs_win[32 * q : 32 * q + 8, :].bitcast(I32), x_scales[:, 4 * q : 4 * q + 4, :].bitcast(I32))
+        w2s = keep.tile([P, N], U8, name="w2s", align_bytes=64)
+        nc.vector.memset(w2s[:].bitcast(I32), 0)
+
+        offs_t = load_list("offs_t", offs)
+        xwin = [load_x(0)]
+        w1raw = [load_w1(0), load_w1(1)]
+        xwin.append(load_x(1))
 
         w2w = keep.tile([P, 2 * N], U8, name="w2w", align_bytes=64)
         nc.sync.dma_start(w2w[:].bitcast(I32), w2_words[0].bitcast(I32))
@@ -83,6 +75,8 @@ def tile_picked_zappnp_gelu_p_kernel(tc, x_words, x_scales, w1, w2_words, w2_sca
         g2 = keep.tile([P, D, U], F32, name="g2")
         nc.sync.dma_start(g2[:], gate2.rearrange("d p v -> p d v"))
 
+        x0 = keep.tile([P, S], U32, name="x0", align_bytes=64)
+        nc.vector.tensor_copy(x0[:], xwin[0][:].bitcast(U32).indirect(offs_t[:]))
         xs = keep.tile([P, S], U8, name="xs", align_bytes=64)
         nc.vector.tensor_copy(xs[:], xs_win[:].indirect(offs_t[:]))
 
@@ -92,34 +86,29 @@ def tile_picked_zappnp_gelu_p_kernel(tc, x_words, x_scales, w1, w2_words, w2_sca
             src = w1raw[g][:].rearrange("p j (m t) -> p m t j", t=PACK)
             halves = []
             for hf in range(2):
-                grp = keep.tile([P, 2, P, PACK], BF16, name=f"w1b{g}{hf}", align_bytes=64)
-                dst = grp[:].rearrange("p t m j -> p m t j")
-                if hf < SCALAR_HALVES[g]:
-                    nc.scalar.copy(dst, src[:, :, 2 * hf : 2 * hf + 2, :])
+                last = (g, hf) == (1, 1)
+                if last:
+                    grp = reuse.tile([P, 2, P, PACK], BF16, name=f"w1b{g}{hf}", align_bytes=64, offset=WIN + 64 + 4 * 256)
                 else:
+                    grp = keep.tile([P, 2, P, PACK], BF16, name=f"w1b{g}{hf}", align_bytes=64)
+                dst = grp[:].rearrange("p t m j -> p m t j")
+                if last:
                     nc.vector.tensor_copy(dst, src[:, :, 2 * hf : 2 * hf + 2, :])
+                else:
+                    nc.scalar.copy(dst, src[:, :, 2 * hf : 2 * hf + 2, :])
                 halves.append(grp)
             for hf in range(2):
                 c = keep.tile([P, 2 * P], U32, name=f"w1c{g}{hf}", align_bytes=64)
-                s = keep.tile([P, 2 * P], U8, name=f"w1s{g}{hf}", align_bytes=64)
+                s = reuse.tile([P, 2 * P], U8, name=f"w1s{g}{hf}", align_bytes=64, offset=WIN + 64 + (2 * g + hf) * 256)
                 nc.vector.quantize_mx(out=c[:].bitcast(FP8X4), scales=s[:], in_=halves[hf][:].rearrange("p t m j -> p (t m j)"))
                 for tt in range(2):
                     w1c[(g, 2 * hf + tt)] = c[:, tt * P : (tt + 1) * P]
                     w1s[(g, 2 * hf + tt)] = s[:, tt * P : (tt + 1) * P]
 
-        x0 = []
-        warm_bank = yps.tile([P, SLICE], F32, name="ybank")
-        for sl in range(S // SLICE):
-            t = keep.tile([P, SLICE], U32, name=f"x0_{sl}", align_bytes=64)
-            nc.vector.tensor_copy(t[:], xwin[0][:].bitcast(U32).indirect(offs_t[:, sl * SLICE // 16 : (sl + 1) * SLICE // 16]))
-            x0.append(t)
-            nc.tensor.matmul_mx(out=warm_bank[:], lhsT=w1c[(0, 0)].bitcast(FP8X4), lhsT_scale=w1s[(0, 0)], rhs=t[:].bitcast(FP8X4), rhs_scale=xs[:, sl * SLICE : (sl + 1) * SLICE], start=True, stop=True)
         ywin = keep.tile([P, S], F32, name="ywin")
-        x1 = []
+        x1 = reuse.tile([P, S], U32, name="x1", align_bytes=64, offset=64)
         for sl in range(S // SLICE):
-            t = keep.tile([P, SLICE], U32, name=f"x1_{sl}", align_bytes=64)
-            nc.vector.tensor_copy(t[:], xwin[1][:].bitcast(U32).indirect(offs_t[:, sl * SLICE // 16 : (sl + 1) * SLICE // 16]))
-            x1.append(t)
+            nc.vector.tensor_copy(x1[:, sl * SLICE : (sl + 1) * SLICE], xwin[1][:].bitcast(U32).indirect(offs_t[:, sl * SLICE // 16 : (sl + 1) * SLICE // 16]))
 
         hbs = []
         c0 = 0
@@ -131,12 +120,11 @@ def tile_picked_zappnp_gelu_p_kernel(tc, x_words, x_scales, w1, w2_words, w2_sca
                 bank = hps.tile([P, PACK, BLK], F32, name="hbank")
                 for t in range(PACK):
                     for g in range(PASSES):
-                        words = (x0, x1)[g][n0 // SLICE][:, n0 % SLICE : n0 % SLICE + BLK]
                         nc.tensor.matmul_mx(
                             out=bank[:, t, :],
                             lhsT=w1c[(g, t)].bitcast(FP8X4),
                             lhsT_scale=w1s[(g, t)],
-                            rhs=words.bitcast(FP8X4),
+                            rhs=(x0, x1)[g][:, n0 : n0 + BLK].bitcast(FP8X4),
                             rhs_scale=xs[4 * g : P, n0 : n0 + BLK],
                             start=(g == 0),
                             stop=(g == PASSES - 1),

@@ -1,6 +1,7 @@
 from contextlib import ExitStack
 
 import concourse.mybir as mybir
+from concourse.masks import make_identity
 
 K, T, S, D, V, H, N, U = 1024, 2048, 1024, 3, 512, 512, 128, 256
 FLOPS = 2 * K * H * S + 2 * H * N * S
@@ -24,20 +25,29 @@ PASSES = K // (P * PACK)
 BLK = 128
 SLICE = 256
 H_STRETCHES = [256,256,256,128,128]
+SCALAR_HALVES = [1,1]
 
 
 def tile_picked_zappnp_gelu_p_kernel(tc, x_words, x_scales, w1, w2_words, w2_scales, gate, gate2, offs, cen, pos1, pos2, pos3, nxt1, nxt2, nxt3, root, out):
     nc = tc.nc
     with ExitStack() as ctx:
         keep = ctx.enter_context(tc.tile_pool(name="keep", bufs=1))
-        reuse = ctx.enter_context(tc.tile_pool(name="reuse", bufs=1))
-        hps = ctx.enter_context(tc.psum_pool(name="hps", bufs=6))
-        yps = ctx.enter_context(tc.psum_pool(name="yps", bufs=2))
+        hps = ctx.enter_context(tc.psum_pool(name="hps", bufs=5))
+        yps = ctx.enter_context(tc.psum_pool(name="yps", bufs=3))
 
         def load_list(name, src):
             t = keep.tile([P, src.shape[1]], U16, name=name)
             nc.sync.dma_start(t[:], src)
             return t
+
+        xs_win = keep.tile([P, T], U8, name="xs_win", align_bytes=64)
+        nc.vector.memset(xs_win[:].bitcast(I32), 0)
+        w2s = keep.tile([P, N], U8, name="w2s", align_bytes=64)
+        nc.vector.memset(w2s[:].bitcast(I32), 0)
+        warm_in = keep.tile([P, 8], F32, name="warm_in")
+        nc.vector.memset(warm_in[:], 0.0)
+        warm_out = keep.tile([P, 8], F32, name="warm_out")
+        nc.scalar.activation(warm_out[:], warm_in[:], GELU)
 
         def load_w1(g):
             t = keep.tile([P, PACK, H], F32, name=f"w1raw{g}")
@@ -49,24 +59,26 @@ def tile_picked_zappnp_gelu_p_kernel(tc, x_words, x_scales, w1, w2_words, w2_sca
             nc.sync.dma_start(t[:], x_words[g].rearrange("p n t -> p (n t)").bitcast(I32))
             return t
 
-        WIN = 4096
-        xs_win = reuse.tile([P, T], U8, name="xs_win", align_bytes=64, offset=WIN)
-        nc.gpsimd.memset(xs_win[:].bitcast(I32), 0)
-        for q in range(4):
-            nc.gpsimd.dma_start(xs_win[32 * q : 32 * q + 8, :].bitcast(I32), x_scales[:, 4 * q : 4 * q + 4, :].bitcast(I32))
-        w2s = keep.tile([P, N], U8, name="w2s", align_bytes=64)
-        nc.vector.memset(w2s[:].bitcast(I32), 0)
-
+        ident = keep.tile([P, P], F32, name="ident")
+        make_identity(nc, ident[:])
         offs_t = load_list("offs_t", offs)
-        xwin = [load_x(0)]
-        w1raw = [load_w1(0), load_w1(1)]
-        xwin.append(load_x(1))
-
+        for q in range(4):
+            nc.sync.dma_start(xs_win[32 * q : 32 * q + 8, :].bitcast(I32), x_scales[:, 4 * q : 4 * q + 4, :].bitcast(I32))
+        w1first = keep.tile([P, PACK, H], F32, name="w1raw0")
+        w1rows = w1[0:512, :].rearrange("(p j) c -> p j c", j=PACK)
+        for j in range(0, PACK, 2):
+            nc.sync.dma_start(w1first[:, j : j + 2, :], w1rows[:, j : j + 2, :])
+        w1raw = [w1first]
         w2w = keep.tile([P, 2 * N], U8, name="w2w", align_bytes=64)
         nc.sync.dma_start(w2w[:].bitcast(I32), w2_words[0].bitcast(I32))
+        pos_t = [load_list("pos0", pos1)]
+        xwin = [load_x(0)]
+        w1raw.append(load_w1(1))
+        xwin.append(load_x(1))
+
         for q in range(4):
             nc.sync.dma_start(w2s[32 * q : 32 * q + 4, :].bitcast(I32), w2_scales[0, 4 * q : 4 * q + 4, :].bitcast(I32))
-        pos_t = [load_list(f"pos{d}", src) for d, src in enumerate((pos1, pos2, pos3))]
+        pos_t.extend([load_list("pos1", pos2), load_list("pos2", pos3)])
         g1 = keep.tile([P, D, V], F32, name="g1")
         nc.sync.dma_start(g1[:], gate.rearrange("d p v -> p d v"))
         cen_t = load_list("cen_t", cen)
@@ -75,10 +87,14 @@ def tile_picked_zappnp_gelu_p_kernel(tc, x_words, x_scales, w1, w2_words, w2_sca
         g2 = keep.tile([P, D, U], F32, name="g2")
         nc.sync.dma_start(g2[:], gate2.rearrange("d p v -> p d v"))
 
-        x0 = keep.tile([P, S], U32, name="x0", align_bytes=64)
-        nc.vector.tensor_copy(x0[:], xwin[0][:].bitcast(U32).indirect(offs_t[:]))
         xs = keep.tile([P, S], U8, name="xs", align_bytes=64)
         nc.vector.tensor_copy(xs[:], xs_win[:].indirect(offs_t[:]))
+
+        x0 = keep.tile([P, S], U32, name="x0", align_bytes=64)
+        warm_bank = yps.tile([P, 512], F32, name="ybank")
+
+        def warm_pass(g, t, c0, width):
+            nc.tensor.matmul_mx(out=warm_bank[:, 0:width], lhsT=w1c[(g, t)].bitcast(FP8X4), lhsT_scale=w1s[(g, t)], rhs=x0[:, c0 : c0 + width].bitcast(FP8X4), rhs_scale=xs[:, c0 : c0 + width], start=True, stop=True)
 
         w1c = {}
         w1s = {}
@@ -86,77 +102,118 @@ def tile_picked_zappnp_gelu_p_kernel(tc, x_words, x_scales, w1, w2_words, w2_sca
             src = w1raw[g][:].rearrange("p j (m t) -> p m t j", t=PACK)
             halves = []
             for hf in range(2):
-                last = (g, hf) == (1, 1)
-                if last:
-                    grp = reuse.tile([P, 2, P, PACK], BF16, name=f"w1b{g}{hf}", align_bytes=64, offset=WIN + 64 + 4 * 256)
-                else:
-                    grp = keep.tile([P, 2, P, PACK], BF16, name=f"w1b{g}{hf}", align_bytes=64)
+                grp = keep.tile([P, 2, P, PACK], BF16, name=f"w1b{g}{hf}", align_bytes=64)
                 dst = grp[:].rearrange("p t m j -> p m t j")
-                if last:
-                    nc.vector.tensor_copy(dst, src[:, :, 2 * hf : 2 * hf + 2, :])
-                else:
+                if hf < SCALAR_HALVES[g]:
                     nc.scalar.copy(dst, src[:, :, 2 * hf : 2 * hf + 2, :])
+                else:
+                    nc.vector.tensor_copy(dst, src[:, :, 2 * hf : 2 * hf + 2, :])
                 halves.append(grp)
-            for hf in range(2):
+            for hf in (1, 0):
                 c = keep.tile([P, 2 * P], U32, name=f"w1c{g}{hf}", align_bytes=64)
-                s = reuse.tile([P, 2 * P], U8, name=f"w1s{g}{hf}", align_bytes=64, offset=WIN + 64 + (2 * g + hf) * 256)
+                s = keep.tile([P, 2 * P], U8, name=f"w1s{g}{hf}", align_bytes=64)
                 nc.vector.quantize_mx(out=c[:].bitcast(FP8X4), scales=s[:], in_=halves[hf][:].rearrange("p t m j -> p (t m j)"))
                 for tt in range(2):
                     w1c[(g, 2 * hf + tt)] = c[:, tt * P : (tt + 1) * P]
                     w1s[(g, 2 * hf + tt)] = s[:, tt * P : (tt + 1) * P]
+                if g == 1:
+                    warm_pass(1, 2 * hf, 0, 512)
+            if g == 0:
+                for sl in range(S // SLICE):
+                    nc.vector.tensor_copy(x0[:, sl * SLICE : (sl + 1) * SLICE], xwin[0][:].bitcast(U32).indirect(offs_t[:, sl * SLICE // 16 : (sl + 1) * SLICE // 16]))
+                    if sl > 0:
+                        warm_pass(0, 0, sl * SLICE, SLICE)
+                warm_pass(0, 1, 3 * SLICE, SLICE)
 
         ywin = keep.tile([P, S], F32, name="ywin")
-        x1 = reuse.tile([P, S], U32, name="x1", align_bytes=64, offset=64)
+        x1 = []
         for sl in range(S // SLICE):
-            nc.vector.tensor_copy(x1[:, sl * SLICE : (sl + 1) * SLICE], xwin[1][:].bitcast(U32).indirect(offs_t[:, sl * SLICE // 16 : (sl + 1) * SLICE // 16]))
+            t = keep.tile([P, SLICE], U32, name=f"x1_{sl}", align_bytes=64)
+            nc.vector.tensor_copy(t[:], xwin[1][:].bitcast(U32).indirect(offs_t[:, sl * SLICE // 16 : (sl + 1) * SLICE // 16]))
+            x1.append(t)
 
         hbs = []
-        c0 = 0
-        for i, width in enumerate(H_STRETCHES):
+        starts = [sum(H_STRETCHES[:i]) for i in range(len(H_STRETCHES))]
+
+        def first_layer(i):
+            width = H_STRETCHES[i]
             hb = keep.tile([P, width, PACK], BF16, name=f"hb{i}", align_bytes=64)
             hbs.append(hb)
             for b0 in range(0, width, BLK):
-                n0 = c0 + b0
+                n0 = starts[i] + b0
                 bank = hps.tile([P, PACK, BLK], F32, name="hbank")
                 for t in range(PACK):
                     for g in range(PASSES):
+                        words = x0[:, n0 : n0 + BLK] if g == 0 else x1[n0 // SLICE][:, n0 % SLICE : n0 % SLICE + BLK]
                         nc.tensor.matmul_mx(
                             out=bank[:, t, :],
                             lhsT=w1c[(g, t)].bitcast(FP8X4),
                             lhsT_scale=w1s[(g, t)],
-                            rhs=(x0, x1)[g][:, n0 : n0 + BLK].bitcast(FP8X4),
+                            rhs=words.bitcast(FP8X4),
                             rhs_scale=xs[4 * g : P, n0 : n0 + BLK],
                             start=(g == 0),
                             stop=(g == PASSES - 1),
                         )
                 nc.scalar.activation(hb[:, b0 : b0 + BLK, :], bank[:].rearrange("p t n -> p n t"), GELU)
+
+        def second_layer(i):
+            width = H_STRETCHES[i]
             hc = keep.tile([P, width], U32, name=f"hc{i}", align_bytes=64)
             hs = keep.tile([P, width], U8, name=f"hs{i}", align_bytes=64)
-            nc.vector.quantize_mx(out=hc[:].bitcast(FP8X4), scales=hs[:], in_=hb[:].rearrange("p n t -> p (n t)"))
+            nc.vector.quantize_mx(out=hc[:].bitcast(FP8X4), scales=hs[:], in_=hbs[i][:].rearrange("p n t -> p (n t)"))
             ybank = yps.tile([P, width], F32, name="ybank")
             nc.tensor.matmul_mx(out=ybank[:], lhsT=w2w[:].bitcast(FP4X4), lhsT_scale=w2s[:], rhs=hc[:].bitcast(FP8X4), rhs_scale=hs[:], start=True, stop=True)
-            nc.vector.tensor_scalar(ywin[:, c0 : c0 + width], ybank[:], 0.64, None, MULT)
-            c0 = c0 + width
+            nc.vector.tensor_scalar(ywin[:, starts[i] : starts[i] + width], ybank[:], 0.64, None, MULT)
+
+        for i in range(len(H_STRETCHES)):
+            first_layer(i)
+        for i in range(len(H_STRETCHES)):
+            second_layer(i)
 
         ycen = keep.tile([P, S], F32, name="ycen")
         nc.scalar.activation(ycen[:], ywin[:], COPY, scale=0.25)
         yroot = keep.tile([P, S], F32, name="yroot")
         nc.scalar.activation(yroot[:], ywin[:], COPY, scale=0.3125)
 
-        def step(tag, window, lists, gates, own_window, own_list, width):
-            a = []
-            for d in range(D):
-                t = keep.tile([P, width], F32, name=f"{tag}a{d}")
-                nc.vector.tensor_tensor(t[:], window[:].indirect(lists[d][:]), gates[:, d, :], MULT)
-                a.append(t)
-            s01 = keep.tile([P, width], F32, name=f"{tag}s01")
-            nc.vector.tensor_tensor(s01[:], a[0][:], a[1][:], ADD)
-            s2 = keep.tile([P, width], F32, name=f"{tag}s2")
-            nc.vector.tensor_tensor(s2[:], own_window[:].indirect(own_list[:]), a[2][:], ADD)
+        def weighted(name, window, offsets, weights, width):
+            t = keep.tile([P, width], F32, name=name)
+            nc.vector.tensor_tensor(t[:], window[:].indirect(offsets), weights, MULT)
+            return t
+
+        def finish(tag, first_two, window, third_list, third_gate, own_window, own_list, width):
+            half = width // 2
             res = keep.tile([P, width], F32, name=f"{tag}res")
-            nc.vector.tensor_tensor(res[:], s01[:], s2[:], ADD)
+            third = [weighted(f"{tag}a2{u}", window, third_list[:, u * half // 16 : (u + 1) * half // 16], third_gate[:, u * half : (u + 1) * half], half) for u in range(2)]
+            both = first_two()
+            rest = []
+            for u in range(2):
+                t = keep.tile([P, half], F32, name=f"{tag}rest{u}")
+                nc.vector.tensor_tensor(t[:], own_window[:].indirect(own_list[:, u * half // 16 : (u + 1) * half // 16]), third[u][:], ADD)
+                rest.append(t)
+            for u in range(2):
+                nc.vector.tensor_tensor(res[:, u * half : (u + 1) * half], rest[u][:], both[:, u * half : (u + 1) * half], ADD)
             return res
 
-        z = step("z", ywin, pos_t, g1, ycen, cen_t, V)
-        o = step("o", z, nxt_t, g2, yroot, root_t, U)
+        za = [weighted(f"za{d}", ywin, pos_t[d][:], g1[:, d, :], V) for d in range(2)]
+
+        def sum_on_tensor():
+            s01 = yps.tile([P, V], F32, name="ybank")
+            turned = keep.tile([P, V], F32, name="turned")
+            for c0 in range(0, V, P):
+                bank = hps.tile([P, P], F32, name="hbank")
+                for d in range(2):
+                    nc.tensor.matmul(bank[:], za[d][:, c0 : c0 + P], ident[:], start=(d == 0), stop=(d == 1), is_transpose=True)
+                nc.scalar.copy(turned[:, c0 : c0 + P], bank[:])
+                nc.tensor.transpose(s01[:, c0 : c0 + P], turned[:, c0 : c0 + P], ident[:])
+            return s01
+
+        z = finish("z", sum_on_tensor, ywin, pos_t[2], g1[:, 2, :], ycen, cen_t, V)
+        oa = [weighted(f"oa{d}", z, nxt_t[d][:], g2[:, d, :], U) for d in range(2)]
+
+        def sum_on_vector():
+            s01 = keep.tile([P, U], F32, name="os01")
+            nc.vector.tensor_tensor(s01[:], oa[0][:], oa[1][:], ADD)
+            return s01
+
+        o = finish("o", sum_on_vector, z, nxt_t[2], g2[:, 2, :], yroot, root_t, U)
         nc.sync.dma_start(out, o[:])

@@ -3,7 +3,7 @@ from contextlib import ExitStack
 import concourse.mybir as mybir
 from concourse.masks import make_identity
 
-K, T, S, D, V, H, N, U = 1024, 2048, 1024, 3, 512, 512, 128, 256
+K, T, S, V, H, N, U = 1024, 2048, 1024, 512, 512, 128, 256
 FLOPS = 2 * K * H * S + 2 * H * N * S
 
 F32 = mybir.dt.float32
@@ -21,199 +21,224 @@ GELU = mybir.ActivationFunctionType.Gelu_apprx_tanh
 
 P = 128
 PACK = 4
-PASSES = K // (P * PACK)
-BLK = 128
+K_PASS = P * PACK
+PASSES = K // K_PASS
+QUADRANTS = 4
+LIST_ROWS = 16
+BLOCK = 128
 SLICE = 256
-H_STRETCHES = [256,256,256,128,128]
-SCALAR_HALVES = [1,1]
+BANK = 512
+H_BANKS = 5
+Y_BANKS = 3
+
+STRETCHES = [256, 256, 256, 128, 128]
+
+SCALAR_GROUPS = [84, 48]
+
+NEAR = 0.8 * 0.8
+CEN_OVER_NEAR = 0.2 / 0.8
+ROOT_OVER_NEAR = 0.2 / NEAR
 
 
 def tile_picked_zappnp_gelu_p_kernel(tc, x_words, x_scales, w1, w2_words, w2_scales, gate, gate2, offs, cen, pos1, pos2, pos3, nxt1, nxt2, nxt3, root, out):
     nc = tc.nc
     with ExitStack() as ctx:
         keep = ctx.enter_context(tc.tile_pool(name="keep", bufs=1))
-        hps = ctx.enter_context(tc.psum_pool(name="hps", bufs=5))
-        yps = ctx.enter_context(tc.psum_pool(name="yps", bufs=3))
+        h_psum = ctx.enter_context(tc.psum_pool(name="h_psum", bufs=H_BANKS))
+        y_psum = ctx.enter_context(tc.psum_pool(name="y_psum", bufs=Y_BANKS))
 
         def load_list(name, src):
-            t = keep.tile([P, src.shape[1]], U16, name=name)
-            nc.sync.dma_start(t[:], src)
-            return t
+            tile = keep.tile([P, src.shape[1]], U16, name=name)
+            nc.sync.dma_start(tile[:], src)
+            return tile
 
-        xs_win = keep.tile([P, T], U8, name="xs_win", align_bytes=64)
-        nc.vector.memset(xs_win[:].bitcast(I32), 0)
-        w2s = keep.tile([P, N], U8, name="w2s", align_bytes=64)
-        nc.vector.memset(w2s[:].bitcast(I32), 0)
-        warm_in = keep.tile([P, 8], F32, name="warm_in")
-        nc.vector.memset(warm_in[:], 0.0)
-        warm_out = keep.tile([P, 8], F32, name="warm_out")
-        nc.scalar.activation(warm_out[:], warm_in[:], GELU)
+        def entries(list_tile, first, count):
+            return list_tile[:, first // LIST_ROWS : (first + count) // LIST_ROWS]
 
-        def load_w1(g):
-            t = keep.tile([P, PACK, H], F32, name=f"w1raw{g}")
-            nc.sync.dma_start(t[:], w1[512 * g : 512 * (g + 1), :].rearrange("(p j) c -> p j c", j=PACK))
-            return t
+        def w1_rows(g):
+            return w1[K_PASS * g : K_PASS * (g + 1), :].rearrange("(p j) c -> p j c", j=PACK)
 
-        def load_x(g):
-            t = keep.tile([P, T], I32, name=f"xwin{g}", align_bytes=64)
-            nc.sync.dma_start(t[:], x_words[g].rearrange("p n t -> p (n t)").bitcast(I32))
-            return t
+        def load_x_words(g):
+            tile = keep.tile([P, T], I32, name=f"x_table{g}", align_bytes=64)
+            nc.sync.dma_start(tile[:], x_words[g].rearrange("p n t -> p (n t)").bitcast(I32))
+            return tile
 
-        ident = keep.tile([P, P], F32, name="ident")
-        make_identity(nc, ident[:])
-        offs_t = load_list("offs_t", offs)
-        for q in range(4):
-            nc.sync.dma_start(xs_win[32 * q : 32 * q + 8, :].bitcast(I32), x_scales[:, 4 * q : 4 * q + 4, :].bitcast(I32))
-        w1first = keep.tile([P, PACK, H], F32, name="w1raw0")
-        w1rows = w1[0:512, :].rearrange("(p j) c -> p j c", j=PACK)
+        x_scale_table = keep.tile([P, T], U8, name="x_scale_table", align_bytes=64)
+        nc.vector.memset(x_scale_table[:].bitcast(I32), 0)
+        w2_scale = keep.tile([P, N], U8, name="w2_scale", align_bytes=64)
+        nc.vector.memset(w2_scale[:].bitcast(I32), 0)
+
+        table_in = keep.tile([P, 8], F32, name="table_in")
+        nc.vector.memset(table_in[:], 0.0)
+        table_out = keep.tile([P, 8], F32, name="table_out")
+        nc.scalar.activation(table_out[:], table_in[:], GELU)
+
+        identity = keep.tile([P, P], F32, name="identity")
+        make_identity(nc, identity[:])
+
+        offs_tile = load_list("offs_tile", offs)
+        for q in range(QUADRANTS):
+            nc.sync.dma_start(x_scale_table[32 * q : 32 * q + 4 * PASSES, :].bitcast(I32), x_scales[:, 4 * q : 4 * q + 4, :].bitcast(I32))
+        w1_raw = [keep.tile([P, PACK, H], F32, name=f"w1_raw{g}") for g in range(PASSES)]
         for j in range(0, PACK, 2):
-            nc.sync.dma_start(w1first[:, j : j + 2, :], w1rows[:, j : j + 2, :])
-        w1raw = [w1first]
-        w2w = keep.tile([P, 2 * N], U8, name="w2w", align_bytes=64)
-        nc.sync.dma_start(w2w[:].bitcast(I32), w2_words[0].bitcast(I32))
-        pos_t = [load_list("pos0", pos1)]
-        xwin = [load_x(0)]
-        w1raw.append(load_w1(1))
-        xwin.append(load_x(1))
+            nc.sync.dma_start(w1_raw[0][:, j : j + 2, :], w1_rows(0)[:, j : j + 2, :])
+        w2_word = keep.tile([P, 2 * N], U8, name="w2_word", align_bytes=64)
+        nc.sync.dma_start(w2_word[:].bitcast(I32), w2_words[0].bitcast(I32))
+        pos_tiles = [load_list("pos1_tile", pos1)]
+        x_table = [load_x_words(0)]
+        nc.sync.dma_start(w1_raw[1][:], w1_rows(1))
+        x_table.append(load_x_words(1))
 
-        for q in range(4):
-            nc.sync.dma_start(w2s[32 * q : 32 * q + 4, :].bitcast(I32), w2_scales[0, 4 * q : 4 * q + 4, :].bitcast(I32))
-        pos_t.extend([load_list("pos1", pos2), load_list("pos2", pos3)])
-        g1 = keep.tile([P, D, V], F32, name="g1")
-        nc.sync.dma_start(g1[:], gate.rearrange("d p v -> p d v"))
-        cen_t = load_list("cen_t", cen)
-        nxt_t = [load_list(f"nxt{d}", src) for d, src in enumerate((nxt1, nxt2, nxt3))]
-        root_t = load_list("root_t", root)
-        g2 = keep.tile([P, D, U], F32, name="g2")
-        nc.sync.dma_start(g2[:], gate2.rearrange("d p v -> p d v"))
+        for q in range(QUADRANTS):
+            nc.sync.dma_start(w2_scale[32 * q : 32 * q + 4, :].bitcast(I32), w2_scales[0, 4 * q : 4 * q + 4, :].bitcast(I32))
+        pos_tiles.extend([load_list("pos2_tile", pos2), load_list("pos3_tile", pos3)])
+        gate_tile = keep.tile([P, gate.shape[0], V], F32, name="gate_tile")
+        nc.sync.dma_start(gate_tile[:], gate.rearrange("d p v -> p d v"))
+        cen_tile = load_list("cen_tile", cen)
+        nxt_tiles = [load_list(f"nxt{d + 1}_tile", src) for d, src in enumerate((nxt1, nxt2, nxt3))]
+        root_tile = load_list("root_tile", root)
+        gate2_tile = keep.tile([P, gate2.shape[0], U], F32, name="gate2_tile")
+        nc.sync.dma_start(gate2_tile[:], gate2.rearrange("d p v -> p d v"))
 
-        xs = keep.tile([P, S], U8, name="xs", align_bytes=64)
-        nc.vector.tensor_copy(xs[:], xs_win[:].indirect(offs_t[:]))
+        x_scale = keep.tile([P, S], U8, name="x_scale", align_bytes=64)
+        nc.vector.tensor_copy(x_scale[:], x_scale_table[:].indirect(offs_tile[:]))
 
-        x0 = keep.tile([P, S], U32, name="x0", align_bytes=64)
-        warm_bank = yps.tile([P, 512], F32, name="ybank")
+        def gather_words(g, dst, first):
+            nc.vector.tensor_copy(dst, x_table[g][:].bitcast(U32).indirect(entries(offs_tile, first, SLICE)))
 
-        def warm_pass(g, t, c0, width):
-            nc.tensor.matmul_mx(out=warm_bank[:, 0:width], lhsT=w1c[(g, t)].bitcast(FP8X4), lhsT_scale=w1s[(g, t)], rhs=x0[:, c0 : c0 + width].bitcast(FP8X4), rhs_scale=xs[:, c0 : c0 + width], start=True, stop=True)
+        x0_word = keep.tile([P, S], U32, name="x0_word", align_bytes=64)
+        w1_word = {}
+        w1_scale = {}
 
-        w1c = {}
-        w1s = {}
-        for g in range(PASSES):
-            src = w1raw[g][:].rearrange("p j (m t) -> p m t j", t=PACK)
-            halves = []
-            for hf in range(2):
-                grp = keep.tile([P, 2, P, PACK], BF16, name=f"w1b{g}{hf}", align_bytes=64)
-                dst = grp[:].rearrange("p t m j -> p m t j")
-                if hf < SCALAR_HALVES[g]:
-                    nc.scalar.copy(dst, src[:, :, 2 * hf : 2 * hf + 2, :])
-                else:
-                    nc.vector.tensor_copy(dst, src[:, :, 2 * hf : 2 * hf + 2, :])
-                halves.append(grp)
-            for hf in (1, 0):
-                c = keep.tile([P, 2 * P], U32, name=f"w1c{g}{hf}", align_bytes=64)
-                s = keep.tile([P, 2 * P], U8, name=f"w1s{g}{hf}", align_bytes=64)
-                nc.vector.quantize_mx(out=c[:].bitcast(FP8X4), scales=s[:], in_=halves[hf][:].rearrange("p t m j -> p (t m j)"))
-                for tt in range(2):
-                    w1c[(g, 2 * hf + tt)] = c[:, tt * P : (tt + 1) * P]
-                    w1s[(g, 2 * hf + tt)] = s[:, tt * P : (tt + 1) * P]
-                if g == 1:
-                    warm_pass(1, 2 * hf, 0, 512)
-            if g == 0:
-                for sl in range(S // SLICE):
-                    nc.vector.tensor_copy(x0[:, sl * SLICE : (sl + 1) * SLICE], xwin[0][:].bitcast(U32).indirect(offs_t[:, sl * SLICE // 16 : (sl + 1) * SLICE // 16]))
-                    if sl > 0:
-                        warm_pass(0, 0, sl * SLICE, SLICE)
-                warm_pass(0, 1, 3 * SLICE, SLICE)
+        warm_bank = y_psum.tile([P, BANK], F32, name="y_bank")
 
-        ywin = keep.tile([P, S], F32, name="ywin")
-        x1 = []
-        for sl in range(S // SLICE):
-            t = keep.tile([P, SLICE], U32, name=f"x1_{sl}", align_bytes=64)
-            nc.vector.tensor_copy(t[:], xwin[1][:].bitcast(U32).indirect(offs_t[:, sl * SLICE // 16 : (sl + 1) * SLICE // 16]))
-            x1.append(t)
+        def warm_pass(g, t, first, width):
+            nc.tensor.matmul_mx(
+                out=warm_bank[:, 0:width],
+                lhsT=w1_word[(g, t)].bitcast(FP8X4),
+                lhsT_scale=w1_scale[(g, t)],
+                rhs=x0_word[:, first : first + width].bitcast(FP8X4),
+                rhs_scale=x_scale[:, first : first + width],
+                start=True,
+                stop=True,
+            )
 
-        hbs = []
-        starts = [sum(H_STRETCHES[:i]) for i in range(len(H_STRETCHES))]
+        def quantise_w1(g):
+            rounded = keep.tile([P, PACK, P, PACK], BF16, name=f"w1_rounded{g}", align_bytes=64)
+            src = w1_raw[g][:].rearrange("p j (m t) -> p m t j", t=PACK)
+            dst = rounded[:].rearrange("p t m j -> p m t j")
+            split = SCALAR_GROUPS[g]
+            nc.scalar.copy(dst[:, 0:split, :, :], src[:, 0:split, :, :])
+            nc.vector.tensor_copy(dst[:, split:P, :, :], src[:, split:P, :, :])
+            for t0 in range(0, PACK, 2):
+                words = keep.tile([P, 2 * P], U32, name=f"w1_word{g}{t0}", align_bytes=64)
+                scales = keep.tile([P, 2 * P], U8, name=f"w1_scale{g}{t0}", align_bytes=64)
+                nc.vector.quantize_mx(out=words[:].bitcast(FP8X4), scales=scales[:], in_=rounded[:, t0 : t0 + 2, :, :].rearrange("p t m j -> p (t m j)"))
+                for u in range(2):
+                    w1_word[(g, t0 + u)] = words[:, u * P : (u + 1) * P]
+                    w1_scale[(g, t0 + u)] = scales[:, u * P : (u + 1) * P]
+                if g == PASSES - 1:
+                    warm_pass(g, t0, 0, BANK)
 
-        def first_layer(i):
-            width = H_STRETCHES[i]
-            hb = keep.tile([P, width, PACK], BF16, name=f"hb{i}", align_bytes=64)
-            hbs.append(hb)
-            for b0 in range(0, width, BLK):
-                n0 = starts[i] + b0
-                bank = hps.tile([P, PACK, BLK], F32, name="hbank")
+        quantise_w1(0)
+        for first in range(0, S, SLICE):
+            gather_words(0, x0_word[:, first : first + SLICE], first)
+            if first > 0:
+                warm_pass(0, 0, first, SLICE)
+        warm_pass(0, 1, S - SLICE, SLICE)
+        quantise_w1(1)
+
+        y_near = keep.tile([P, S], F32, name="y_near")
+        x1_word = []
+        for first in range(0, S, SLICE):
+            tile = keep.tile([P, SLICE], U32, name=f"x1_word{first}", align_bytes=64)
+            gather_words(1, tile[:], first)
+            x1_word.append(tile)
+
+        def first_layer(first, width):
+            h_rounded = keep.tile([P, width, PACK], BF16, name=f"h_rounded{first}", align_bytes=64)
+            for b0 in range(0, width, BLOCK):
+                n0 = first + b0
+                moving = (x0_word[:, n0 : n0 + BLOCK], x1_word[n0 // SLICE][:, n0 % SLICE : n0 % SLICE + BLOCK])
+                bank = h_psum.tile([P, PACK, BLOCK], F32, name="h_bank")
                 for t in range(PACK):
                     for g in range(PASSES):
-                        words = x0[:, n0 : n0 + BLK] if g == 0 else x1[n0 // SLICE][:, n0 % SLICE : n0 % SLICE + BLK]
                         nc.tensor.matmul_mx(
                             out=bank[:, t, :],
-                            lhsT=w1c[(g, t)].bitcast(FP8X4),
-                            lhsT_scale=w1s[(g, t)],
-                            rhs=words.bitcast(FP8X4),
-                            rhs_scale=xs[4 * g : P, n0 : n0 + BLK],
+                            lhsT=w1_word[(g, t)].bitcast(FP8X4),
+                            lhsT_scale=w1_scale[(g, t)],
+                            rhs=moving[g].bitcast(FP8X4),
+                            rhs_scale=x_scale[4 * g : P, n0 : n0 + BLOCK],
                             start=(g == 0),
                             stop=(g == PASSES - 1),
                         )
-                nc.scalar.activation(hb[:, b0 : b0 + BLK, :], bank[:].rearrange("p t n -> p n t"), GELU)
+                nc.scalar.activation(h_rounded[:, b0 : b0 + BLOCK, :], bank[:].rearrange("p t n -> p n t"), GELU)
+            return h_rounded
 
-        def second_layer(i):
-            width = H_STRETCHES[i]
-            hc = keep.tile([P, width], U32, name=f"hc{i}", align_bytes=64)
-            hs = keep.tile([P, width], U8, name=f"hs{i}", align_bytes=64)
-            nc.vector.quantize_mx(out=hc[:].bitcast(FP8X4), scales=hs[:], in_=hbs[i][:].rearrange("p n t -> p (n t)"))
-            ybank = yps.tile([P, width], F32, name="ybank")
-            nc.tensor.matmul_mx(out=ybank[:], lhsT=w2w[:].bitcast(FP4X4), lhsT_scale=w2s[:], rhs=hc[:].bitcast(FP8X4), rhs_scale=hs[:], start=True, stop=True)
-            nc.vector.tensor_scalar(ywin[:, starts[i] : starts[i] + width], ybank[:], 0.64, None, MULT)
+        def second_layer(first, width, h_rounded):
+            h_word = keep.tile([P, width], U32, name=f"h_word{first}", align_bytes=64)
+            h_scale = keep.tile([P, width], U8, name=f"h_scale{first}", align_bytes=64)
+            nc.vector.quantize_mx(out=h_word[:].bitcast(FP8X4), scales=h_scale[:], in_=h_rounded[:].rearrange("p n t -> p (n t)"))
+            bank = y_psum.tile([P, width], F32, name="y_bank")
+            nc.tensor.matmul_mx(
+                out=bank[:],
+                lhsT=w2_word[:].bitcast(FP4X4),
+                lhsT_scale=w2_scale[:],
+                rhs=h_word[:].bitcast(FP8X4),
+                rhs_scale=h_scale[:],
+                start=True,
+                stop=True,
+            )
+            nc.vector.tensor_scalar(y_near[:, first : first + width], bank[:], NEAR, None, MULT)
 
-        for i in range(len(H_STRETCHES)):
-            first_layer(i)
-        for i in range(len(H_STRETCHES)):
-            second_layer(i)
+        firsts = [sum(STRETCHES[:i]) for i in range(len(STRETCHES))]
+        hidden = [first_layer(first, width) for first, width in zip(firsts, STRETCHES)]
+        for first, width, h_rounded in zip(firsts, STRETCHES, hidden):
+            second_layer(first, width, h_rounded)
 
-        ycen = keep.tile([P, S], F32, name="ycen")
-        nc.scalar.activation(ycen[:], ywin[:], COPY, scale=0.25)
-        yroot = keep.tile([P, S], F32, name="yroot")
-        nc.scalar.activation(yroot[:], ywin[:], COPY, scale=0.3125)
+        y_cen = keep.tile([P, S], F32, name="y_cen")
+        nc.scalar.activation(y_cen[:], y_near[:], COPY, scale=CEN_OVER_NEAR)
+        y_root = keep.tile([P, S], F32, name="y_root")
+        nc.scalar.activation(y_root[:], y_near[:], COPY, scale=ROOT_OVER_NEAR)
 
-        def weighted(name, window, offsets, weights, width):
-            t = keep.tile([P, width], F32, name=name)
-            nc.vector.tensor_tensor(t[:], window[:].indirect(offsets), weights, MULT)
-            return t
+        def weighted(name, table, offsets, weights, width):
+            tile = keep.tile([P, width], F32, name=name)
+            nc.vector.tensor_tensor(tile[:], table[:].indirect(offsets), weights, MULT)
+            return tile
 
-        def finish(tag, first_two, window, third_list, third_gate, own_window, own_list, width):
-            half = width // 2
-            res = keep.tile([P, width], F32, name=f"{tag}res")
-            third = [weighted(f"{tag}a2{u}", window, third_list[:, u * half // 16 : (u + 1) * half // 16], third_gate[:, u * half : (u + 1) * half], half) for u in range(2)]
-            both = first_two()
-            rest = []
-            for u in range(2):
-                t = keep.tile([P, half], F32, name=f"{tag}rest{u}")
-                nc.vector.tensor_tensor(t[:], own_window[:].indirect(own_list[:, u * half // 16 : (u + 1) * half // 16]), third[u][:], ADD)
-                rest.append(t)
-            for u in range(2):
-                nc.vector.tensor_tensor(res[:, u * half : (u + 1) * half], rest[u][:], both[:, u * half : (u + 1) * half], ADD)
-            return res
-
-        za = [weighted(f"za{d}", ywin, pos_t[d][:], g1[:, d, :], V) for d in range(2)]
-
-        def sum_on_tensor():
-            s01 = yps.tile([P, V], F32, name="ybank")
-            turned = keep.tile([P, V], F32, name="turned")
-            for c0 in range(0, V, P):
-                bank = hps.tile([P, P], F32, name="hbank")
-                for d in range(2):
-                    nc.tensor.matmul(bank[:], za[d][:, c0 : c0 + P], ident[:], start=(d == 0), stop=(d == 1), is_transpose=True)
+        def sum_on_tensor(name, terms, width):
+            total = y_psum.tile([P, width], F32, name="y_bank")
+            turned = keep.tile([P, width], F32, name=name)
+            for c0 in range(0, width, P):
+                bank = h_psum.tile([P, P], F32, name="h_bank")
+                for d, term in enumerate(terms):
+                    nc.tensor.matmul(bank[:], term[:, c0 : c0 + P], identity[:], start=(d == 0), stop=(d == len(terms) - 1), is_transpose=True)
                 nc.scalar.copy(turned[:, c0 : c0 + P], bank[:])
-                nc.tensor.transpose(s01[:, c0 : c0 + P], turned[:, c0 : c0 + P], ident[:])
-            return s01
+                nc.tensor.transpose(total[:, c0 : c0 + P], turned[:, c0 : c0 + P], identity[:])
+            return total
 
-        z = finish("z", sum_on_tensor, ywin, pos_t[2], g1[:, 2, :], ycen, cen_t, V)
-        oa = [weighted(f"oa{d}", z, nxt_t[d][:], g2[:, d, :], U) for d in range(2)]
+        def sum_on_vector(name, terms, width):
+            total = keep.tile([P, width], F32, name=name)
+            nc.vector.tensor_tensor(total[:], terms[0][:], terms[1][:], ADD)
+            return total
 
-        def sum_on_vector():
-            s01 = keep.tile([P, U], F32, name="os01")
-            nc.vector.tensor_tensor(s01[:], oa[0][:], oa[1][:], ADD)
-            return s01
+        def propagate(name, table, lists, gates, own_table, own_list, width, add_two):
+            half = width // 2
+            halves = (0, half)
+            first_two = [weighted(f"{name}_term{d}", table, lists[d][:], gates[:, d, :], width) for d in range(2)]
+            result = keep.tile([P, width], F32, name=name)
+            third = [weighted(f"{name}_third{c0}", table, entries(lists[2], c0, half), gates[:, 2, c0 : c0 + half], half) for c0 in halves]
+            pair = add_two(f"{name}_pair", first_two, width)
+            rest = []
+            for c0, term in zip(halves, third):
+                tile = keep.tile([P, half], F32, name=f"{name}_rest{c0}")
+                nc.vector.tensor_tensor(tile[:], own_table[:].indirect(entries(own_list, c0, half)), term[:], ADD)
+                rest.append(tile)
+            for c0, term in zip(halves, rest):
+                nc.vector.tensor_tensor(result[:, c0 : c0 + half], term[:], pair[:, c0 : c0 + half], ADD)
+            return result
 
-        o = finish("o", sum_on_vector, z, nxt_t[2], g2[:, 2, :], yroot, root_t, U)
-        nc.sync.dma_start(out, o[:])
+        z_near = propagate("z_near", y_near, pos_tiles, gate_tile, y_cen, cen_tile, V, sum_on_tensor)
+        result = propagate("result", z_near, nxt_tiles, gate2_tile, y_root, root_tile, U, sum_on_vector)
+        for c0 in (0, U // 2):
+            nc.sync.dma_start(out[:, c0 : c0 + U // 2], result[:, c0 : c0 + U // 2])

@@ -27,9 +27,8 @@ QUADRANTS = 4
 LIST_ROWS = 16
 BLOCK = 128
 SLICE = 256
-BANK = 512
-H_BANKS = 5
-Y_BANKS = 3
+EARLY_BLOCKS = 5
+BANKS = 8
 
 STRETCHES = [256, 256, 256, 128, 128]
 
@@ -44,8 +43,10 @@ def tile_picked_zappnp_gelu_p_kernel(tc, x_words, x_scales, w1, w2_words, w2_sca
     nc = tc.nc
     with ExitStack() as ctx:
         keep = ctx.enter_context(tc.tile_pool(name="keep", bufs=1))
-        h_psum = ctx.enter_context(tc.psum_pool(name="h_psum", bufs=H_BANKS))
-        y_psum = ctx.enter_context(tc.psum_pool(name="y_psum", bufs=Y_BANKS))
+        psum = ctx.enter_context(tc.psum_pool(name="psum", bufs=1))
+
+        def bank_tile(index, shape):
+            return psum.tile(shape, F32, name=f"bank{index % BANKS}")
 
         def load_list(name, src):
             tile = keep.tile([P, src.shape[1]], U16, name=name)
@@ -109,19 +110,7 @@ def tile_picked_zappnp_gelu_p_kernel(tc, x_words, x_scales, w1, w2_words, w2_sca
         x0_word = keep.tile([P, S], U32, name="x0_word", align_bytes=64)
         w1_word = {}
         w1_scale = {}
-
-        warm_bank = y_psum.tile([P, BANK], F32, name="y_bank")
-
-        def warm_pass(g, t, first, width):
-            nc.tensor.matmul_mx(
-                out=warm_bank[:, 0:width],
-                lhsT=w1_word[(g, t)].bitcast(FP8X4),
-                lhsT_scale=w1_scale[(g, t)],
-                rhs=x0_word[:, first : first + width].bitcast(FP8X4),
-                rhs_scale=x_scale[:, first : first + width],
-                start=True,
-                stop=True,
-            )
+        w1_scales = keep.tile([P, H], U8, name="w1_scales", align_bytes=64)
 
         def quantise_w1(g):
             rounded = keep.tile([P, PACK, P, PACK], BF16, name=f"w1_rounded{g}", align_bytes=64)
@@ -132,21 +121,35 @@ def tile_picked_zappnp_gelu_p_kernel(tc, x_words, x_scales, w1, w2_words, w2_sca
             nc.vector.tensor_copy(dst[:, split:P, :, :], src[:, split:P, :, :])
             for t0 in range(0, PACK, 2):
                 words = keep.tile([P, 2 * P], U32, name=f"w1_word{g}{t0}", align_bytes=64)
-                scales = keep.tile([P, 2 * P], U8, name=f"w1_scale{g}{t0}", align_bytes=64)
-                nc.vector.quantize_mx(out=words[:].bitcast(FP8X4), scales=scales[:], in_=rounded[:, t0 : t0 + 2, :, :].rearrange("p t m j -> p (t m j)"))
+                scales = w1_scales[4 * g : P, t0 * P : (t0 + 2) * P]
+                nc.vector.quantize_mx(out=words[:].bitcast(FP8X4), scales=scales, in_=rounded[:, t0 : t0 + 2, :, :].rearrange("p t m j -> p (t m j)"))
                 for u in range(2):
                     w1_word[(g, t0 + u)] = words[:, u * P : (u + 1) * P]
                     w1_scale[(g, t0 + u)] = scales[:, u * P : (u + 1) * P]
-                if g == PASSES - 1:
-                    warm_pass(g, t0, 0, BANK)
 
         quantise_w1(0)
         for first in range(0, S, SLICE):
             gather_words(0, x0_word[:, first : first + SLICE], first)
-            if first > 0:
-                warm_pass(0, 0, first, SLICE)
-        warm_pass(0, 1, S - SLICE, SLICE)
+
+        def first_layer_pass(g, bank, words, n0, tiles=range(PACK)):
+            for t in tiles:
+                nc.tensor.matmul_mx(
+                    out=bank[:, t, :],
+                    lhsT=w1_word[(g, t)].bitcast(FP8X4),
+                    lhsT_scale=w1_scale[(g, t)],
+                    rhs=words.bitcast(FP8X4),
+                    rhs_scale=x_scale[4 * g : P, n0 : n0 + BLOCK],
+                    start=(g == 0 and t == 0),
+                    stop=(g == PASSES - 1 and t == PACK - 1),
+                )
+
+        h_banks = [bank_tile(b, [P, PACK, BLOCK]) for b in range(S // BLOCK)]
+        for b in range(EARLY_BLOCKS):
+            first_layer_pass(0, h_banks[b], x0_word[:, b * BLOCK : (b + 1) * BLOCK], b * BLOCK)
         quantise_w1(1)
+        for t0 in range(0, PACK, 2):
+            for b in range(EARLY_BLOCKS, len(h_banks)):
+                first_layer_pass(0, h_banks[b], x0_word[:, b * BLOCK : (b + 1) * BLOCK], b * BLOCK, (t0, t0 + 1))
 
         y_near = keep.tile([P, S], F32, name="y_near")
         x1_word = []
@@ -159,19 +162,8 @@ def tile_picked_zappnp_gelu_p_kernel(tc, x_words, x_scales, w1, w2_words, w2_sca
             h_rounded = keep.tile([P, width, PACK], BF16, name=f"h_rounded{first}", align_bytes=64)
             for b0 in range(0, width, BLOCK):
                 n0 = first + b0
-                moving = (x0_word[:, n0 : n0 + BLOCK], x1_word[n0 // SLICE][:, n0 % SLICE : n0 % SLICE + BLOCK])
-                bank = h_psum.tile([P, PACK, BLOCK], F32, name="h_bank")
-                for t in range(PACK):
-                    for g in range(PASSES):
-                        nc.tensor.matmul_mx(
-                            out=bank[:, t, :],
-                            lhsT=w1_word[(g, t)].bitcast(FP8X4),
-                            lhsT_scale=w1_scale[(g, t)],
-                            rhs=moving[g].bitcast(FP8X4),
-                            rhs_scale=x_scale[4 * g : P, n0 : n0 + BLOCK],
-                            start=(g == 0),
-                            stop=(g == PASSES - 1),
-                        )
+                bank = h_banks[n0 // BLOCK]
+                first_layer_pass(1, bank, x1_word[n0 // SLICE][:, n0 % SLICE : n0 % SLICE + BLOCK], n0)
                 nc.scalar.activation(h_rounded[:, b0 : b0 + BLOCK, :], bank[:].rearrange("p t n -> p n t"), GELU)
             return h_rounded
 
@@ -179,7 +171,7 @@ def tile_picked_zappnp_gelu_p_kernel(tc, x_words, x_scales, w1, w2_words, w2_sca
             h_word = keep.tile([P, width], U32, name=f"h_word{first}", align_bytes=64)
             h_scale = keep.tile([P, width], U8, name=f"h_scale{first}", align_bytes=64)
             nc.vector.quantize_mx(out=h_word[:].bitcast(FP8X4), scales=h_scale[:], in_=h_rounded[:].rearrange("p n t -> p (n t)"))
-            bank = y_psum.tile([P, width], F32, name="y_bank")
+            bank = bank_tile(first // BLOCK, [P, width])
             nc.tensor.matmul_mx(
                 out=bank[:],
                 lhsT=w2_word[:].bitcast(FP4X4),
@@ -189,7 +181,10 @@ def tile_picked_zappnp_gelu_p_kernel(tc, x_words, x_scales, w1, w2_words, w2_sca
                 start=True,
                 stop=True,
             )
-            nc.vector.tensor_scalar(y_near[:, first : first + width], bank[:], NEAR, None, MULT)
+            if width == BLOCK:
+                nc.scalar.activation(y_near[:, first : first + width], bank[:], COPY, scale=NEAR)
+            else:
+                nc.vector.tensor_scalar(y_near[:, first : first + width], bank[:], NEAR, None, MULT)
 
         firsts = [sum(STRETCHES[:i]) for i in range(len(STRETCHES))]
         hidden = [first_layer(first, width) for first, width in zip(firsts, STRETCHES)]
@@ -207,10 +202,10 @@ def tile_picked_zappnp_gelu_p_kernel(tc, x_words, x_scales, w1, w2_words, w2_sca
             return tile
 
         def sum_on_tensor(name, terms, width):
-            total = y_psum.tile([P, width], F32, name="y_bank")
+            total = bank_tile(1, [P, width])
             turned = keep.tile([P, width], F32, name=name)
             for c0 in range(0, width, P):
-                bank = h_psum.tile([P, P], F32, name="h_bank")
+                bank = bank_tile(2 + c0 // P, [P, P])
                 for d, term in enumerate(terms):
                     nc.tensor.matmul(bank[:], term[:, c0 : c0 + P], identity[:], start=(d == 0), stop=(d == len(terms) - 1), is_transpose=True)
                 nc.scalar.copy(turned[:, c0 : c0 + P], bank[:])

@@ -32,7 +32,7 @@ BANKS = 8
 
 STRETCHES = [256, 256, 256, 128, 128]
 
-SCALAR_GROUPS = [84, 48]
+SCALAR_GROUPS = [92, 68]
 
 NEAR = 0.8 * 0.8
 CEN_OVER_NEAR = 0.2 / 0.8
@@ -83,18 +83,21 @@ def tile_picked_zappnp_gelu_p_kernel(tc, x_words, x_scales, w1, w2_words, w2_sca
         w1_raw = [keep.tile([P, PACK, H], F32, name=f"w1_raw{g}") for g in range(PASSES)]
         for j in range(0, PACK, 2):
             nc.sync.dma_start(w1_raw[0][:, j : j + 2, :], w1_rows(0)[:, j : j + 2, :])
-        w2_word = keep.tile([P, 2 * N], U8, name="w2_word", align_bytes=64)
-        nc.sync.dma_start(w2_word[:].bitcast(I32), w2_words[0].bitcast(I32))
-        pos_tiles = [load_list("pos1_tile", pos1)]
         x_table = [load_x_words(0)]
         nc.sync.dma_start(w1_raw[1][:], w1_rows(1))
         x_table.append(load_x_words(1))
+        w2_word = keep.tile([P, 2 * N], U8, name="w2_word", align_bytes=64)
+        nc.sync.dma_start(w2_word[:].bitcast(I32), w2_words[0].bitcast(I32))
 
         for q in range(QUADRANTS):
             nc.sync.dma_start(w2_scale[32 * q : 32 * q + 4, :].bitcast(I32), w2_scales[0, 4 * q : 4 * q + 4, :].bitcast(I32))
-        pos_tiles.extend([load_list("pos2_tile", pos2), load_list("pos3_tile", pos3)])
-        gate_tile = keep.tile([P, gate.shape[0], V], F32, name="gate_tile")
-        nc.sync.dma_start(gate_tile[:], gate.rearrange("d p v -> p d v"))
+        pos_tiles = [load_list(f"pos{d + 1}_tile", src) for d, src in enumerate((pos1, pos2, pos3))]
+        gate_last = keep.tile([P, V], F32, name="gate_last")
+        nc.sync.dma_start(gate_last[:], gate[2])
+        gate_cols = keep.tile([P, 2, 8], F32, name="gate_cols")
+        with nc.allow_non_contiguous_dma(reason="one gate value to a partition"):
+            for d in range(2):
+                nc.sync.dma_start(gate_cols[:, d, 0 : V // P], gate[d, 0, :].rearrange("(c p) -> p c", p=P))
         cen_tile = load_list("cen_tile", cen)
         nxt_tiles = [load_list(f"nxt{d + 1}_tile", src) for d, src in enumerate((nxt1, nxt2, nxt3))]
         root_tile = load_list("root_tile", root)
@@ -193,37 +196,54 @@ def tile_picked_zappnp_gelu_p_kernel(tc, x_words, x_scales, w1, w2_words, w2_sca
 
         y_cen = keep.tile([P, S], F32, name="y_cen")
         nc.scalar.activation(y_cen[:], y_near[:], COPY, scale=CEN_OVER_NEAR)
-        y_root = keep.tile([P, S], F32, name="y_root")
-        nc.scalar.activation(y_root[:], y_near[:], COPY, scale=ROOT_OVER_NEAR)
 
         def weighted(name, table, offsets, weights, width):
             tile = keep.tile([P, width], F32, name=name)
             nc.vector.tensor_tensor(tile[:], table[:].indirect(offsets), weights, MULT)
             return tile
 
-        def sum_on_tensor(name, terms, width):
-            total = bank_tile(1, [P, width])
-            turned = keep.tile([P, width], F32, name=name)
-            for c0 in range(0, width, P):
-                bank = bank_tile(2 + c0 // P, [P, P])
-                for d, term in enumerate(terms):
-                    nc.tensor.matmul(bank[:], term[:, c0 : c0 + P], identity[:], start=(d == 0), stop=(d == len(terms) - 1), is_transpose=True)
-                nc.scalar.copy(turned[:, c0 : c0 + P], bank[:])
-                nc.tensor.transpose(total[:, c0 : c0 + P], turned[:, c0 : c0 + P], identity[:])
-            return total
+        def first_two_on_tensor(name, table, lists):
+            picked = []
+            for d in range(2):
+                tile = keep.tile([P, V], F32, name=f"{name}_picked{d}")
+                nc.vector.tensor_copy(tile[:], table[:].indirect(lists[d][:]))
+                picked.append(tile)
 
-        def sum_on_vector(name, terms, width):
-            total = keep.tile([P, width], F32, name=name)
-            nc.vector.tensor_tensor(total[:], terms[0][:], terms[1][:], ADD)
-            return total
+            def finish():
+                total = bank_tile(4, [P, V])
+                for d in range(2):
+                    turned = keep.tile([P, V], F32, name=f"{name}_turned{d}")
+                    for h in range(2):
+                        bank = bank_tile(2 * d + h, [P, 2, P])
+                        for u in range(2):
+                            c = 2 * h + u
+                            nc.tensor.transpose(bank[:, u, :], picked[d][:, c * P : (c + 1) * P], identity[:])
+                        for u in range(2):
+                            c = 2 * h + u
+                            nc.scalar.activation(turned[:, c * P : (c + 1) * P], bank[:, u, :], COPY, scale=gate_cols[:, d, c : c + 1])
+                    for c in range(V // P):
+                        nc.tensor.matmul(total[:, c * P : (c + 1) * P], turned[:, c * P : (c + 1) * P], identity[:], start=(d == 0 and c == 0), stop=(d == 1 and c == V // P - 1), is_transpose=True)
+                return total
 
-        def propagate(name, table, lists, gates, own_table, own_list, width, add_two):
+            return finish
+
+        def first_two_on_vector(name, table, lists):
+            terms = [weighted(f"{name}_term{d}", table, lists[d][:], gate2_tile[:, d, :], U) for d in range(2)]
+
+            def finish():
+                total = keep.tile([P, U], F32, name=name)
+                nc.vector.tensor_tensor(total[:], terms[0][:], terms[1][:], ADD)
+                return total
+
+            return finish
+
+        def propagate(name, table, lists, last_gate, own_table, own_list, width, first_two):
             half = width // 2
             halves = (0, half)
-            first_two = [weighted(f"{name}_term{d}", table, lists[d][:], gates[:, d, :], width) for d in range(2)]
+            finish = first_two(f"{name}_pair", table, lists)
             result = keep.tile([P, width], F32, name=name)
-            third = [weighted(f"{name}_third{c0}", table, entries(lists[2], c0, half), gates[:, 2, c0 : c0 + half], half) for c0 in halves]
-            pair = add_two(f"{name}_pair", first_two, width)
+            third = [weighted(f"{name}_third{c0}", table, entries(lists[2], c0, half), last_gate[:, c0 : c0 + half], half) for c0 in halves]
+            pair = finish()
             rest = []
             for c0, term in zip(halves, third):
                 tile = keep.tile([P, half], F32, name=f"{name}_rest{c0}")
@@ -233,7 +253,9 @@ def tile_picked_zappnp_gelu_p_kernel(tc, x_words, x_scales, w1, w2_words, w2_sca
                 nc.vector.tensor_tensor(result[:, c0 : c0 + half], term[:], pair[:, c0 : c0 + half], ADD)
             return result
 
-        z_near = propagate("z_near", y_near, pos_tiles, gate_tile, y_cen, cen_tile, V, sum_on_tensor)
-        result = propagate("result", z_near, nxt_tiles, gate2_tile, y_root, root_tile, U, sum_on_vector)
+        z_near = propagate("z_near", y_near, pos_tiles, gate_last[:], y_cen, cen_tile, V, first_two_on_tensor)
+        y_root = keep.tile([P, S], F32, name="y_root")
+        nc.scalar.activation(y_root[:], y_near[:], COPY, scale=ROOT_OVER_NEAR)
+        result = propagate("result", z_near, nxt_tiles, gate2_tile[:, 2, :], y_root, root_tile, U, first_two_on_vector)
         for c0 in (0, U // 2):
             nc.sync.dma_start(out[:, c0 : c0 + U // 2], result[:, c0 : c0 + U // 2])

@@ -27,12 +27,12 @@ QUADRANTS = 4
 LIST_ROWS = 16
 BLOCK = 128
 SLICE = 256
-EARLY_BLOCKS = 5
+H_BANKS = 6
 BANKS = 8
 
 STRETCHES = [256, 256, 256, 128, 128]
 
-SCALAR_GROUPS = [92, 68]
+SCALAR_GROUPS = [88, 72]
 
 NEAR = 0.8 * 0.8
 CEN_OVER_NEAR = 0.2 / 0.8
@@ -113,7 +113,6 @@ def tile_picked_zappnp_gelu_p_kernel(tc, x_words, x_scales, w1, w2_words, w2_sca
         x0_word = keep.tile([P, S], U32, name="x0_word", align_bytes=64)
         w1_word = {}
         w1_scale = {}
-        w1_scales = keep.tile([P, H], U8, name="w1_scales", align_bytes=64)
 
         def quantise_w1(g):
             rounded = keep.tile([P, PACK, P, PACK], BF16, name=f"w1_rounded{g}", align_bytes=64)
@@ -124,8 +123,8 @@ def tile_picked_zappnp_gelu_p_kernel(tc, x_words, x_scales, w1, w2_words, w2_sca
             nc.vector.tensor_copy(dst[:, split:P, :, :], src[:, split:P, :, :])
             for t0 in range(0, PACK, 2):
                 words = keep.tile([P, 2 * P], U32, name=f"w1_word{g}{t0}", align_bytes=64)
-                scales = w1_scales[4 * g : P, t0 * P : (t0 + 2) * P]
-                nc.vector.quantize_mx(out=words[:].bitcast(FP8X4), scales=scales, in_=rounded[:, t0 : t0 + 2, :, :].rearrange("p t m j -> p (t m j)"))
+                scales = keep.tile([P, 2 * P], U8, name=f"w1_scale{g}{t0}", align_bytes=64)
+                nc.vector.quantize_mx(out=words[:].bitcast(FP8X4), scales=scales[:], in_=rounded[:, t0 : t0 + 2, :, :].rearrange("p t m j -> p (t m j)"))
                 for u in range(2):
                     w1_word[(g, t0 + u)] = words[:, u * P : (u + 1) * P]
                     w1_scale[(g, t0 + u)] = scales[:, u * P : (u + 1) * P]
@@ -134,8 +133,8 @@ def tile_picked_zappnp_gelu_p_kernel(tc, x_words, x_scales, w1, w2_words, w2_sca
         for first in range(0, S, SLICE):
             gather_words(0, x0_word[:, first : first + SLICE], first)
 
-        def first_layer_pass(g, bank, words, n0, tiles=range(PACK)):
-            for t in tiles:
+        def first_layer_pass(g, bank, words, n0):
+            for t in range(PACK):
                 nc.tensor.matmul_mx(
                     out=bank[:, t, :],
                     lhsT=w1_word[(g, t)].bitcast(FP8X4),
@@ -146,13 +145,16 @@ def tile_picked_zappnp_gelu_p_kernel(tc, x_words, x_scales, w1, w2_words, w2_sca
                     stop=(g == PASSES - 1 and t == PACK - 1),
                 )
 
-        h_banks = [bank_tile(b, [P, PACK, BLOCK]) for b in range(S // BLOCK)]
-        for b in range(EARLY_BLOCKS):
+        h_banks = []
+
+        def open_block():
+            b = len(h_banks)
+            h_banks.append(bank_tile(b % H_BANKS, [P, PACK, BLOCK]))
             first_layer_pass(0, h_banks[b], x0_word[:, b * BLOCK : (b + 1) * BLOCK], b * BLOCK)
+
+        for b in range(H_BANKS):
+            open_block()
         quantise_w1(1)
-        for t0 in range(0, PACK, 2):
-            for b in range(EARLY_BLOCKS, len(h_banks)):
-                first_layer_pass(0, h_banks[b], x0_word[:, b * BLOCK : (b + 1) * BLOCK], b * BLOCK, (t0, t0 + 1))
 
         y_near = keep.tile([P, S], F32, name="y_near")
         x1_word = []
@@ -168,13 +170,15 @@ def tile_picked_zappnp_gelu_p_kernel(tc, x_words, x_scales, w1, w2_words, w2_sca
                 bank = h_banks[n0 // BLOCK]
                 first_layer_pass(1, bank, x1_word[n0 // SLICE][:, n0 % SLICE : n0 % SLICE + BLOCK], n0)
                 nc.scalar.activation(h_rounded[:, b0 : b0 + BLOCK, :], bank[:].rearrange("p t n -> p n t"), GELU)
+                if len(h_banks) < S // BLOCK:
+                    open_block()
             return h_rounded
 
-        def second_layer(first, width, h_rounded):
+        def second_layer(index, first, width, h_rounded):
             h_word = keep.tile([P, width], U32, name=f"h_word{first}", align_bytes=64)
             h_scale = keep.tile([P, width], U8, name=f"h_scale{first}", align_bytes=64)
             nc.vector.quantize_mx(out=h_word[:].bitcast(FP8X4), scales=h_scale[:], in_=h_rounded[:].rearrange("p n t -> p (n t)"))
-            bank = bank_tile(first // BLOCK, [P, width])
+            bank = bank_tile(H_BANKS + index % (BANKS - H_BANKS), [P, width])
             nc.tensor.matmul_mx(
                 out=bank[:],
                 lhsT=w2_word[:].bitcast(FP4X4),
@@ -191,8 +195,8 @@ def tile_picked_zappnp_gelu_p_kernel(tc, x_words, x_scales, w1, w2_words, w2_sca
 
         firsts = [sum(STRETCHES[:i]) for i in range(len(STRETCHES))]
         hidden = [first_layer(first, width) for first, width in zip(firsts, STRETCHES)]
-        for first, width, h_rounded in zip(firsts, STRETCHES, hidden):
-            second_layer(first, width, h_rounded)
+        for index, (first, width, h_rounded) in enumerate(zip(firsts, STRETCHES, hidden)):
+            second_layer(index, first, width, h_rounded)
 
         y_cen = keep.tile([P, S], F32, name="y_cen")
         nc.scalar.activation(y_cen[:], y_near[:], COPY, scale=CEN_OVER_NEAR)

@@ -28,6 +28,7 @@ LIST_ROWS = 16
 BLOCK = 128
 SLICE = 256
 H_BANKS = 6
+Y_BANKS = [6, 7, 2, 3, 4]
 BANKS = 8
 
 STRETCHES = [256, 256, 256, 128, 128]
@@ -92,12 +93,8 @@ def tile_picked_zappnp_gelu_p_kernel(tc, x_words, x_scales, w1, w2_words, w2_sca
         for q in range(QUADRANTS):
             nc.sync.dma_start(w2_scale[32 * q : 32 * q + 4, :].bitcast(I32), w2_scales[0, 4 * q : 4 * q + 4, :].bitcast(I32))
         pos_tiles = [load_list(f"pos{d + 1}_tile", src) for d, src in enumerate((pos1, pos2, pos3))]
-        gate_last = keep.tile([P, V], F32, name="gate_last")
-        nc.sync.dma_start(gate_last[:], gate[2])
-        gate_cols = keep.tile([P, 2, 8], F32, name="gate_cols")
-        with nc.allow_non_contiguous_dma(reason="one gate value to a partition"):
-            for d in range(2):
-                nc.sync.dma_start(gate_cols[:, d, 0 : V // P], gate[d, 0, :].rearrange("(c p) -> p c", p=P))
+        gate_tile = keep.tile([P, gate.shape[0], V], F32, name="gate_tile")
+        nc.sync.dma_start(gate_tile[:], gate.rearrange("d p v -> p d v"))
         cen_tile = load_list("cen_tile", cen)
         nxt_tiles = [load_list(f"nxt{d + 1}_tile", src) for d, src in enumerate((nxt1, nxt2, nxt3))]
         root_tile = load_list("root_tile", root)
@@ -178,7 +175,7 @@ def tile_picked_zappnp_gelu_p_kernel(tc, x_words, x_scales, w1, w2_words, w2_sca
             h_word = keep.tile([P, width], U32, name=f"h_word{first}", align_bytes=64)
             h_scale = keep.tile([P, width], U8, name=f"h_scale{first}", align_bytes=64)
             nc.vector.quantize_mx(out=h_word[:].bitcast(FP8X4), scales=h_scale[:], in_=h_rounded[:].rearrange("p n t -> p (n t)"))
-            bank = bank_tile(H_BANKS + index % (BANKS - H_BANKS), [P, width])
+            bank = bank_tile(Y_BANKS[index], [P, width])
             nc.tensor.matmul_mx(
                 out=bank[:],
                 lhsT=w2_word[:].bitcast(FP4X4),
@@ -207,26 +204,20 @@ def tile_picked_zappnp_gelu_p_kernel(tc, x_words, x_scales, w1, w2_words, w2_sca
             return tile
 
         def first_two_on_tensor(name, table, lists):
-            picked = []
-            for d in range(2):
-                tile = keep.tile([P, V], F32, name=f"{name}_picked{d}")
-                nc.vector.tensor_copy(tile[:], table[:].indirect(lists[d][:]))
-                picked.append(tile)
+            half = V // 2
+            first = weighted(f"{name}_term0", table, lists[0][:], gate_tile[:, 0, :], V)
+            second = [weighted(f"{name}_term1_{c0}", table, entries(lists[1], c0, half), gate_tile[:, 1, c0 : c0 + half], half) for c0 in (0, half)]
 
             def finish():
                 total = bank_tile(4, [P, V])
-                for d in range(2):
-                    turned = keep.tile([P, V], F32, name=f"{name}_turned{d}")
-                    for h in range(2):
-                        bank = bank_tile(2 * d + h, [P, 2, P])
-                        for u in range(2):
-                            c = 2 * h + u
-                            nc.tensor.transpose(bank[:, u, :], picked[d][:, c * P : (c + 1) * P], identity[:])
-                        for u in range(2):
-                            c = 2 * h + u
-                            nc.scalar.activation(turned[:, c * P : (c + 1) * P], bank[:, u, :], COPY, scale=gate_cols[:, d, c : c + 1])
-                    for c in range(V // P):
-                        nc.tensor.matmul(total[:, c * P : (c + 1) * P], turned[:, c * P : (c + 1) * P], identity[:], start=(d == 0 and c == 0), stop=(d == 1 and c == V // P - 1), is_transpose=True)
+                turned = keep.tile([P, V], F32, name=f"{name}_turned")
+                for c0 in range(0, V, P):
+                    bank = bank_tile(c0 // P, [P, P])
+                    terms = (first[:, c0 : c0 + P], second[c0 // half][:, c0 % half : c0 % half + P])
+                    for d, term in enumerate(terms):
+                        nc.tensor.matmul(bank[:], term, identity[:], start=(d == 0), stop=(d == 1), is_transpose=True)
+                    nc.scalar.copy(turned[:, c0 : c0 + P], bank[:])
+                    nc.tensor.transpose(total[:, c0 : c0 + P], turned[:, c0 : c0 + P], identity[:])
                 return total
 
             return finish
@@ -257,7 +248,7 @@ def tile_picked_zappnp_gelu_p_kernel(tc, x_words, x_scales, w1, w2_words, w2_sca
                 nc.vector.tensor_tensor(result[:, c0 : c0 + half], term[:], pair[:, c0 : c0 + half], ADD)
             return result
 
-        z_near = propagate("z_near", y_near, pos_tiles, gate_last[:], y_cen, cen_tile, V, first_two_on_tensor)
+        z_near = propagate("z_near", y_near, pos_tiles, gate_tile[:, 2, :], y_cen, cen_tile, V, first_two_on_tensor)
         y_root = keep.tile([P, S], F32, name="y_root")
         nc.scalar.activation(y_root[:], y_near[:], COPY, scale=ROOT_OVER_NEAR)
         result = propagate("result", z_near, nxt_tiles, gate2_tile[:, 2, :], y_root, root_tile, U, first_two_on_vector)

@@ -27,13 +27,16 @@ QUADRANTS = 4
 LIST_ROWS = 16
 BLOCK = 128
 SLICE = 256
-H_BANKS = 6
-Y_BANKS = [6, 7, 2, 3, 4]
-BANKS = 8
+GATE_PITCH = 8
+
+EARLY_BLOCKS = 6
+LATE_BANK_DISTANCE = 4
 
 STRETCHES = [256, 256, 256, 128, 128]
+EARLY_STRETCHES = 3
+Y_BANKS = [6, 7, 0, 1, 4]
 
-SCALAR_GROUPS = [88, 72]
+SCALAR_GROUPS = [88, 52]
 
 NEAR = 0.8 * 0.8
 CEN_OVER_NEAR = 0.2 / 0.8
@@ -47,7 +50,7 @@ def tile_picked_zappnp_gelu_p_kernel(tc, x_words, x_scales, w1, w2_words, w2_sca
         psum = ctx.enter_context(tc.psum_pool(name="psum", bufs=1))
 
         def bank_tile(index, shape):
-            return psum.tile(shape, F32, name=f"bank{index % BANKS}")
+            return psum.tile(shape, F32, name=f"bank{index}")
 
         def load_list(name, src):
             tile = keep.tile([P, src.shape[1]], U16, name=name)
@@ -61,7 +64,7 @@ def tile_picked_zappnp_gelu_p_kernel(tc, x_words, x_scales, w1, w2_words, w2_sca
             return w1[K_PASS * g : K_PASS * (g + 1), :].rearrange("(p j) c -> p j c", j=PACK)
 
         def load_x_words(g):
-            tile = keep.tile([P, T], I32, name=f"x_table{g}", align_bytes=64)
+            tile = keep.tile([P, T], I32, name=f"x_table{g}", tag=f"x_table{g}", align_bytes=64)
             nc.sync.dma_start(tile[:], x_words[g].rearrange("p n t -> p (n t)").bitcast(I32))
             return tile
 
@@ -93,8 +96,12 @@ def tile_picked_zappnp_gelu_p_kernel(tc, x_words, x_scales, w1, w2_words, w2_sca
         for q in range(QUADRANTS):
             nc.sync.dma_start(w2_scale[32 * q : 32 * q + 4, :].bitcast(I32), w2_scales[0, 4 * q : 4 * q + 4, :].bitcast(I32))
         pos_tiles = [load_list(f"pos{d + 1}_tile", src) for d, src in enumerate((pos1, pos2, pos3))]
-        gate_tile = keep.tile([P, gate.shape[0], V], F32, name="gate_tile")
-        nc.sync.dma_start(gate_tile[:], gate.rearrange("d p v -> p d v"))
+        gate_last = keep.tile([P, V], F32, name="gate_last")
+        nc.sync.dma_start(gate_last[:], gate[2])
+        gate_cols = keep.tile([P, 2, GATE_PITCH], F32, name="gate_cols")
+        with nc.allow_non_contiguous_dma(reason="one gate value to a partition"):
+            for d in range(2):
+                nc.sync.dma_start(gate_cols[:, d, 0 : V // P], gate[d, 0, :].rearrange("(c p) -> p c", p=P))
         cen_tile = load_list("cen_tile", cen)
         nxt_tiles = [load_list(f"nxt{d + 1}_tile", src) for d, src in enumerate((nxt1, nxt2, nxt3))]
         root_tile = load_list("root_tile", root)
@@ -107,7 +114,8 @@ def tile_picked_zappnp_gelu_p_kernel(tc, x_words, x_scales, w1, w2_words, w2_sca
         def gather_words(g, dst, first):
             nc.vector.tensor_copy(dst, x_table[g][:].bitcast(U32).indirect(entries(offs_tile, first, SLICE)))
 
-        x0_word = keep.tile([P, S], U32, name="x0_word", align_bytes=64)
+        early_nodes = EARLY_BLOCKS * BLOCK
+        x0_word = keep.tile([P, early_nodes], U32, name="x0_word", align_bytes=64)
         w1_word = {}
         w1_scale = {}
 
@@ -127,8 +135,9 @@ def tile_picked_zappnp_gelu_p_kernel(tc, x_words, x_scales, w1, w2_words, w2_sca
                     w1_scale[(g, t0 + u)] = scales[:, u * P : (u + 1) * P]
 
         quantise_w1(0)
-        for first in range(0, S, SLICE):
+        for first in range(0, early_nodes, SLICE):
             gather_words(0, x0_word[:, first : first + SLICE], first)
+        x0_blocks = [x0_word[:, n0 : n0 + BLOCK] for n0 in range(0, early_nodes, BLOCK)]
 
         def first_layer_pass(g, bank, words, n0):
             for t in range(PACK):
@@ -146,10 +155,10 @@ def tile_picked_zappnp_gelu_p_kernel(tc, x_words, x_scales, w1, w2_words, w2_sca
 
         def open_block():
             b = len(h_banks)
-            h_banks.append(bank_tile(b % H_BANKS, [P, PACK, BLOCK]))
-            first_layer_pass(0, h_banks[b], x0_word[:, b * BLOCK : (b + 1) * BLOCK], b * BLOCK)
+            h_banks.append(bank_tile(b if b < EARLY_BLOCKS else b - LATE_BANK_DISTANCE, [P, PACK, BLOCK]))
+            first_layer_pass(0, h_banks[b], x0_blocks[b], b * BLOCK)
 
-        for b in range(H_BANKS):
+        while len(h_banks) < EARLY_BLOCKS:
             open_block()
         quantise_w1(1)
 
@@ -159,16 +168,19 @@ def tile_picked_zappnp_gelu_p_kernel(tc, x_words, x_scales, w1, w2_words, w2_sca
             tile = keep.tile([P, SLICE], U32, name=f"x1_word{first}", align_bytes=64)
             gather_words(1, tile[:], first)
             x1_word.append(tile)
+        x0_late = keep.tile([P, S - early_nodes], U32, name="x0_late", tag="x_table1", align_bytes=64)
+        gather_words(0, x0_late[:], early_nodes)
+        x0_blocks.extend([x0_late[:, n0 : n0 + BLOCK] for n0 in range(0, S - early_nodes, BLOCK)])
 
         def first_layer(first, width):
             h_rounded = keep.tile([P, width, PACK], BF16, name=f"h_rounded{first}", align_bytes=64)
             for b0 in range(0, width, BLOCK):
                 n0 = first + b0
+                if n0 >= early_nodes:
+                    open_block()
                 bank = h_banks[n0 // BLOCK]
                 first_layer_pass(1, bank, x1_word[n0 // SLICE][:, n0 % SLICE : n0 % SLICE + BLOCK], n0)
                 nc.scalar.activation(h_rounded[:, b0 : b0 + BLOCK, :], bank[:].rearrange("p t n -> p n t"), GELU)
-                if len(h_banks) < S // BLOCK:
-                    open_block()
             return h_rounded
 
         def second_layer(index, first, width, h_rounded):
@@ -191,9 +203,11 @@ def tile_picked_zappnp_gelu_p_kernel(tc, x_words, x_scales, w1, w2_words, w2_sca
                 nc.vector.tensor_scalar(y_near[:, first : first + width], bank[:], NEAR, None, MULT)
 
         firsts = [sum(STRETCHES[:i]) for i in range(len(STRETCHES))]
-        hidden = [first_layer(first, width) for first, width in zip(firsts, STRETCHES)]
-        for index, (first, width, h_rounded) in enumerate(zip(firsts, STRETCHES, hidden)):
-            second_layer(index, first, width, h_rounded)
+        hidden = [first_layer(first, width) for first, width in zip(firsts[:EARLY_STRETCHES], STRETCHES[:EARLY_STRETCHES])]
+        second_layer(0, firsts[0], STRETCHES[0], hidden[0])
+        hidden.extend([first_layer(first, width) for first, width in zip(firsts[EARLY_STRETCHES:], STRETCHES[EARLY_STRETCHES:])])
+        for index in range(1, len(STRETCHES)):
+            second_layer(index, firsts[index], STRETCHES[index], hidden[index])
 
         y_cen = keep.tile([P, S], F32, name="y_cen")
         nc.scalar.activation(y_cen[:], y_near[:], COPY, scale=CEN_OVER_NEAR)
@@ -203,54 +217,49 @@ def tile_picked_zappnp_gelu_p_kernel(tc, x_words, x_scales, w1, w2_words, w2_sca
             nc.vector.tensor_tensor(tile[:], table[:].indirect(offsets), weights, MULT)
             return tile
 
-        def first_two_on_tensor(name, table, lists):
-            half = V // 2
-            first = weighted(f"{name}_term0", table, lists[0][:], gate_tile[:, 0, :], V)
-            second = [weighted(f"{name}_term1_{c0}", table, entries(lists[1], c0, half), gate_tile[:, 1, c0 : c0 + half], half) for c0 in (0, half)]
-
-            def finish():
-                total = bank_tile(4, [P, V])
-                turned = keep.tile([P, V], F32, name=f"{name}_turned")
-                for c0 in range(0, V, P):
-                    bank = bank_tile(c0 // P, [P, P])
-                    terms = (first[:, c0 : c0 + P], second[c0 // half][:, c0 % half : c0 % half + P])
-                    for d, term in enumerate(terms):
-                        nc.tensor.matmul(bank[:], term, identity[:], start=(d == 0), stop=(d == 1), is_transpose=True)
-                    nc.scalar.copy(turned[:, c0 : c0 + P], bank[:])
-                    nc.tensor.transpose(total[:, c0 : c0 + P], turned[:, c0 : c0 + P], identity[:])
-                return total
-
-            return finish
-
-        def first_two_on_vector(name, table, lists):
-            terms = [weighted(f"{name}_term{d}", table, lists[d][:], gate2_tile[:, d, :], U) for d in range(2)]
-
-            def finish():
-                total = keep.tile([P, U], F32, name=name)
-                nc.vector.tensor_tensor(total[:], terms[0][:], terms[1][:], ADD)
-                return total
-
-            return finish
-
-        def propagate(name, table, lists, last_gate, own_table, own_list, width, first_two):
+        def third_neighbour(name, table, list_tile, weights, width):
             half = width // 2
-            halves = (0, half)
-            finish = first_two(f"{name}_pair", table, lists)
-            result = keep.tile([P, width], F32, name=name)
-            third = [weighted(f"{name}_third{c0}", table, entries(lists[2], c0, half), last_gate[:, c0 : c0 + half], half) for c0 in halves]
-            pair = finish()
+            return [weighted(f"{name}_third{c0}", table, entries(list_tile, c0, half), weights[:, c0 : c0 + half], half) for c0 in (0, half)]
+
+        def add_up(name, third, pair, own_table, own_list, width):
+            half = width // 2
+            total = keep.tile([P, width], F32, name=name)
             rest = []
-            for c0, term in zip(halves, third):
+            for c0, term in zip((0, half), third):
                 tile = keep.tile([P, half], F32, name=f"{name}_rest{c0}")
                 nc.vector.tensor_tensor(tile[:], own_table[:].indirect(entries(own_list, c0, half)), term[:], ADD)
                 rest.append(tile)
-            for c0, term in zip(halves, rest):
-                nc.vector.tensor_tensor(result[:, c0 : c0 + half], term[:], pair[:, c0 : c0 + half], ADD)
-            return result
+            for c0, term in zip((0, half), rest):
+                nc.vector.tensor_tensor(total[:, c0 : c0 + half], term[:], pair[:, c0 : c0 + half], ADD)
+            return total
 
-        z_near = propagate("z_near", y_near, pos_tiles, gate_tile[:, 2, :], y_cen, cen_tile, V, first_two_on_tensor)
+        picked = []
+        for d, piece in enumerate((V, V // 2)):
+            tile = keep.tile([P, V], F32, name=f"picked{d}")
+            for c0 in range(0, V, piece):
+                nc.vector.tensor_copy(tile[:, c0 : c0 + piece], y_near[:].indirect(entries(pos_tiles[d], c0, piece)))
+            picked.append(tile)
+        z_third = third_neighbour("z_near", y_near, pos_tiles[2], gate_last[:], V)
+        chunks = V // P
+        z_pair = bank_tile(chunks, [P, V])
+        for d in range(2):
+            gated = keep.tile([P, V], F32, name=f"gated{d}")
+            for c0 in range(0, chunks, 2):
+                bank = bank_tile(2 * d + c0 // 2, [P, 2, P])
+                for c in (c0, c0 + 1):
+                    nc.tensor.transpose(bank[:, c - c0, :], picked[d][:, c * P : (c + 1) * P], identity[:])
+                for c in (c0, c0 + 1):
+                    nc.scalar.activation(gated[:, c * P : (c + 1) * P], bank[:, c - c0, :], COPY, scale=gate_cols[:, d, c : c + 1])
+            for c in range(chunks):
+                nc.tensor.matmul(z_pair[:, c * P : (c + 1) * P], gated[:, c * P : (c + 1) * P], identity[:], start=(d == 0 and c == 0), stop=(d == 1 and c == chunks - 1), is_transpose=True)
+        z_near = add_up("z_near", z_third, z_pair, y_cen, cen_tile, V)
+
         y_root = keep.tile([P, S], F32, name="y_root")
         nc.scalar.activation(y_root[:], y_near[:], COPY, scale=ROOT_OVER_NEAR)
-        result = propagate("result", z_near, nxt_tiles, gate2_tile[:, 2, :], y_root, root_tile, U, first_two_on_vector)
+        first_two = [weighted(f"onward{d}", z_near, nxt_tiles[d][:], gate2_tile[:, d, :], U) for d in range(2)]
+        out_third = third_neighbour("result", z_near, nxt_tiles[2], gate2_tile[:, 2, :], U)
+        out_pair = keep.tile([P, U], F32, name="out_pair")
+        nc.vector.tensor_tensor(out_pair[:], first_two[0][:], first_two[1][:], ADD)
+        result = add_up("result", out_third, out_pair, y_root, root_tile, U)
         for c0 in (0, U // 2):
             nc.sync.dma_start(out[:, c0 : c0 + U // 2], result[:, c0 : c0 + U // 2])

@@ -73,11 +73,6 @@ def tile_picked_zappnp_gelu_p_kernel(tc, x_words, x_scales, w1, w2_words, w2_sca
         w2_scale = keep.tile([P, N], U8, name="w2_scale", align_bytes=64)
         nc.vector.memset(w2_scale[:].bitcast(I32), 0)
 
-        table_in = keep.tile([P, 8], F32, name="table_in")
-        nc.vector.memset(table_in[:], 0.0)
-        table_out = keep.tile([P, 8], F32, name="table_out")
-        nc.scalar.activation(table_out[:], table_in[:], GELU)
-
         identity = keep.tile([P, P], F32, name="identity")
         make_identity(nc, identity[:])
 

@@ -36,7 +36,7 @@ STRETCHES = [256, 256, 256, 128, 128]
 EARLY_STRETCHES = 3
 Y_BANKS = [6, 7, 0, 1, 4]
 
-SCALAR_GROUPS = [88, 52]
+SCALAR_GROUPS = [56, 52]
 
 NEAR = 0.8 * 0.8
 CEN_OVER_NEAR = 0.2 / 0.8
@@ -69,7 +69,7 @@ def tile_picked_zappnp_gelu_p_kernel(tc, x_words, x_scales, w1, w2_words, w2_sca
             return tile
 
         x_scale_table = keep.tile([P, T], U8, name="x_scale_table", align_bytes=64)
-        nc.vector.memset(x_scale_table[:].bitcast(I32), 0)
+        nc.gpsimd.memset(x_scale_table[:].bitcast(I32), 0)
         w2_scale = keep.tile([P, N], U8, name="w2_scale", align_bytes=64)
         nc.vector.memset(w2_scale[:].bitcast(I32), 0)
 
@@ -77,16 +77,15 @@ def tile_picked_zappnp_gelu_p_kernel(tc, x_words, x_scales, w1, w2_words, w2_sca
         make_identity(nc, identity[:])
 
         offs_tile = load_list("offs_tile", offs)
-        for q in range(QUADRANTS):
+        for q in (2, 3, 0, 1):
             nc.sync.dma_start(x_scale_table[32 * q : 32 * q + 4 * PASSES, :].bitcast(I32), x_scales[:, 4 * q : 4 * q + 4, :].bitcast(I32))
+        w2_word = keep.tile([P, 2 * N], U8, name="w2_word", align_bytes=64)
+        nc.sync.dma_start(w2_word[:].bitcast(I32), w2_words[0].bitcast(I32))
         w1_raw = [keep.tile([P, PACK, H], F32, name=f"w1_raw{g}") for g in range(PASSES)]
-        for j in range(0, PACK, 2):
-            nc.sync.dma_start(w1_raw[0][:, j : j + 2, :], w1_rows(0)[:, j : j + 2, :])
+        nc.sync.dma_start(w1_raw[0][:], w1_rows(0))
         x_table = [load_x_words(0)]
         nc.sync.dma_start(w1_raw[1][:], w1_rows(1))
         x_table.append(load_x_words(1))
-        w2_word = keep.tile([P, 2 * N], U8, name="w2_word", align_bytes=64)
-        nc.sync.dma_start(w2_word[:].bitcast(I32), w2_words[0].bitcast(I32))
 
         for q in range(QUADRANTS):
             nc.sync.dma_start(w2_scale[32 * q : 32 * q + 4, :].bitcast(I32), w2_scales[0, 4 * q : 4 * q + 4, :].bitcast(I32))
@@ -110,12 +109,11 @@ def tile_picked_zappnp_gelu_p_kernel(tc, x_words, x_scales, w1, w2_words, w2_sca
             nc.vector.tensor_copy(dst, x_table[g][:].bitcast(U32).indirect(entries(offs_tile, first, SLICE)))
 
         early_nodes = EARLY_BLOCKS * BLOCK
-        x0_word = keep.tile([P, early_nodes], U32, name="x0_word", align_bytes=64)
         w1_word = {}
         w1_scale = {}
 
         def quantise_w1(g):
-            rounded = keep.tile([P, PACK, P, PACK], BF16, name=f"w1_rounded{g}", align_bytes=64)
+            rounded = keep.tile([P, PACK, P, PACK], BF16, name=f"w1_rounded{g}", tag=f"w1_rounded{g}", align_bytes=64)
             src = w1_raw[g][:].rearrange("p j (m t) -> p m t j", t=PACK)
             dst = rounded[:].rearrange("p t m j -> p m t j")
             split = SCALAR_GROUPS[g]
@@ -130,6 +128,7 @@ def tile_picked_zappnp_gelu_p_kernel(tc, x_words, x_scales, w1, w2_words, w2_sca
                     w1_scale[(g, t0 + u)] = scales[:, u * P : (u + 1) * P]
 
         quantise_w1(0)
+        x0_word = keep.tile([P, early_nodes], U32, name="x0_word", tag="w1_rounded0", align_bytes=64)
         for first in range(0, early_nodes, SLICE):
             gather_words(0, x0_word[:, first : first + SLICE], first)
         x0_blocks = [x0_word[:, n0 : n0 + BLOCK] for n0 in range(0, early_nodes, BLOCK)]

@@ -36,7 +36,7 @@ STRETCHES = [256, 256, 256, 128, 128]
 EARLY_STRETCHES = 3
 Y_BANKS = [6, 7, 0, 1, 4]
 
-SCALAR_GROUPS = [56, 52]
+SCALAR_GROUPS = [64, 52]
 
 NEAR = 0.8 * 0.8
 CEN_OVER_NEAR = 0.2 / 0.8
@@ -76,16 +76,21 @@ def tile_picked_zappnp_gelu_p_kernel(tc, x_words, x_scales, w1, w2_words, w2_sca
         identity = keep.tile([P, P], F32, name="identity")
         make_identity(nc, identity[:])
 
+        warm = keep.tile([P, 2], F32, name="warm")
+        nc.vector.memset(warm[:, 0:1], 0.0)
+        nc.scalar.activation(warm[:, 1:2], warm[:, 0:1], GELU)
+
         offs_tile = load_list("offs_tile", offs)
         for q in (2, 3, 0, 1):
             nc.sync.dma_start(x_scale_table[32 * q : 32 * q + 4 * PASSES, :].bitcast(I32), x_scales[:, 4 * q : 4 * q + 4, :].bitcast(I32))
-        w2_word = keep.tile([P, 2 * N], U8, name="w2_word", align_bytes=64)
-        nc.sync.dma_start(w2_word[:].bitcast(I32), w2_words[0].bitcast(I32))
         w1_raw = [keep.tile([P, PACK, H], F32, name=f"w1_raw{g}") for g in range(PASSES)]
-        nc.sync.dma_start(w1_raw[0][:], w1_rows(0))
+        nc.sync.dma_start(w1_raw[0][:, 0:1, :], w1_rows(0)[:, 0:1, :])
+        nc.sync.dma_start(w1_raw[0][:, 1:PACK, :], w1_rows(0)[:, 1:PACK, :])
         x_table = [load_x_words(0)]
         nc.sync.dma_start(w1_raw[1][:], w1_rows(1))
         x_table.append(load_x_words(1))
+        w2_word = keep.tile([P, 2 * N], U8, name="w2_word", align_bytes=64)
+        nc.sync.dma_start(w2_word[:].bitcast(I32), w2_words[0].bitcast(I32))
 
         for q in range(QUADRANTS):
             nc.sync.dma_start(w2_scale[32 * q : 32 * q + 4, :].bitcast(I32), w2_scales[0, 4 * q : 4 * q + 4, :].bitcast(I32))

@@ -35,6 +35,7 @@ LATE_BANK_DISTANCE = 4
 STRETCHES = [256, 256, 256, 128, 128]
 EARLY_STRETCHES = 3
 Y_BANKS = [6, 7, 0, 1, 4]
+VECTOR_STRETCHES = 2
 
 SCALAR_GROUPS = [64, 52]
 
@@ -196,10 +197,10 @@ def tile_picked_zappnp_gelu_p_kernel(tc, x_words, x_scales, w1, w2_words, w2_sca
                 start=True,
                 stop=True,
             )
-            if width == BLOCK:
-                nc.scalar.activation(y_near[:, first : first + width], bank[:], COPY, scale=NEAR)
-            else:
+            if index < VECTOR_STRETCHES:
                 nc.vector.tensor_scalar(y_near[:, first : first + width], bank[:], NEAR, None, MULT)
+            else:
+                nc.scalar.activation(y_near[:, first : first + width], bank[:], COPY, scale=NEAR)
 
         firsts = [sum(STRETCHES[:i]) for i in range(len(STRETCHES))]
         hidden = [first_layer(first, width) for first, width in zip(firsts[:EARLY_STRETCHES], STRETCHES[:EARLY_STRETCHES])]

@@ -1,7 +1,6 @@
 from contextlib import ExitStack
 
 import concourse.mybir as mybir
-from concourse.masks import make_identity
 
 K, T, S, V, H, N, U = 1024, 2048, 1024, 512, 512, 128, 256
 FLOPS = 2 * K * H * S + 2 * H * N * S
@@ -74,9 +73,6 @@ def tile_picked_zappnp_gelu_p_kernel(tc, x_words, x_scales, w1, w2_words, w2_sca
         w2_scale = keep.tile([P, N], U8, name="w2_scale", align_bytes=64)
         nc.vector.memset(w2_scale[:].bitcast(I32), 0)
 
-        identity = keep.tile([P, P], F32, name="identity")
-        make_identity(nc, identity[:])
-
         warm = keep.tile([P, 2], F32, name="warm")
         nc.vector.memset(warm[:, 0:1], 0.0)
         nc.scalar.activation(warm[:, 1:2], warm[:, 0:1], GELU)
@@ -96,12 +92,8 @@ def tile_picked_zappnp_gelu_p_kernel(tc, x_words, x_scales, w1, w2_words, w2_sca
         for q in range(QUADRANTS):
             nc.sync.dma_start(w2_scale[32 * q : 32 * q + 4, :].bitcast(I32), w2_scales[0, 4 * q : 4 * q + 4, :].bitcast(I32))
         pos_tiles = [load_list(f"pos{d + 1}_tile", src) for d, src in enumerate((pos1, pos2, pos3))]
-        gate_last = keep.tile([P, V], F32, name="gate_last")
-        nc.sync.dma_start(gate_last[:], gate[2])
-        gate_cols = keep.tile([P, 2, GATE_PITCH], F32, name="gate_cols")
-        with nc.allow_non_contiguous_dma(reason="one gate value to a partition"):
-            for d in range(2):
-                nc.sync.dma_start(gate_cols[:, d, 0 : V // P], gate[d, 0, :].rearrange("(c p) -> p c", p=P))
+        gate_tile = keep.tile([P, gate.shape[0], V], F32, name="gate_tile")
+        nc.sync.dma_start(gate_tile[:], gate.rearrange("d p v -> p d v"))
         cen_tile = load_list("cen_tile", cen)
         nxt_tiles = [load_list(f"nxt{d + 1}_tile", src) for d, src in enumerate((nxt1, nxt2, nxt3))]
         root_tile = load_list("root_tile", root)
@@ -209,57 +201,44 @@ def tile_picked_zappnp_gelu_p_kernel(tc, x_words, x_scales, w1, w2_words, w2_sca
         for index in range(1, len(STRETCHES)):
             second_layer(index, firsts[index], STRETCHES[index], hidden[index])
 
-        y_cen = keep.tile([P, S], F32, name="y_cen")
-        nc.scalar.activation(y_cen[:], y_near[:], COPY, scale=CEN_OVER_NEAR)
+        def propagate(name, table, lists, gates, own, width):
+            half = width // 2
+            starts = (0, half)
 
-        def weighted(name, table, offsets, weights, width):
+            def halves(label):
+                return [keep.tile([P, half], F32, name=f"{name}_{label}{c0}") for c0 in starts]
+
+            picked = []
+            for d in (1, 2):
+                tiles = halves(f"picked{d}")
+                for c0, tile in zip(starts, tiles):
+                    nc.scalar.activation(tile[:], table[:].indirect(entries(lists[d], c0, half)), COPY)
+                picked.append(tiles)
+            own_terms = own()
+            total = halves("sum0")
+            for c0, tile in zip(starts, total):
+                nc.vector.tensor_tensor(tile[:], table[:].indirect(entries(lists[0], c0, half)), gates[:, 0, c0 : c0 + half], MULT)
+            for d in (1, 2):
+                terms = halves(f"term{d}")
+                for c0, tile, src in zip(starts, terms, picked[d - 1]):
+                    nc.vector.tensor_tensor(tile[:], src[:], gates[:, d, c0 : c0 + half], MULT)
+                sums = halves(f"sum{d}")
+                for tile, a, b in zip(sums, total, terms):
+                    nc.vector.tensor_tensor(tile[:], a[:], b[:], ADD)
+                total = sums
+            result = keep.tile([P, width], F32, name=name)
+            for c0, a, b in zip(starts, total, own_terms):
+                nc.vector.tensor_tensor(result[:, c0 : c0 + half], a[:], b, ADD)
+            return result
+
+        def own_term(name, list_tile, width, piece, factor):
             tile = keep.tile([P, width], F32, name=name)
-            nc.vector.tensor_tensor(tile[:], table[:].indirect(offsets), weights, MULT)
-            return tile
+            for c0 in range(0, width, piece):
+                nc.scalar.activation(tile[:, c0 : c0 + piece], y_near[:].indirect(entries(list_tile, c0, piece)), COPY, scale=factor)
+            return [tile[:, 0 : width // 2], tile[:, width // 2 : width]]
 
-        def third_neighbour(name, table, list_tile, weights, width):
-            half = width // 2
-            return [weighted(f"{name}_third{c0}", table, entries(list_tile, c0, half), weights[:, c0 : c0 + half], half) for c0 in (0, half)]
-
-        def add_up(name, third, pair, own_table, own_list, width):
-            half = width // 2
-            total = keep.tile([P, width], F32, name=name)
-            rest = []
-            for c0, term in zip((0, half), third):
-                tile = keep.tile([P, half], F32, name=f"{name}_rest{c0}")
-                nc.vector.tensor_tensor(tile[:], own_table[:].indirect(entries(own_list, c0, half)), term[:], ADD)
-                rest.append(tile)
-            for c0, term in zip((0, half), rest):
-                nc.vector.tensor_tensor(total[:, c0 : c0 + half], term[:], pair[:, c0 : c0 + half], ADD)
-            return total
-
-        picked = []
-        for d, piece in enumerate((V, V // 2)):
-            tile = keep.tile([P, V], F32, name=f"picked{d}")
-            for c0 in range(0, V, piece):
-                nc.vector.tensor_copy(tile[:, c0 : c0 + piece], y_near[:].indirect(entries(pos_tiles[d], c0, piece)))
-            picked.append(tile)
-        z_third = third_neighbour("z_near", y_near, pos_tiles[2], gate_last[:], V)
-        chunks = V // P
-        z_pair = bank_tile(chunks, [P, V])
-        for d in range(2):
-            gated = keep.tile([P, V], F32, name=f"gated{d}")
-            for c0 in range(0, chunks, 2):
-                bank = bank_tile(2 * d + c0 // 2, [P, 2, P])
-                for c in (c0, c0 + 1):
-                    nc.tensor.transpose(bank[:, c - c0, :], picked[d][:, c * P : (c + 1) * P], identity[:])
-                for c in (c0, c0 + 1):
-                    nc.scalar.activation(gated[:, c * P : (c + 1) * P], bank[:, c - c0, :], COPY, scale=gate_cols[:, d, c : c + 1])
-            for c in range(chunks):
-                nc.tensor.matmul(z_pair[:, c * P : (c + 1) * P], gated[:, c * P : (c + 1) * P], identity[:], start=(d == 0 and c == 0), stop=(d == 1 and c == chunks - 1), is_transpose=True)
-        z_near = add_up("z_near", z_third, z_pair, y_cen, cen_tile, V)
-
-        y_root = keep.tile([P, S], F32, name="y_root")
-        nc.scalar.activation(y_root[:], y_near[:], COPY, scale=ROOT_OVER_NEAR)
-        first_two = [weighted(f"onward{d}", z_near, nxt_tiles[d][:], gate2_tile[:, d, :], U) for d in range(2)]
-        out_third = third_neighbour("result", z_near, nxt_tiles[2], gate2_tile[:, 2, :], U)
-        out_pair = keep.tile([P, U], F32, name="out_pair")
-        nc.vector.tensor_tensor(out_pair[:], first_two[0][:], first_two[1][:], ADD)
-        result = add_up("result", out_third, out_pair, y_root, root_tile, U)
+        z_near = propagate("z_near", y_near, pos_tiles, gate_tile, lambda: own_term("cen_term", cen_tile, V, V // 2, CEN_OVER_NEAR), V)
+        root_term = own_term("root_term", root_tile, U, U, ROOT_OVER_NEAR)
+        result = propagate("result", z_near, nxt_tiles, gate2_tile, lambda: root_term, U)
         for c0 in (0, U // 2):
             nc.sync.dma_start(out[:, c0 : c0 + U // 2], result[:, c0 : c0 + U // 2])

@@ -26,18 +26,13 @@ QUADRANTS = 4
 LIST_ROWS = 16
 BLOCK = 128
 SLICE = 256
-GATE_PITCH = 8
-
 EARLY_BLOCKS = 6
-LATE_BANK_DISTANCE = 4
-
-STRETCHES = [256, 256, 256, 128, 128]
-EARLY_STRETCHES = 3
-Y_BANKS = [6, 7, 0, 1, 4]
-VECTOR_STRETCHES = 2
-
-SCALAR_GROUPS = [64, 52]
-
+OPEN_AHEAD = 6
+LAST_SLICES = [128,128,256,256,256]
+STRETCHES = [256,256,256,128,128]
+Y_BANKS = [0,1,2,3,4]
+VECTOR_STRETCHES = [0,1,4]
+SCALAR_GROUPS = [64,52]
 NEAR = 0.8 * 0.8
 CEN_OVER_NEAR = 0.2 / 0.8
 ROOT_OVER_NEAR = 0.2 / NEAR
@@ -88,7 +83,6 @@ def tile_picked_zappnp_gelu_p_kernel(tc, x_words, x_scales, w1, w2_words, w2_sca
         x_table.append(load_x_words(1))
         w2_word = keep.tile([P, 2 * N], U8, name="w2_word", align_bytes=64)
         nc.sync.dma_start(w2_word[:].bitcast(I32), w2_words[0].bitcast(I32))
-
         for q in range(QUADRANTS):
             nc.sync.dma_start(w2_scale[32 * q : 32 * q + 4, :].bitcast(I32), w2_scales[0, 4 * q : 4 * q + 4, :].bitcast(I32))
         pos_tiles = [load_list(f"pos{d + 1}_tile", src) for d, src in enumerate((pos1, pos2, pos3))]
@@ -103,8 +97,8 @@ def tile_picked_zappnp_gelu_p_kernel(tc, x_words, x_scales, w1, w2_words, w2_sca
         x_scale = keep.tile([P, S], U8, name="x_scale", align_bytes=64)
         nc.vector.tensor_copy(x_scale[:], x_scale_table[:].indirect(offs_tile[:]))
 
-        def gather_words(g, dst, first):
-            nc.vector.tensor_copy(dst, x_table[g][:].bitcast(U32).indirect(entries(offs_tile, first, SLICE)))
+        def gather_words(g, dst, first, count):
+            nc.vector.tensor_copy(dst, x_table[g][:].bitcast(U32).indirect(entries(offs_tile, first, count)))
 
         early_nodes = EARLY_BLOCKS * BLOCK
         w1_word = {}
@@ -125,13 +119,7 @@ def tile_picked_zappnp_gelu_p_kernel(tc, x_words, x_scales, w1, w2_words, w2_sca
                     w1_word[(g, t0 + u)] = words[:, u * P : (u + 1) * P]
                     w1_scale[(g, t0 + u)] = scales[:, u * P : (u + 1) * P]
 
-        quantise_w1(0)
-        x0_word = keep.tile([P, early_nodes], U32, name="x0_word", tag="w1_rounded0", align_bytes=64)
-        for first in range(0, early_nodes, SLICE):
-            gather_words(0, x0_word[:, first : first + SLICE], first)
-        x0_blocks = [x0_word[:, n0 : n0 + BLOCK] for n0 in range(0, early_nodes, BLOCK)]
-
-        def first_layer_pass(g, bank, words, n0):
+        def first_layer_pass(g, bank, words, n0, opens):
             for t in range(PACK):
                 nc.tensor.matmul_mx(
                     out=bank[:, t, :],
@@ -139,40 +127,43 @@ def tile_picked_zappnp_gelu_p_kernel(tc, x_words, x_scales, w1, w2_words, w2_sca
                     lhsT_scale=w1_scale[(g, t)],
                     rhs=words.bitcast(FP8X4),
                     rhs_scale=x_scale[4 * g : P, n0 : n0 + BLOCK],
-                    start=(g == 0 and t == 0),
-                    stop=(g == PASSES - 1 and t == PACK - 1),
+                    start=(opens and t == 0),
+                    stop=(not opens and t == PACK - 1),
                 )
 
-        h_banks = []
+        h_banks = [bank_tile(b, [P, PACK, BLOCK]) for b in range(S // BLOCK)]
+        x0_blocks = []
 
-        def open_block():
-            b = len(h_banks)
-            h_banks.append(bank_tile(b if b < EARLY_BLOCKS else b - LATE_BANK_DISTANCE, [P, PACK, BLOCK]))
-            first_layer_pass(0, h_banks[b], x0_blocks[b], b * BLOCK)
-
-        while len(h_banks) < EARLY_BLOCKS:
-            open_block()
+        quantise_w1(0)
+        x0_word = keep.tile([P, early_nodes], U32, name="x0_word", tag="w1_rounded0", align_bytes=64)
+        for first in range(0, early_nodes, SLICE):
+            count = min(SLICE, early_nodes - first)
+            gather_words(0, x0_word[:, first : first + count], first, count)
+        x0_blocks.extend([x0_word[:, n0 : n0 + BLOCK] for n0 in range(0, early_nodes, BLOCK)])
+        for b in range(OPEN_AHEAD):
+            first_layer_pass(0, h_banks[b], x0_blocks[b], b * BLOCK, True)
         quantise_w1(1)
 
         y_near = keep.tile([P, S], F32, name="y_near")
-        x1_word = []
-        for first in range(0, S, SLICE):
-            tile = keep.tile([P, SLICE], U32, name=f"x1_word{first}", align_bytes=64)
-            gather_words(1, tile[:], first)
-            x1_word.append(tile)
+        x1_blocks = []
+        first = 0
+        for count in LAST_SLICES:
+            tile = keep.tile([P, count], U32, name=f"x1_word{first}", align_bytes=64)
+            gather_words(1, tile[:], first, count)
+            x1_blocks.extend([tile[:, n0 : n0 + BLOCK] for n0 in range(0, count, BLOCK)])
+            first = first + count
         x0_late = keep.tile([P, S - early_nodes], U32, name="x0_late", tag="x_table1", align_bytes=64)
-        gather_words(0, x0_late[:], early_nodes)
+        gather_words(0, x0_late[:], early_nodes, S - early_nodes)
         x0_blocks.extend([x0_late[:, n0 : n0 + BLOCK] for n0 in range(0, S - early_nodes, BLOCK)])
 
         def first_layer(first, width):
             h_rounded = keep.tile([P, width, PACK], BF16, name=f"h_rounded{first}", align_bytes=64)
             for b0 in range(0, width, BLOCK):
-                n0 = first + b0
-                if n0 >= early_nodes:
-                    open_block()
-                bank = h_banks[n0 // BLOCK]
-                first_layer_pass(1, bank, x1_word[n0 // SLICE][:, n0 % SLICE : n0 % SLICE + BLOCK], n0)
-                nc.scalar.activation(h_rounded[:, b0 : b0 + BLOCK, :], bank[:].rearrange("p t n -> p n t"), GELU)
+                b = (first + b0) // BLOCK
+                first_layer_pass(1, h_banks[b], x1_blocks[b], b * BLOCK, b >= OPEN_AHEAD)
+                if b >= OPEN_AHEAD:
+                    first_layer_pass(0, h_banks[b], x0_blocks[b], b * BLOCK, False)
+                nc.scalar.activation(h_rounded[:, b0 : b0 + BLOCK, :], h_banks[b][:].rearrange("p t n -> p n t"), GELU)
             return h_rounded
 
         def second_layer(index, first, width, h_rounded):
@@ -189,56 +180,59 @@ def tile_picked_zappnp_gelu_p_kernel(tc, x_words, x_scales, w1, w2_words, w2_sca
                 start=True,
                 stop=True,
             )
-            if index < VECTOR_STRETCHES:
+            if index in VECTOR_STRETCHES:
                 nc.vector.tensor_scalar(y_near[:, first : first + width], bank[:], NEAR, None, MULT)
             else:
                 nc.scalar.activation(y_near[:, first : first + width], bank[:], COPY, scale=NEAR)
 
         firsts = [sum(STRETCHES[:i]) for i in range(len(STRETCHES))]
-        hidden = [first_layer(first, width) for first, width in zip(firsts[:EARLY_STRETCHES], STRETCHES[:EARLY_STRETCHES])]
+        early_stretches = len([f for f, w in zip(firsts, STRETCHES) if f + w <= early_nodes])
+        hidden = [first_layer(first, width) for first, width in zip(firsts[:early_stretches], STRETCHES[:early_stretches])]
         second_layer(0, firsts[0], STRETCHES[0], hidden[0])
-        hidden.extend([first_layer(first, width) for first, width in zip(firsts[EARLY_STRETCHES:], STRETCHES[EARLY_STRETCHES:])])
+        hidden.extend([first_layer(first, width) for first, width in zip(firsts[early_stretches:], STRETCHES[early_stretches:])])
         for index in range(1, len(STRETCHES)):
             second_layer(index, firsts[index], STRETCHES[index], hidden[index])
 
-        def propagate(name, table, lists, gates, own, width):
-            half = width // 2
-            starts = (0, half)
+        def fresh(name, width, tag=None):
+            return keep.tile([P, width], F32, name=name, tag=tag or name)
 
-            def halves(label):
-                return [keep.tile([P, half], F32, name=f"{name}_{label}{c0}") for c0 in starts]
+        def pick(name, table, list_tile, first, count, factor=1.0, tag=None):
+            tile = fresh(name, count, tag)
+            nc.scalar.activation(tile[:], table[:].indirect(entries(list_tile, first, count)), COPY, scale=factor)
+            return tile[:]
 
-            picked = []
-            for d in (1, 2):
-                tiles = halves(f"picked{d}")
-                for c0, tile in zip(starts, tiles):
-                    nc.scalar.activation(tile[:], table[:].indirect(entries(lists[d], c0, half)), COPY)
-                picked.append(tiles)
-            own_terms = own()
-            total = halves("sum0")
-            for c0, tile in zip(starts, total):
-                nc.vector.tensor_tensor(tile[:], table[:].indirect(entries(lists[0], c0, half)), gates[:, 0, c0 : c0 + half], MULT)
-            for d in (1, 2):
-                terms = halves(f"term{d}")
-                for c0, tile, src in zip(starts, terms, picked[d - 1]):
-                    nc.vector.tensor_tensor(tile[:], src[:], gates[:, d, c0 : c0 + half], MULT)
-                sums = halves(f"sum{d}")
-                for tile, a, b in zip(sums, total, terms):
-                    nc.vector.tensor_tensor(tile[:], a[:], b[:], ADD)
-                total = sums
-            result = keep.tile([P, width], F32, name=name)
-            for c0, a, b in zip(starts, total, own_terms):
-                nc.vector.tensor_tensor(result[:, c0 : c0 + half], a[:], b, ADD)
-            return result
+        def pick_gated(name, table, list_tile, first, count, gates):
+            tile = fresh(name, count)
+            nc.vector.tensor_tensor(tile[:], table[:].indirect(entries(list_tile, first, count)), gates[:, first : first + count], MULT)
+            return tile[:]
 
-        def own_term(name, list_tile, width, piece, factor):
-            tile = keep.tile([P, width], F32, name=name)
-            for c0 in range(0, width, piece):
-                nc.scalar.activation(tile[:, c0 : c0 + piece], y_near[:].indirect(entries(list_tile, c0, piece)), COPY, scale=factor)
-            return [tile[:, 0 : width // 2], tile[:, width // 2 : width]]
+        def combine(name, a, b, op, dst=None):
+            if dst is None:
+                dst = fresh(name, a.shape[1])[:]
+            nc.vector.tensor_tensor(dst, a, b, op)
+            return dst
 
-        z_near = propagate("z_near", y_near, pos_tiles, gate_tile, lambda: own_term("cen_term", cen_tile, V, V // 2, CEN_OVER_NEAR), V)
-        root_term = own_term("root_term", root_tile, U, U, ROOT_OVER_NEAR)
-        result = propagate("result", z_near, nxt_tiles, gate2_tile, lambda: root_term, U)
-        for c0 in (0, U // 2):
-            nc.sync.dma_start(out[:, c0 : c0 + U // 2], result[:, c0 : c0 + U // 2])
+        half = V // 2
+        starts = (0, half)
+        picked = [[pick(f"picked{d}_{c0}", y_near, pos_tiles[d], c0, half) for c0 in starts] for d in (1, 2)]
+        own = [pick(f"cen{c0}", y_near, cen_tile, c0, half, CEN_OVER_NEAR) for c0 in starts]
+        root_term = pick("root_term", y_near, root_tile, 0, U, ROOT_OVER_NEAR)
+        total = [pick_gated(f"near0_{c0}", y_near, pos_tiles[0], c0, half, gate_tile[:, 0, :]) for c0 in starts]
+        for d in (1, 2):
+            terms = [combine(f"near{d}_{c0}", src, gate_tile[:, d, c0 : c0 + half], MULT) for c0, src in zip(starts, picked[d - 1])]
+            total = [combine(f"sum{d}_{c0}", a, b, ADD) for c0, a, b in zip(starts, total, terms)]
+        z_near = fresh("z_near", V)
+        for c0, a, b in zip(starts, total, own):
+            combine(None, a, b, ADD, z_near[:, c0 : c0 + half])
+
+        half = U // 2
+        starts = (0, half)
+        onward = [[pick(f"onward{d}_{c0}", z_near, nxt_tiles[d], c0, half) for c0 in starts] for d in (1, 2)]
+        total = [pick_gated(f"onward0_{c0}", z_near, nxt_tiles[0], c0, half, gate2_tile[:, 0, :]) for c0 in starts]
+        total = [combine(f"with_root{c0}", a, root_term[:, c0 : c0 + half], ADD) for c0, a in zip(starts, total)]
+        result = fresh("result", U)
+        for d in (1, 2):
+            terms = [combine(f"far{d}_{c0}", src, gate2_tile[:, d, c0 : c0 + half], MULT) for c0, src in zip(starts, onward[d - 1])]
+            total = [combine(f"far_sum{d}_{c0}", a, b, ADD, result[:, c0 : c0 + half] if d == 2 else None) for c0, a, b in zip(starts, total, terms)]
+        for c0 in starts:
+            nc.sync.dma_start(out[:, c0 : c0 + half], result[:, c0 : c0 + half])

@@ -73,8 +73,11 @@ def tile_picked_zappnp_gelu_p_kernel(tc, x_words, x_scales, w1, w2_words, w2_sca
         nc.scalar.activation(warm[:, 1:2], warm[:, 0:1], GELU)
 
         offs_tile = load_list("offs_tile", offs)
-        for q in (2, 3, 0, 1):
+        for q in (2, 3):
             nc.sync.dma_start(x_scale_table[32 * q : 32 * q + 4 * PASSES, :].bitcast(I32), x_scales[:, 4 * q : 4 * q + 4, :].bitcast(I32))
+        for q in (0, 1):
+            for g in range(PASSES):
+                nc.sync.dma_start(x_scale_table[32 * q + 4 * g : 32 * q + 4 * g + 4, :].bitcast(I32), x_scales[g, 4 * q : 4 * q + 4, :].bitcast(I32))
         w1_raw = [keep.tile([P, PACK, H], F32, name=f"w1_raw{g}") for g in range(PASSES)]
         nc.sync.dma_start(w1_raw[0][:, 0:1, :], w1_rows(0)[:, 0:1, :])
         nc.sync.dma_start(w1_raw[0][:, 1:PACK, :], w1_rows(0)[:, 1:PACK, :])
@@ -214,16 +217,25 @@ def tile_picked_zappnp_gelu_p_kernel(tc, x_words, x_scales, w1, w2_words, w2_sca
 
         half = V // 2
         starts = (0, half)
-        picked = [[pick(f"picked{d}_{c0}", y_near, pos_tiles[d], c0, half) for c0 in starts] for d in (1, 2)]
-        own = [pick(f"cen{c0}", y_near, cen_tile, c0, half, CEN_OVER_NEAR) for c0 in starts]
+        share = 64
+        second = [pick("picked1_0", y_near, pos_tiles[1], share, half - share), pick("picked1_1", y_near, pos_tiles[1], half, half)]
+        third = [pick(f"picked2_{c0}", y_near, pos_tiles[2], c0, half) for c0 in starts]
+        own_pieces = [(0, 256), (256, 128), (384, 128)]
+        own = [pick(f"cen{c0}", y_near, cen_tile, c0, width, CEN_OVER_NEAR) for c0, width in own_pieces]
         root_term = pick("root_term", y_near, root_tile, 0, U, ROOT_OVER_NEAR)
-        total = [pick_gated(f"near0_{c0}", y_near, pos_tiles[0], c0, half, gate_tile[:, 0, :]) for c0 in starts]
-        for d in (1, 2):
-            terms = [combine(f"near{d}_{c0}", src, gate_tile[:, d, c0 : c0 + half], MULT) for c0, src in zip(starts, picked[d - 1])]
-            total = [combine(f"sum{d}_{c0}", a, b, ADD) for c0, a, b in zip(starts, total, terms)]
+        first_terms = [pick_gated(f"near0_{c0}", y_near, pos_tiles[0], c0, half, gate_tile[:, 0, :]) for c0 in starts]
+        second_terms = [fresh(f"near1_{c0}", half)[:] for c0 in starts]
+        nc.vector.tensor_tensor(second_terms[0][:, 0:share], y_near[:].indirect(entries(pos_tiles[1], 0, share)), gate_tile[:, 1, 0:share], MULT)
+        combine(None, second[0], gate_tile[:, 1, share:half], MULT, second_terms[0][:, share:half])
+        combine(None, second[1], gate_tile[:, 1, half:V], MULT, second_terms[1])
+        total = [combine(f"sum1_{c0}", a, b, ADD) for c0, a, b in zip(starts, first_terms, second_terms)]
+        terms = [combine(f"near2_{c0}", src, gate_tile[:, 2, c0 : c0 + half], MULT) for c0, src in zip(starts, third)]
+        neighbours = fresh("neighbours", V)
+        for c0, a, b in zip(starts, total, terms):
+            combine(None, a, b, ADD, neighbours[:, c0 : c0 + half])
         z_near = fresh("z_near", V)
-        for c0, a, b in zip(starts, total, own):
-            combine(None, a, b, ADD, z_near[:, c0 : c0 + half])
+        for (c0, width), b in zip(own_pieces, own):
+            combine(None, neighbours[:, c0 : c0 + width], b, ADD, z_near[:, c0 : c0 + width])
 
         half = U // 2
         starts = (0, half)

@@ -68,10 +68,6 @@ def tile_picked_zappnp_gelu_p_kernel(tc, x_words, x_scales, w1, w2_words, w2_sca
         w2_scale = keep.tile([P, N], U8, name="w2_scale", align_bytes=64)
         nc.vector.memset(w2_scale[:].bitcast(I32), 0)
 
-        warm = keep.tile([P, 2], F32, name="warm")
-        nc.vector.memset(warm[:, 0:1], 0.0)
-        nc.scalar.activation(warm[:, 1:2], warm[:, 0:1], GELU)
-
         offs_tile = load_list("offs_tile", offs)
         for q in (2, 3):
             nc.sync.dma_start(x_scale_table[32 * q : 32 * q + 4 * PASSES, :].bitcast(I32), x_scales[:, 4 * q : 4 * q + 4, :].bitcast(I32))

@@ -24,15 +24,20 @@ K_PASS = P * PACK
 PASSES = K // K_PASS
 QUADRANTS = 4
 LIST_ROWS = 16
-BLOCK = 128
+BATCH = 128
 SLICE = 256
-EARLY_BLOCKS = 6
-OPEN_AHEAD = 6
-LAST_SLICES = [128,128,256,256,256]
-STRETCHES = [256,256,256,128,128]
-Y_BANKS = [0,1,2,3,4]
-VECTOR_STRETCHES = [0,1,4]
-SCALAR_GROUPS = [64,52]
+
+EARLY_BATCHES = 6
+LAST_SLICES = [128, 128, 256, 256, 256]
+
+STRETCHES = [256, 256, 256, 128, 128]
+VECTOR_STRETCHES = [0, 1, 4]
+
+SCALAR_GROUPS = [64, 52]
+
+VECTOR_SHARE = 64
+OWN_PIECES = [(0, 256), (256, 128), (384, 128)]
+
 NEAR = 0.8 * 0.8
 CEN_OVER_NEAR = 0.2 / 0.8
 ROOT_OVER_NEAR = 0.2 / NEAR
@@ -64,7 +69,7 @@ def tile_picked_zappnp_gelu_p_kernel(tc, x_words, x_scales, w1, w2_words, w2_sca
             return tile
 
         x_scale_table = keep.tile([P, T], U8, name="x_scale_table", align_bytes=64)
-        nc.gpsimd.memset(x_scale_table[:].bitcast(I32), 0)
+        nc.vector.memset(x_scale_table[:].bitcast(I32), 0)
         w2_scale = keep.tile([P, N], U8, name="w2_scale", align_bytes=64)
         nc.vector.memset(w2_scale[:].bitcast(I32), 0)
 
@@ -99,14 +104,14 @@ def tile_picked_zappnp_gelu_p_kernel(tc, x_words, x_scales, w1, w2_words, w2_sca
         def gather_words(g, dst, first, count):
             nc.vector.tensor_copy(dst, x_table[g][:].bitcast(U32).indirect(entries(offs_tile, first, count)))
 
-        early_nodes = EARLY_BLOCKS * BLOCK
+        early_nodes = EARLY_BATCHES * BATCH
         w1_word = {}
         w1_scale = {}
 
         def quantise_w1(g):
             rounded = keep.tile([P, PACK, P, PACK], BF16, name=f"w1_rounded{g}", tag=f"w1_rounded{g}", align_bytes=64)
-            src = w1_raw[g][:].rearrange("p j (m t) -> p m t j", t=PACK)
-            dst = rounded[:].rearrange("p t m j -> p m t j")
+            src = w1_raw[g][:].rearrange("p j (m t) -> p m j t", t=PACK)
+            dst = rounded[:].rearrange("p t m j -> p m j t")
             split = SCALAR_GROUPS[g]
             nc.scalar.copy(dst[:, 0:split, :, :], src[:, 0:split, :, :])
             nc.vector.tensor_copy(dst[:, split:P, :, :], src[:, split:P, :, :])
@@ -125,51 +130,52 @@ def tile_picked_zappnp_gelu_p_kernel(tc, x_words, x_scales, w1, w2_words, w2_sca
                     lhsT=w1_word[(g, t)].bitcast(FP8X4),
                     lhsT_scale=w1_scale[(g, t)],
                     rhs=words.bitcast(FP8X4),
-                    rhs_scale=x_scale[4 * g : P, n0 : n0 + BLOCK],
+                    rhs_scale=x_scale[4 * g : P, n0 : n0 + BATCH],
                     start=(opens and t == 0),
                     stop=(not opens and t == PACK - 1),
                 )
 
-        h_banks = [bank_tile(b, [P, PACK, BLOCK]) for b in range(S // BLOCK)]
-        x0_blocks = []
+        h_banks = [bank_tile(b, [P, PACK, BATCH]) for b in range(S // BATCH)]
+        x0_batches = []
 
         quantise_w1(0)
         x0_word = keep.tile([P, early_nodes], U32, name="x0_word", tag="w1_rounded0", align_bytes=64)
         for first in range(0, early_nodes, SLICE):
             count = min(SLICE, early_nodes - first)
             gather_words(0, x0_word[:, first : first + count], first, count)
-        x0_blocks.extend([x0_word[:, n0 : n0 + BLOCK] for n0 in range(0, early_nodes, BLOCK)])
-        for b in range(OPEN_AHEAD):
-            first_layer_pass(0, h_banks[b], x0_blocks[b], b * BLOCK, True)
+        x0_batches.extend([x0_word[:, n0 : n0 + BATCH] for n0 in range(0, early_nodes, BATCH)])
+        for b in range(EARLY_BATCHES):
+            first_layer_pass(0, h_banks[b], x0_batches[b], b * BATCH, True)
         quantise_w1(1)
 
         y_near = keep.tile([P, S], F32, name="y_near")
-        x1_blocks = []
+        x1_batches = []
         first = 0
         for count in LAST_SLICES:
             tile = keep.tile([P, count], U32, name=f"x1_word{first}", align_bytes=64)
             gather_words(1, tile[:], first, count)
-            x1_blocks.extend([tile[:, n0 : n0 + BLOCK] for n0 in range(0, count, BLOCK)])
+            x1_batches.extend([tile[:, n0 : n0 + BATCH] for n0 in range(0, count, BATCH)])
             first = first + count
         x0_late = keep.tile([P, S - early_nodes], U32, name="x0_late", tag="x_table1", align_bytes=64)
         gather_words(0, x0_late[:], early_nodes, S - early_nodes)
-        x0_blocks.extend([x0_late[:, n0 : n0 + BLOCK] for n0 in range(0, S - early_nodes, BLOCK)])
+        x0_batches.extend([x0_late[:, n0 : n0 + BATCH] for n0 in range(0, S - early_nodes, BATCH)])
 
         def first_layer(first, width):
             h_rounded = keep.tile([P, width, PACK], BF16, name=f"h_rounded{first}", align_bytes=64)
-            for b0 in range(0, width, BLOCK):
-                b = (first + b0) // BLOCK
-                first_layer_pass(1, h_banks[b], x1_blocks[b], b * BLOCK, b >= OPEN_AHEAD)
-                if b >= OPEN_AHEAD:
-                    first_layer_pass(0, h_banks[b], x0_blocks[b], b * BLOCK, False)
-                nc.scalar.activation(h_rounded[:, b0 : b0 + BLOCK, :], h_banks[b][:].rearrange("p t n -> p n t"), GELU)
+            for b0 in range(0, width, BATCH):
+                b = (first + b0) // BATCH
+                late = b >= EARLY_BATCHES
+                first_layer_pass(1, h_banks[b], x1_batches[b], b * BATCH, late)
+                if late:
+                    first_layer_pass(0, h_banks[b], x0_batches[b], b * BATCH, False)
+                nc.scalar.activation(h_rounded[:, b0 : b0 + BATCH, :], h_banks[b][:].rearrange("p t n -> p n t"), GELU)
             return h_rounded
 
         def second_layer(index, first, width, h_rounded):
             h_word = keep.tile([P, width], U32, name=f"h_word{first}", align_bytes=64)
             h_scale = keep.tile([P, width], U8, name=f"h_scale{first}", align_bytes=64)
             nc.vector.quantize_mx(out=h_word[:].bitcast(FP8X4), scales=h_scale[:], in_=h_rounded[:].rearrange("p n t -> p (n t)"))
-            bank = bank_tile(Y_BANKS[index], [P, width])
+            bank = bank_tile(index, [P, width])
             nc.tensor.matmul_mx(
                 out=bank[:],
                 lhsT=w2_word[:].bitcast(FP4X4),
@@ -192,55 +198,51 @@ def tile_picked_zappnp_gelu_p_kernel(tc, x_words, x_scales, w1, w2_words, w2_sca
         for index in range(1, len(STRETCHES)):
             second_layer(index, firsts[index], STRETCHES[index], hidden[index])
 
-        def fresh(name, width, tag=None):
-            return keep.tile([P, width], F32, name=name, tag=tag or name)
+        def fresh(name, width):
+            return keep.tile([P, width], F32, name=name)
 
-        def pick(name, table, list_tile, first, count, factor=1.0, tag=None):
-            tile = fresh(name, count, tag)
+        def pick(name, table, list_tile, first, count, factor=1.0):
+            tile = fresh(name, count)
             nc.scalar.activation(tile[:], table[:].indirect(entries(list_tile, first, count)), COPY, scale=factor)
             return tile[:]
 
-        def pick_gated(name, table, list_tile, first, count, gates):
-            tile = fresh(name, count)
-            nc.vector.tensor_tensor(tile[:], table[:].indirect(entries(list_tile, first, count)), gates[:, first : first + count], MULT)
-            return tile[:]
+        def pick_gated(dst, table, list_tile, first, gates):
+            count = dst.shape[1]
+            nc.vector.tensor_tensor(dst, table[:].indirect(entries(list_tile, first, count)), gates[:, first : first + count], MULT)
+            return dst
 
-        def combine(name, a, b, op, dst=None):
-            if dst is None:
-                dst = fresh(name, a.shape[1])[:]
+        def combine(dst, a, b, op):
             nc.vector.tensor_tensor(dst, a, b, op)
             return dst
 
-        half = V // 2
-        starts = (0, half)
-        share = 64
-        second = [pick("picked1_0", y_near, pos_tiles[1], share, half - share), pick("picked1_1", y_near, pos_tiles[1], half, half)]
-        third = [pick(f"picked2_{c0}", y_near, pos_tiles[2], c0, half) for c0 in starts]
-        own_pieces = [(0, 256), (256, 128), (384, 128)]
-        own = [pick(f"cen{c0}", y_near, cen_tile, c0, width, CEN_OVER_NEAR) for c0, width in own_pieces]
+        z_half = V // 2
+        z_starts = (0, z_half)
+        second = [pick("picked1_0", y_near, pos_tiles[1], VECTOR_SHARE, z_half - VECTOR_SHARE), pick("picked1_1", y_near, pos_tiles[1], z_half, z_half)]
+        third = [pick(f"picked2_{c0}", y_near, pos_tiles[2], c0, z_half) for c0 in z_starts]
+        own = [pick(f"cen{c0}", y_near, cen_tile, c0, width, CEN_OVER_NEAR) for c0, width in OWN_PIECES]
         root_term = pick("root_term", y_near, root_tile, 0, U, ROOT_OVER_NEAR)
-        first_terms = [pick_gated(f"near0_{c0}", y_near, pos_tiles[0], c0, half, gate_tile[:, 0, :]) for c0 in starts]
-        second_terms = [fresh(f"near1_{c0}", half)[:] for c0 in starts]
-        nc.vector.tensor_tensor(second_terms[0][:, 0:share], y_near[:].indirect(entries(pos_tiles[1], 0, share)), gate_tile[:, 1, 0:share], MULT)
-        combine(None, second[0], gate_tile[:, 1, share:half], MULT, second_terms[0][:, share:half])
-        combine(None, second[1], gate_tile[:, 1, half:V], MULT, second_terms[1])
-        total = [combine(f"sum1_{c0}", a, b, ADD) for c0, a, b in zip(starts, first_terms, second_terms)]
-        terms = [combine(f"near2_{c0}", src, gate_tile[:, 2, c0 : c0 + half], MULT) for c0, src in zip(starts, third)]
+        first_terms = [pick_gated(fresh(f"near0_{c0}", z_half)[:], y_near, pos_tiles[0], c0, gate_tile[:, 0, :]) for c0 in z_starts]
+        second_terms = [fresh(f"near1_{c0}", z_half)[:] for c0 in z_starts]
+        pick_gated(second_terms[0][:, 0:VECTOR_SHARE], y_near, pos_tiles[1], 0, gate_tile[:, 1, :])
+        combine(second_terms[0][:, VECTOR_SHARE:z_half], second[0], gate_tile[:, 1, VECTOR_SHARE:z_half], MULT)
+        combine(second_terms[1], second[1], gate_tile[:, 1, z_half:V], MULT)
+        first_two = [combine(fresh(f"sum1_{c0}", z_half)[:], a, b, ADD) for c0, a, b in zip(z_starts, first_terms, second_terms)]
+        third_terms = [combine(fresh(f"near2_{c0}", z_half)[:], src, gate_tile[:, 2, c0 : c0 + z_half], MULT) for c0, src in zip(z_starts, third)]
         neighbours = fresh("neighbours", V)
-        for c0, a, b in zip(starts, total, terms):
-            combine(None, a, b, ADD, neighbours[:, c0 : c0 + half])
+        for c0, a, b in zip(z_starts, first_two, third_terms):
+            combine(neighbours[:, c0 : c0 + z_half], a, b, ADD)
         z_near = fresh("z_near", V)
-        for (c0, width), b in zip(own_pieces, own):
-            combine(None, neighbours[:, c0 : c0 + width], b, ADD, z_near[:, c0 : c0 + width])
+        for (c0, width), term in zip(OWN_PIECES, own):
+            combine(z_near[:, c0 : c0 + width], neighbours[:, c0 : c0 + width], term, ADD)
 
-        half = U // 2
-        starts = (0, half)
-        onward = [[pick(f"onward{d}_{c0}", z_near, nxt_tiles[d], c0, half) for c0 in starts] for d in (1, 2)]
-        total = [pick_gated(f"onward0_{c0}", z_near, nxt_tiles[0], c0, half, gate2_tile[:, 0, :]) for c0 in starts]
-        total = [combine(f"with_root{c0}", a, root_term[:, c0 : c0 + half], ADD) for c0, a in zip(starts, total)]
+        out_half = U // 2
+        out_starts = (0, out_half)
+        onward = [[pick(f"onward{d}_{c0}", z_near, nxt_tiles[d], c0, out_half) for c0 in out_starts] for d in (1, 2)]
+        total = [pick_gated(fresh(f"onward0_{c0}", out_half)[:], z_near, nxt_tiles[0], c0, gate2_tile[:, 0, :]) for c0 in out_starts]
+        total = [combine(fresh(f"with_root{c0}", out_half)[:], a, root_term[:, c0 : c0 + out_half], ADD) for c0, a in zip(out_starts, total)]
         result = fresh("result", U)
         for d in (1, 2):
-            terms = [combine(f"far{d}_{c0}", src, gate2_tile[:, d, c0 : c0 + half], MULT) for c0, src in zip(starts, onward[d - 1])]
-            total = [combine(f"far_sum{d}_{c0}", a, b, ADD, result[:, c0 : c0 + half] if d == 2 else None) for c0, a, b in zip(starts, total, terms)]
-        for c0 in starts:
-            nc.sync.dma_start(out[:, c0 : c0 + half], result[:, c0 : c0 + half])
+            terms = [combine(fresh(f"far{d}_{c0}", out_half)[:], src, gate2_tile[:, d, c0 : c0 + out_half], MULT) for c0, src in zip(out_starts, onward[d - 1])]
+            total = [combine(result[:, c0 : c0 + out_half] if d == 2 else fresh(f"far_sum{c0}", out_half)[:], a, b, ADD) for c0, a, b in zip(out_starts, total, terms)]
+        for c0 in out_starts:
+            nc.sync.dma_start(out[:, c0 : c0 + out_half], result[:, c0 : c0 + out_half])

@@ -31,9 +31,9 @@ EARLY_BATCHES = 6
 LAST_SLICES = [128, 128, 256, 256, 256]
 
 STRETCHES = [256, 256, 256, 128, 128]
-VECTOR_STRETCHES = [0, 1, 4]
+VECTOR_STRETCHES = [0, 4]
 
-SCALAR_GROUPS = [64, 52]
+SCALAR_GROUPS = [56, 52]
 
 VECTOR_SHARE = 64
 OWN_PIECES = [(0, 256), (256, 128), (384, 128)]
@@ -64,7 +64,7 @@ def tile_picked_zappnp_gelu_p_kernel(tc, x_words, x_scales, w1, w2_words, w2_sca
             return w1[K_PASS * g : K_PASS * (g + 1), :].rearrange("(p j) c -> p j c", j=PACK)
 
         def load_x_words(g):
-            tile = keep.tile([P, T], I32, name=f"x_table{g}", tag=f"x_table{g}", align_bytes=64)
+            tile = keep.tile([P, T], I32, name=f"x_table{g}", align_bytes=64)
             nc.sync.dma_start(tile[:], x_words[g].rearrange("p n t -> p (n t)").bitcast(I32))
             return tile
 
@@ -79,7 +79,7 @@ def tile_picked_zappnp_gelu_p_kernel(tc, x_words, x_scales, w1, w2_words, w2_sca
         for q in (0, 1):
             for g in range(PASSES):
                 nc.sync.dma_start(x_scale_table[32 * q + 4 * g : 32 * q + 4 * g + 4, :].bitcast(I32), x_scales[g, 4 * q : 4 * q + 4, :].bitcast(I32))
-        w1_raw = [keep.tile([P, PACK, H], F32, name=f"w1_raw{g}") for g in range(PASSES)]
+        w1_raw = [keep.tile([P, PACK, H], F32, name=f"w1_raw{g}", tag=f"w1_raw{g}", align_bytes=64) for g in range(PASSES)]
         nc.sync.dma_start(w1_raw[0][:, 0:1, :], w1_rows(0)[:, 0:1, :])
         nc.sync.dma_start(w1_raw[0][:, 1:PACK, :], w1_rows(0)[:, 1:PACK, :])
         x_table = [load_x_words(0)]
@@ -98,18 +98,24 @@ def tile_picked_zappnp_gelu_p_kernel(tc, x_words, x_scales, w1, w2_words, w2_sca
         gate2_tile = keep.tile([P, gate2.shape[0], U], F32, name="gate2_tile")
         nc.sync.dma_start(gate2_tile[:], gate2.rearrange("d p v -> p d v"))
 
-        x_scale = keep.tile([P, S], U8, name="x_scale", align_bytes=64)
-        nc.vector.tensor_copy(x_scale[:], x_scale_table[:].indirect(offs_tile[:]))
+        early_nodes = EARLY_BATCHES * BATCH
+
+        def gather_scales(tile, first):
+            count = tile.shape[1]
+            nc.vector.tensor_copy(tile[:], x_scale_table[:].indirect(entries(offs_tile, first, count)))
+            return [tile[:, n0 : n0 + BATCH] for n0 in range(0, count, BATCH)]
+
+        scale_early = keep.tile([P, early_nodes], U8, name="scale_early", align_bytes=64)
+        scale_batches = gather_scales(scale_early, 0)
 
         def gather_words(g, dst, first, count):
             nc.vector.tensor_copy(dst, x_table[g][:].bitcast(U32).indirect(entries(offs_tile, first, count)))
 
-        early_nodes = EARLY_BATCHES * BATCH
         w1_word = {}
         w1_scale = {}
 
         def quantise_w1(g):
-            rounded = keep.tile([P, PACK, P, PACK], BF16, name=f"w1_rounded{g}", tag=f"w1_rounded{g}", align_bytes=64)
+            rounded = keep.tile([P, PACK, P, PACK], BF16, name=f"w1_rounded{g}", align_bytes=64)
             src = w1_raw[g][:].rearrange("p j (m t) -> p m j t", t=PACK)
             dst = rounded[:].rearrange("p t m j -> p m j t")
             split = SCALAR_GROUPS[g]
@@ -123,14 +129,14 @@ def tile_picked_zappnp_gelu_p_kernel(tc, x_words, x_scales, w1, w2_words, w2_sca
                     w1_word[(g, t0 + u)] = words[:, u * P : (u + 1) * P]
                     w1_scale[(g, t0 + u)] = scales[:, u * P : (u + 1) * P]
 
-        def first_layer_pass(g, bank, words, n0, opens):
+        def first_layer_pass(g, bank, words, scales, opens):
             for t in range(PACK):
                 nc.tensor.matmul_mx(
                     out=bank[:, t, :],
                     lhsT=w1_word[(g, t)].bitcast(FP8X4),
                     lhsT_scale=w1_scale[(g, t)],
                     rhs=words.bitcast(FP8X4),
-                    rhs_scale=x_scale[4 * g : P, n0 : n0 + BATCH],
+                    rhs_scale=scales[4 * g : P, :],
                     start=(opens and t == 0),
                     stop=(not opens and t == PACK - 1),
                 )
@@ -139,35 +145,31 @@ def tile_picked_zappnp_gelu_p_kernel(tc, x_words, x_scales, w1, w2_words, w2_sca
         x0_batches = []
 
         quantise_w1(0)
-        x0_word = keep.tile([P, early_nodes], U32, name="x0_word", tag="w1_rounded0", align_bytes=64)
+        x0_word = keep.tile([P, early_nodes], U32, name="x0_word", tag="w1_raw0", align_bytes=64)
         for first in range(0, early_nodes, SLICE):
             count = min(SLICE, early_nodes - first)
             gather_words(0, x0_word[:, first : first + count], first, count)
         x0_batches.extend([x0_word[:, n0 : n0 + BATCH] for n0 in range(0, early_nodes, BATCH)])
         for b in range(EARLY_BATCHES):
-            first_layer_pass(0, h_banks[b], x0_batches[b], b * BATCH, True)
+            first_layer_pass(0, h_banks[b], x0_batches[b], scale_batches[b], True)
         quantise_w1(1)
 
         y_near = keep.tile([P, S], F32, name="y_near")
         x1_batches = []
-        first = 0
-        for count in LAST_SLICES:
-            tile = keep.tile([P, count], U32, name=f"x1_word{first}", align_bytes=64)
+        slice_firsts = [sum(LAST_SLICES[:i]) for i in range(len(LAST_SLICES))]
+        for first, count in zip(slice_firsts, LAST_SLICES):
+            tile = keep.tile([P, count], U32, name=f"x1_word{first}", tag=f"x1_word{first}", align_bytes=64)
             gather_words(1, tile[:], first, count)
             x1_batches.extend([tile[:, n0 : n0 + BATCH] for n0 in range(0, count, BATCH)])
-            first = first + count
-        x0_late = keep.tile([P, S - early_nodes], U32, name="x0_late", tag="x_table1", align_bytes=64)
-        gather_words(0, x0_late[:], early_nodes, S - early_nodes)
-        x0_batches.extend([x0_late[:, n0 : n0 + BATCH] for n0 in range(0, S - early_nodes, BATCH)])
 
         def first_layer(first, width):
             h_rounded = keep.tile([P, width, PACK], BF16, name=f"h_rounded{first}", align_bytes=64)
             for b0 in range(0, width, BATCH):
                 b = (first + b0) // BATCH
                 late = b >= EARLY_BATCHES
-                first_layer_pass(1, h_banks[b], x1_batches[b], b * BATCH, late)
+                first_layer_pass(1, h_banks[b], x1_batches[b], scale_batches[b], late)
                 if late:
-                    first_layer_pass(0, h_banks[b], x0_batches[b], b * BATCH, False)
+                    first_layer_pass(0, h_banks[b], x0_batches[b], scale_batches[b], False)
                 nc.scalar.activation(h_rounded[:, b0 : b0 + BATCH, :], h_banks[b][:].rearrange("p t n -> p n t"), GELU)
             return h_rounded
 
@@ -193,9 +195,14 @@ def tile_picked_zappnp_gelu_p_kernel(tc, x_words, x_scales, w1, w2_words, w2_sca
         firsts = [sum(STRETCHES[:i]) for i in range(len(STRETCHES))]
         early_stretches = len([f for f, w in zip(firsts, STRETCHES) if f + w <= early_nodes])
         hidden = [first_layer(first, width) for first, width in zip(firsts[:early_stretches], STRETCHES[:early_stretches])]
-        second_layer(0, firsts[0], STRETCHES[0], hidden[0])
+        scale_late = keep.tile([P, S - early_nodes], U8, name="scale_late", tag="x1_word0", align_bytes=64)
+        scale_batches.extend(gather_scales(scale_late, early_nodes))
+        for first, freed in zip(range(early_nodes, S, BATCH), slice_firsts[1:]):
+            tile = keep.tile([P, BATCH], U32, name=f"x0_word{first}", tag=f"x1_word{freed}", align_bytes=64)
+            gather_words(0, tile[:], first, BATCH)
+            x0_batches.append(tile[:])
         hidden.extend([first_layer(first, width) for first, width in zip(firsts[early_stretches:], STRETCHES[early_stretches:])])
-        for index in range(1, len(STRETCHES)):
+        for index in range(len(STRETCHES)):
             second_layer(index, firsts[index], STRETCHES[index], hidden[index])
 
         def fresh(name, width):

@@ -35,7 +35,6 @@ VECTOR_STRETCHES = [0, 4]
 
 SCALAR_GROUPS = [56, 52]
 
-VECTOR_SHARE = 64
 OWN_PIECES = [(0, 256), (256, 128), (384, 128)]
 
 NEAR = 0.8 * 0.8
@@ -224,19 +223,19 @@ def tile_picked_zappnp_gelu_p_kernel(tc, x_words, x_scales, w1, w2_words, w2_sca
 
         z_half = V // 2
         z_starts = (0, z_half)
-        second = [pick("picked1_0", y_near, pos_tiles[1], VECTOR_SHARE, z_half - VECTOR_SHARE), pick("picked1_1", y_near, pos_tiles[1], z_half, z_half)]
+        second = [pick(f"picked1_{c0}", y_near, pos_tiles[1], c0, z_half) for c0 in z_starts]
         third = [pick(f"picked2_{c0}", y_near, pos_tiles[2], c0, z_half) for c0 in z_starts]
         own = [pick(f"cen{c0}", y_near, cen_tile, c0, width, CEN_OVER_NEAR) for c0, width in OWN_PIECES]
         root_term = pick("root_term", y_near, root_tile, 0, U, ROOT_OVER_NEAR)
-        first_terms = [pick_gated(fresh(f"near0_{c0}", z_half)[:], y_near, pos_tiles[0], c0, gate_tile[:, 0, :]) for c0 in z_starts]
-        second_terms = [fresh(f"near1_{c0}", z_half)[:] for c0 in z_starts]
-        pick_gated(second_terms[0][:, 0:VECTOR_SHARE], y_near, pos_tiles[1], 0, gate_tile[:, 1, :])
-        combine(second_terms[0][:, VECTOR_SHARE:z_half], second[0], gate_tile[:, 1, VECTOR_SHARE:z_half], MULT)
-        combine(second_terms[1], second[1], gate_tile[:, 1, z_half:V], MULT)
-        first_two = [combine(fresh(f"sum1_{c0}", z_half)[:], a, b, ADD) for c0, a, b in zip(z_starts, first_terms, second_terms)]
-        third_terms = [combine(fresh(f"near2_{c0}", z_half)[:], src, gate_tile[:, 2, c0 : c0 + z_half], MULT) for c0, src in zip(z_starts, third)]
+        near0 = pick_gated(fresh("near0", V)[:], y_near, pos_tiles[0], 0, gate_tile[:, 0, :])
+        near1 = [combine(fresh(f"near1_{c0}", z_half)[:], src, gate_tile[:, 1, c0 : c0 + z_half], MULT) for c0, src in zip(z_starts, second)]
+        first_two = []
+        near2 = []
+        for c0, a, src in zip(z_starts, near1, third):
+            first_two.append(combine(fresh(f"sum1_{c0}", z_half)[:], near0[:, c0 : c0 + z_half], a, ADD))
+            near2.append(combine(fresh(f"near2_{c0}", z_half)[:], src, gate_tile[:, 2, c0 : c0 + z_half], MULT))
         neighbours = fresh("neighbours", V)
-        for c0, a, b in zip(z_starts, first_two, third_terms):
+        for c0, a, b in zip(z_starts, first_two, near2):
             combine(neighbours[:, c0 : c0 + z_half], a, b, ADD)
         z_near = fresh("z_near", V)
         for (c0, width), term in zip(OWN_PIECES, own):

@@ -31,11 +31,11 @@ EARLY_BATCHES = 6
 LAST_SLICES = [128, 128, 256, 256, 256]
 
 STRETCHES = [256, 256, 256, 128, 128]
-VECTOR_STRETCHES = [0, 4]
+VECTOR_STRETCHES = [4]
 
 SCALAR_GROUPS = [56, 52]
 
-OWN_PIECES = [(0, 256), (256, 128), (384, 128)]
+OWN_PIECES = [(0, 256), (256, 192), (448, 64)]
 
 NEAR = 0.8 * 0.8
 CEN_OVER_NEAR = 0.2 / 0.8

@@ -28,10 +28,9 @@ BATCH = 128
 SLICE = 256
 
 EARLY_BATCHES = 6
-LAST_SLICES = [128, 128, 256, 256, 256]
+LAST_SLICES = [128, 128, 128, 128, 256, 256]
 
 STRETCHES = [256, 256, 256, 128, 128]
-VECTOR_STRETCHES = [4]
 
 SCALAR_GROUPS = [56, 52]
 
@@ -128,30 +127,37 @@ def tile_picked_zappnp_gelu_p_kernel(tc, x_words, x_scales, w1, w2_words, w2_sca
                     w1_word[(g, t0 + u)] = words[:, u * P : (u + 1) * P]
                     w1_scale[(g, t0 + u)] = scales[:, u * P : (u + 1) * P]
 
-        def first_layer_pass(g, bank, words, scales, opens):
-            for t in range(PACK):
+        def first_layer_pass(g, bank, words, scales, opens, t0=0):
+            tiles = bank.shape[1]
+            for t in range(t0, t0 + tiles):
                 nc.tensor.matmul_mx(
-                    out=bank[:, t, :],
+                    out=bank[:, t - t0, :],
                     lhsT=w1_word[(g, t)].bitcast(FP8X4),
                     lhsT_scale=w1_scale[(g, t)],
                     rhs=words.bitcast(FP8X4),
                     rhs_scale=scales[4 * g : P, :],
-                    start=(opens and t == 0),
-                    stop=(not opens and t == PACK - 1),
+                    start=(opens and t == t0),
+                    stop=(not opens and t == t0 + tiles - 1),
                 )
 
-        h_banks = [bank_tile(b, [P, PACK, BATCH]) for b in range(S // BATCH)]
+        last_batch = S // BATCH - 1
+        half_banks = [bank_tile(b, [P, 2, BATCH]) for b in (0, last_batch)]
+        h_banks = {b: bank_tile(b, [P, PACK, BATCH]) for b in range(1, last_batch)}
         x0_batches = []
 
         quantise_w1(0)
         x0_word = keep.tile([P, early_nodes], U32, name="x0_word", tag="w1_raw0", align_bytes=64)
         for first in range(0, early_nodes, SLICE):
-            count = min(SLICE, early_nodes - first)
-            gather_words(0, x0_word[:, first : first + count], first, count)
+            gather_words(0, x0_word[:, first : first + SLICE], first, SLICE)
         x0_batches.extend([x0_word[:, n0 : n0 + BATCH] for n0 in range(0, early_nodes, BATCH)])
-        for b in range(EARLY_BATCHES):
+        for u in range(2):
+            first_layer_pass(0, half_banks[u], x0_batches[0], scale_batches[0], True, 2 * u)
+        for b in range(1, EARLY_BATCHES):
             first_layer_pass(0, h_banks[b], x0_batches[b], scale_batches[b], True)
         quantise_w1(1)
+        x0_waiting = keep.tile([P, BATCH], U32, name="x0_waiting", tag="w1_raw1", align_bytes=64)
+        gather_words(0, x0_waiting[:], early_nodes, BATCH)
+        x0_batches.append(x0_waiting[:])
 
         y_near = keep.tile([P, S], F32, name="y_near")
         x1_batches = []
@@ -161,15 +167,32 @@ def tile_picked_zappnp_gelu_p_kernel(tc, x_words, x_scales, w1, w2_words, w2_sca
             gather_words(1, tile[:], first, count)
             x1_batches.extend([tile[:, n0 : n0 + BATCH] for n0 in range(0, count, BATCH)])
 
+        def first_batch(h_rounded):
+            halves = keep.tile([P, 2, BATCH, 2], BF16, name="h_halves", align_bytes=64)
+            for u in range(2):
+                first_layer_pass(1, half_banks[u], x1_batches[0], scale_batches[0], False, 2 * u)
+                nc.scalar.activation(halves[:, u, :, :], half_banks[u][:].rearrange("p t n -> p n t"), GELU)
+            pairs_in = halves[:].rearrange("p u n e -> p (u n e)").bitcast(I32).rearrange("p (u n) -> p n u", u=2)
+            pairs_out = h_rounded.rearrange("p n t -> p (n t)").bitcast(I32).rearrange("p (n u) -> p n u", u=2)
+            nc.vector.tensor_copy(pairs_out, pairs_in)
+
+        def whole_batch(b, h_rounded):
+            if b == last_batch:
+                h_banks[b] = bank_tile(b, [P, PACK, BATCH])
+            late = b >= EARLY_BATCHES
+            first_layer_pass(1, h_banks[b], x1_batches[b], scale_batches[b], late)
+            if late:
+                first_layer_pass(0, h_banks[b], x0_batches[b], scale_batches[b], False)
+            nc.scalar.activation(h_rounded, h_banks[b][:].rearrange("p t n -> p n t"), GELU)
+
         def first_layer(first, width):
             h_rounded = keep.tile([P, width, PACK], BF16, name=f"h_rounded{first}", align_bytes=64)
             for b0 in range(0, width, BATCH):
                 b = (first + b0) // BATCH
-                late = b >= EARLY_BATCHES
-                first_layer_pass(1, h_banks[b], x1_batches[b], scale_batches[b], late)
-                if late:
-                    first_layer_pass(0, h_banks[b], x0_batches[b], scale_batches[b], False)
-                nc.scalar.activation(h_rounded[:, b0 : b0 + BATCH, :], h_banks[b][:].rearrange("p t n -> p n t"), GELU)
+                if b == 0:
+                    first_batch(h_rounded[:, b0 : b0 + BATCH, :])
+                else:
+                    whole_batch(b, h_rounded[:, b0 : b0 + BATCH, :])
             return h_rounded
 
         def second_layer(index, first, width, h_rounded):
@@ -186,7 +209,7 @@ def tile_picked_zappnp_gelu_p_kernel(tc, x_words, x_scales, w1, w2_words, w2_sca
                 start=True,
                 stop=True,
             )
-            if index in VECTOR_STRETCHES:
+            if index == len(STRETCHES) - 1:
                 nc.vector.tensor_scalar(y_near[:, first : first + width], bank[:], NEAR, None, MULT)
             else:
                 nc.scalar.activation(y_near[:, first : first + width], bank[:], COPY, scale=NEAR)
@@ -194,12 +217,11 @@ def tile_picked_zappnp_gelu_p_kernel(tc, x_words, x_scales, w1, w2_words, w2_sca
         firsts = [sum(STRETCHES[:i]) for i in range(len(STRETCHES))]
         early_stretches = len([f for f, w in zip(firsts, STRETCHES) if f + w <= early_nodes])
         hidden = [first_layer(first, width) for first, width in zip(firsts[:early_stretches], STRETCHES[:early_stretches])]
-        scale_late = keep.tile([P, S - early_nodes], U8, name="scale_late", tag="x1_word0", align_bytes=64)
+        scale_late = keep.tile([P, S - early_nodes], U8, name="scale_late", tag=f"x1_word{slice_firsts[0]}", align_bytes=64)
         scale_batches.extend(gather_scales(scale_late, early_nodes))
-        for first, freed in zip(range(early_nodes, S, BATCH), slice_firsts[1:]):
-            tile = keep.tile([P, BATCH], U32, name=f"x0_word{first}", tag=f"x1_word{freed}", align_bytes=64)
-            gather_words(0, tile[:], first, BATCH)
-            x0_batches.append(tile[:])
+        x0_last = keep.tile([P, BATCH], U32, name="x0_last", tag=f"x1_word{slice_firsts[1]}", align_bytes=64)
+        gather_words(0, x0_last[:], last_batch * BATCH, BATCH)
+        x0_batches.append(x0_last[:])
         hidden.extend([first_layer(first, width) for first, width in zip(firsts[early_stretches:], STRETCHES[early_stretches:])])
         for index in range(len(STRETCHES)):
             second_layer(index, firsts[index], STRETCHES[index], hidden[index])

@@ -32,7 +32,9 @@ LAST_SLICES = [128, 128, 128, 128, 256, 256]
 
 STRETCHES = [256, 256, 256, 128, 128]
 
-SCALAR_GROUPS = [56, 52]
+SCALAR_GROUPS = [100, 60]
+PRELOAD = 768
+SCALE_LOADS_AHEAD = 6
 
 OWN_PIECES = [(0, 256), (256, 192), (448, 64)]
 
@@ -72,14 +74,19 @@ def tile_picked_zappnp_gelu_p_kernel(tc, x_words, x_scales, w1, w2_words, w2_sca
         nc.vector.memset(w2_scale[:].bitcast(I32), 0)
 
         offs_tile = load_list("offs_tile", offs)
-        for q in (2, 3):
-            nc.sync.dma_start(x_scale_table[32 * q : 32 * q + 4 * PASSES, :].bitcast(I32), x_scales[:, 4 * q : 4 * q + 4, :].bitcast(I32))
-        for q in (0, 1):
-            for g in range(PASSES):
+
+        def load_scale_rows(loads):
+            for q, g in loads:
                 nc.sync.dma_start(x_scale_table[32 * q + 4 * g : 32 * q + 4 * g + 4, :].bitcast(I32), x_scales[g, 4 * q : 4 * q + 4, :].bitcast(I32))
+
+        scale_loads = [(q + 2 * upper, g) for q in range(2) for g in range(PASSES) for upper in (1, 0)]
+        load_scale_rows(scale_loads[:SCALE_LOADS_AHEAD])
         w1_raw = [keep.tile([P, PACK, H], F32, name=f"w1_raw{g}", tag=f"w1_raw{g}", align_bytes=64) for g in range(PASSES)]
-        nc.sync.dma_start(w1_raw[0][:, 0:1, :], w1_rows(0)[:, 0:1, :])
-        nc.sync.dma_start(w1_raw[0][:, 1:PACK, :], w1_rows(0)[:, 1:PACK, :])
+        flat_raw = w1_raw[0][:].rearrange("p j c -> p (j c)")
+        flat_rows = w1_rows(0).rearrange("p j c -> p (j c)")
+        nc.sync.dma_start(flat_raw[:, 0:PRELOAD], flat_rows[:, 0:PRELOAD])
+        nc.sync.dma_start(flat_raw[:, PRELOAD : PACK * H], flat_rows[:, PRELOAD : PACK * H])
+        load_scale_rows(scale_loads[SCALE_LOADS_AHEAD:])
         x_table = [load_x_words(0)]
         nc.sync.dma_start(w1_raw[1][:], w1_rows(1))
         x_table.append(load_x_words(1))
@@ -112,20 +119,22 @@ def tile_picked_zappnp_gelu_p_kernel(tc, x_words, x_scales, w1, w2_words, w2_sca
         w1_word = {}
         w1_scale = {}
 
-        def quantise_w1(g):
+        def round_w1(g):
             rounded = keep.tile([P, PACK, P, PACK], BF16, name=f"w1_rounded{g}", align_bytes=64)
             src = w1_raw[g][:].rearrange("p j (m t) -> p m j t", t=PACK)
             dst = rounded[:].rearrange("p t m j -> p m j t")
             split = SCALAR_GROUPS[g]
             nc.scalar.copy(dst[:, 0:split, :, :], src[:, 0:split, :, :])
             nc.vector.tensor_copy(dst[:, split:P, :, :], src[:, split:P, :, :])
-            for t0 in range(0, PACK, 2):
-                words = keep.tile([P, 2 * P], U32, name=f"w1_word{g}{t0}", align_bytes=64)
-                scales = keep.tile([P, 2 * P], U8, name=f"w1_scale{g}{t0}", align_bytes=64)
-                nc.vector.quantize_mx(out=words[:].bitcast(FP8X4), scales=scales[:], in_=rounded[:, t0 : t0 + 2, :, :].rearrange("p t m j -> p (t m j)"))
-                for u in range(2):
-                    w1_word[(g, t0 + u)] = words[:, u * P : (u + 1) * P]
-                    w1_scale[(g, t0 + u)] = scales[:, u * P : (u + 1) * P]
+            return rounded
+
+        def quantise_w1(g, rounded, t0):
+            words = keep.tile([P, 2 * P], U32, name=f"w1_word{g}{t0}", align_bytes=64)
+            scales = keep.tile([P, 2 * P], U8, name=f"w1_scale{g}{t0}", align_bytes=64)
+            nc.vector.quantize_mx(out=words[:].bitcast(FP8X4), scales=scales[:], in_=rounded[:, t0 : t0 + 2, :, :].rearrange("p t m j -> p (t m j)"))
+            for u in range(2):
+                w1_word[(g, t0 + u)] = words[:, u * P : (u + 1) * P]
+                w1_scale[(g, t0 + u)] = scales[:, u * P : (u + 1) * P]
 
         def first_layer_pass(g, bank, words, scales, opens, t0=0):
             tiles = bank.shape[1]
@@ -145,19 +154,22 @@ def tile_picked_zappnp_gelu_p_kernel(tc, x_words, x_scales, w1, w2_words, w2_sca
         h_banks = {b: bank_tile(b, [P, PACK, BATCH]) for b in range(1, last_batch)}
         x0_batches = []
 
-        quantise_w1(0)
         x0_word = keep.tile([P, early_nodes], U32, name="x0_word", tag="w1_raw0", align_bytes=64)
-        for first in range(0, early_nodes, SLICE):
+        rounded = round_w1(0)
+        quantise_w1(0, rounded, 0)
+        gather_words(0, x0_word[:, 0:BATCH], 0, BATCH)
+        quantise_w1(0, rounded, 2)
+        gather_words(0, x0_word[:, BATCH:SLICE], BATCH, BATCH)
+        for first in range(SLICE, early_nodes, SLICE):
             gather_words(0, x0_word[:, first : first + SLICE], first, SLICE)
         x0_batches.extend([x0_word[:, n0 : n0 + BATCH] for n0 in range(0, early_nodes, BATCH)])
         for u in range(2):
             first_layer_pass(0, half_banks[u], x0_batches[0], scale_batches[0], True, 2 * u)
         for b in range(1, EARLY_BATCHES):
             first_layer_pass(0, h_banks[b], x0_batches[b], scale_batches[b], True)
-        quantise_w1(1)
-        x0_waiting = keep.tile([P, BATCH], U32, name="x0_waiting", tag="w1_raw1", align_bytes=64)
-        gather_words(0, x0_waiting[:], early_nodes, BATCH)
-        x0_batches.append(x0_waiting[:])
+        rounded = round_w1(1)
+        for t0 in range(0, PACK, 2):
+            quantise_w1(1, rounded, t0)
 
         y_near = keep.tile([P, S], F32, name="y_near")
         x1_batches = []
@@ -219,9 +231,10 @@ def tile_picked_zappnp_gelu_p_kernel(tc, x_words, x_scales, w1, w2_words, w2_sca
         hidden = [first_layer(first, width) for first, width in zip(firsts[:early_stretches], STRETCHES[:early_stretches])]
         scale_late = keep.tile([P, S - early_nodes], U8, name="scale_late", tag=f"x1_word{slice_firsts[0]}", align_bytes=64)
         scale_batches.extend(gather_scales(scale_late, early_nodes))
-        x0_last = keep.tile([P, BATCH], U32, name="x0_last", tag=f"x1_word{slice_firsts[1]}", align_bytes=64)
-        gather_words(0, x0_last[:], last_batch * BATCH, BATCH)
-        x0_batches.append(x0_last[:])
+        for first, freed in zip(range(early_nodes, S, BATCH), slice_firsts[1:]):
+            tile = keep.tile([P, BATCH], U32, name=f"x0_word{first}", tag=f"x1_word{freed}", align_bytes=64)
+            gather_words(0, tile[:], first, BATCH)
+            x0_batches.append(tile[:])
         hidden.extend([first_layer(first, width) for first, width in zip(firsts[early_stretches:], STRETCHES[early_stretches:])])
         for index in range(len(STRETCHES)):
             second_layer(index, firsts[index], STRETCHES[index], hidden[index])

@@ -32,9 +32,10 @@ LAST_SLICES = [128, 128, 128, 128, 256, 256]
 
 STRETCHES = [256, 256, 256, 128, 128]
 
-SCALAR_GROUPS = [100, 60]
-PRELOAD = 768
-SCALE_LOADS_AHEAD = 6
+SCALAR_GROUPS = [96, 60]
+PRELOAD = 640
+LAST_PIECE = 1920
+SCALE_LOADS_AHEAD = 3
 
 OWN_PIECES = [(0, 256), (256, 192), (448, 64)]
 
@@ -73,6 +74,11 @@ def tile_picked_zappnp_gelu_p_kernel(tc, x_words, x_scales, w1, w2_words, w2_sca
         w2_scale = keep.tile([P, N], U8, name="w2_scale", align_bytes=64)
         nc.vector.memset(w2_scale[:].bitcast(I32), 0)
 
+        warm_in = keep.tile([P, 1], F32, name="warm_in")
+        nc.gpsimd.memset(warm_in[:], 0.0)
+        warm_out = keep.tile([P, 1], F32, name="warm_out")
+        nc.scalar.activation(warm_out[:], warm_in[:], GELU)
+
         offs_tile = load_list("offs_tile", offs)
 
         def load_scale_rows(loads):
@@ -85,8 +91,9 @@ def tile_picked_zappnp_gelu_p_kernel(tc, x_words, x_scales, w1, w2_words, w2_sca
         flat_raw = w1_raw[0][:].rearrange("p j c -> p (j c)")
         flat_rows = w1_rows(0).rearrange("p j c -> p (j c)")
         nc.sync.dma_start(flat_raw[:, 0:PRELOAD], flat_rows[:, 0:PRELOAD])
-        nc.sync.dma_start(flat_raw[:, PRELOAD : PACK * H], flat_rows[:, PRELOAD : PACK * H])
+        nc.sync.dma_start(flat_raw[:, PRELOAD:LAST_PIECE], flat_rows[:, PRELOAD:LAST_PIECE])
         load_scale_rows(scale_loads[SCALE_LOADS_AHEAD:])
+        nc.sync.dma_start(flat_raw[:, LAST_PIECE : PACK * H], flat_rows[:, LAST_PIECE : PACK * H])
         x_table = [load_x_words(0)]
         nc.sync.dma_start(w1_raw[1][:], w1_rows(1))
         x_table.append(load_x_words(1))
@@ -125,7 +132,8 @@ def tile_picked_zappnp_gelu_p_kernel(tc, x_words, x_scales, w1, w2_words, w2_sca
             dst = rounded[:].rearrange("p t m j -> p m j t")
             split = SCALAR_GROUPS[g]
             nc.scalar.copy(dst[:, 0:split, :, :], src[:, 0:split, :, :])
-            nc.vector.tensor_copy(dst[:, split:P, :, :], src[:, split:P, :, :])
+            rest = nc.scalar.copy if g == 0 else nc.vector.tensor_copy
+            rest(dst[:, split:P, :, :], src[:, split:P, :, :])
             return rounded
 
         def quantise_w1(g, rounded, t0):

@@ -32,7 +32,7 @@ LAST_SLICES = [128, 128, 128, 128, 256, 256]
 
 STRETCHES = [256, 256, 256, 128, 128]
 
-SCALAR_GROUPS = [96, 60]
+SCALAR_GROUPS = [96, 68]
 PRELOAD = 640
 LAST_PIECE = 1920
 SCALE_LOADS_AHEAD = 3
@@ -82,10 +82,10 @@ def tile_picked_zappnp_gelu_p_kernel(tc, x_words, x_scales, w1, w2_words, w2_sca
         offs_tile = load_list("offs_tile", offs)
 
         def load_scale_rows(loads):
-            for q, g in loads:
-                nc.sync.dma_start(x_scale_table[32 * q + 4 * g : 32 * q + 4 * g + 4, :].bitcast(I32), x_scales[g, 4 * q : 4 * q + 4, :].bitcast(I32))
+            for r, g in loads:
+                nc.sync.dma_start(x_scale_table[4 * g + r : P : 32, :].bitcast(I32), x_scales[g, r : 16 : 4, :].bitcast(I32))
 
-        scale_loads = [(q + 2 * upper, g) for q in range(2) for g in range(PASSES) for upper in (1, 0)]
+        scale_loads = [(r, g) for r in range(4) for g in range(PASSES)]
         load_scale_rows(scale_loads[:SCALE_LOADS_AHEAD])
         w1_raw = [keep.tile([P, PACK, H], F32, name=f"w1_raw{g}", tag=f"w1_raw{g}", align_bytes=64) for g in range(PASSES)]
         flat_raw = w1_raw[0][:].rearrange("p j c -> p (j c)")

@@ -32,7 +32,7 @@ LAST_SLICES = [128, 128, 128, 128, 256, 256]
 
 STRETCHES = [256, 256, 256, 128, 128]
 
-SCALAR_GROUPS = [96, 68]
+SCALAR_GROUPS = [96, 62]
 PRELOAD = 640
 LAST_PIECE = 1920
 SCALE_LOADS_AHEAD = 3
@@ -132,8 +132,11 @@ def tile_picked_zappnp_gelu_p_kernel(tc, x_words, x_scales, w1, w2_words, w2_sca
             dst = rounded[:].rearrange("p t m j -> p m j t")
             split = SCALAR_GROUPS[g]
             nc.scalar.copy(dst[:, 0:split, :, :], src[:, 0:split, :, :])
-            rest = nc.scalar.copy if g == 0 else nc.vector.tensor_copy
-            rest(dst[:, split:P, :, :], src[:, split:P, :, :])
+            if g == 0:
+                nc.scalar.copy(dst[:, split:P, :, :], src[:, split:P, :, :])
+            else:
+                pairs = "p m j (u e) -> p u m j e"
+                nc.vector.tensor_copy(dst[:, split:P, :, :].rearrange(pairs, e=2), src[:, split:P, :, :].rearrange(pairs, e=2))
             return rounded
 
         def quantise_w1(g, rounded, t0):

@@ -32,7 +32,7 @@ LAST_SLICES = [128, 128, 128, 128, 256, 256]
 
 STRETCHES = [256, 256, 256, 128, 128]
 
-SCALAR_GROUPS = [96, 62]
+SCALAR_GROUPS = [96, 70]
 PRELOAD = 640
 LAST_PIECE = 1920
 SCALE_LOADS_AHEAD = 3
@@ -168,14 +168,18 @@ def tile_picked_zappnp_gelu_p_kernel(tc, x_words, x_scales, w1, w2_words, w2_sca
         x0_word = keep.tile([P, early_nodes], U32, name="x0_word", tag="w1_raw0", align_bytes=64)
         rounded = round_w1(0)
         quantise_w1(0, rounded, 0)
-        gather_words(0, x0_word[:, 0:BATCH], 0, BATCH)
+        x0_first = keep.tile([P, BATCH], U32, name="x0_first", tag="x0_first", align_bytes=64)
+        gather_words(0, x0_first[:], 0, BATCH)
         quantise_w1(0, rounded, 2)
         gather_words(0, x0_word[:, BATCH:SLICE], BATCH, BATCH)
         for first in range(SLICE, early_nodes, SLICE):
             gather_words(0, x0_word[:, first : first + SLICE], first, SLICE)
-        x0_batches.extend([x0_word[:, n0 : n0 + BATCH] for n0 in range(0, early_nodes, BATCH)])
+        x0_batches.append(x0_first[:])
+        x0_batches.extend([x0_word[:, n0 : n0 + BATCH] for n0 in range(BATCH, early_nodes, BATCH)])
         for u in range(2):
             first_layer_pass(0, half_banks[u], x0_batches[0], scale_batches[0], True, 2 * u)
+        scale_late = keep.tile([P, S - early_nodes], U8, name="scale_late", tag="x0_first", align_bytes=64)
+        scale_batches.extend(gather_scales(scale_late, early_nodes))
         for b in range(1, EARLY_BATCHES):
             first_layer_pass(0, h_banks[b], x0_batches[b], scale_batches[b], True)
         rounded = round_w1(1)
@@ -240,9 +244,7 @@ def tile_picked_zappnp_gelu_p_kernel(tc, x_words, x_scales, w1, w2_words, w2_sca
         firsts = [sum(STRETCHES[:i]) for i in range(len(STRETCHES))]
         early_stretches = len([f for f, w in zip(firsts, STRETCHES) if f + w <= early_nodes])
         hidden = [first_layer(first, width) for first, width in zip(firsts[:early_stretches], STRETCHES[:early_stretches])]
-        scale_late = keep.tile([P, S - early_nodes], U8, name="scale_late", tag=f"x1_word{slice_firsts[0]}", align_bytes=64)
-        scale_batches.extend(gather_scales(scale_late, early_nodes))
-        for first, freed in zip(range(early_nodes, S, BATCH), slice_firsts[1:]):
+        for first, freed in zip(range(early_nodes, S, BATCH), slice_firsts):
             tile = keep.tile([P, BATCH], U32, name=f"x0_word{first}", tag=f"x1_word{freed}", align_bytes=64)
             gather_words(0, tile[:], first, BATCH)
             x0_batches.append(tile[:])

from contextlib import ExitStack

import concourse.mybir as mybir

K, T, S, V, H, N, U = 1024, 2048, 1024, 512, 512, 128, 256
FLOPS = 2 * K * H * S + 2 * H * N * S

F32 = mybir.dt.float32
BF16 = mybir.dt.bfloat16
I32 = mybir.dt.int32
U32 = mybir.dt.uint32
U16 = mybir.dt.uint16
U8 = mybir.dt.uint8
FP8X4 = mybir.dt.float8_e4m3fn_x4
FP4X4 = mybir.dt.float4_e2m1fn_x4
MULT = mybir.AluOpType.mult
ADD = mybir.AluOpType.add
COPY = mybir.ActivationFunctionType.Copy
GELU = mybir.ActivationFunctionType.Gelu_apprx_tanh

P = 128
PACK = 4
K_PASS = P * PACK
PASSES = K // K_PASS
QUADRANTS = 4
LIST_ROWS = 16
BATCH = 128
SLICE = 256

EARLY_BATCHES = 6
LAST_SLICES = [128, 128, 128, 128, 256, 256]

STRETCHES = [256, 256, 256, 128, 128]

SCALAR_GROUPS = [96, 70]
PRELOAD = 640
LAST_PIECE = 1920
SCALE_LOADS_AHEAD = 3

OWN_PIECES = [(0, 256), (256, 192), (448, 64)]

NEAR = 0.8 * 0.8
CEN_OVER_NEAR = 0.2 / 0.8
ROOT_OVER_NEAR = 0.2 / NEAR


def tile_picked_zappnp_gelu_p_kernel(tc, x_words, x_scales, w1, w2_words, w2_scales, gate, gate2, offs, cen, pos1, pos2, pos3, nxt1, nxt2, nxt3, root, out):
    nc = tc.nc
    with ExitStack() as ctx:
        keep = ctx.enter_context(tc.tile_pool(name="keep", bufs=1))
        psum = ctx.enter_context(tc.psum_pool(name="psum", bufs=1))

        def bank_tile(index, shape):
            return psum.tile(shape, F32, name=f"bank{index}")

        def load_list(name, src):
            tile = keep.tile([P, src.shape[1]], U16, name=name)
            nc.sync.dma_start(tile[:], src)
            return tile

        def entries(list_tile, first, count):
            return list_tile[:, first // LIST_ROWS : (first + count) // LIST_ROWS]

        def w1_rows(g):
            return w1[K_PASS * g : K_PASS * (g + 1), :].rearrange("(p j) c -> p j c", j=PACK)

        def load_x_words(g):
            tile = keep.tile([P, T], I32, name=f"x_table{g}", align_bytes=64)
            nc.sync.dma_start(tile[:], x_words[g].rearrange("p n t -> p (n t)").bitcast(I32))
            return tile

        x_scale_table = keep.tile([P, T], U8, name="x_scale_table", align_bytes=64)
        nc.vector.memset(x_scale_table[:].bitcast(I32), 0)
        w2_scale = keep.tile([P, N], U8, name="w2_scale", align_bytes=64)
        nc.vector.memset(w2_scale[:].bitcast(I32), 0)

        warm_in = keep.tile([P, 1], F32, name="warm_in")
        nc.gpsimd.memset(warm_in[:], 0.0)
        warm_out = keep.tile([P, 1], F32, name="warm_out")
        nc.scalar.activation(warm_out[:], warm_in[:], GELU)

        offs_tile = load_list("offs_tile", offs)

        def load_scale_rows(loads):
            for r, g in loads:
                nc.sync.dma_start(x_scale_table[4 * g + r : P : 32, :].bitcast(I32), x_scales[g, r : 16 : 4, :].bitcast(I32))

        scale_loads = [(r, g) for r in range(4) for g in range(PASSES)]
        load_scale_rows(scale_loads[:SCALE_LOADS_AHEAD])
        w1_raw = [keep.tile([P, PACK, H], F32, name=f"w1_raw{g}", tag=f"w1_raw{g}", align_bytes=64) for g in range(PASSES)]
        flat_raw = w1_raw[0][:].rearrange("p j c -> p (j c)")
        flat_rows = w1_rows(0).rearrange("p j c -> p (j c)")
        nc.sync.dma_start(flat_raw[:, 0:PRELOAD], flat_rows[:, 0:PRELOAD])
        nc.sync.dma_start(flat_raw[:, PRELOAD:LAST_PIECE], flat_rows[:, PRELOAD:LAST_PIECE])
        load_scale_rows(scale_loads[SCALE_LOADS_AHEAD:])
        nc.sync.dma_start(flat_raw[:, LAST_PIECE : PACK * H], flat_rows[:, LAST_PIECE : PACK * H])
        x_table = [load_x_words(0)]
        nc.sync.dma_start(w1_raw[1][:], w1_rows(1))
        x_table.append(load_x_words(1))
        w2_word = keep.tile([P, 2 * N], U8, name="w2_word", align_bytes=64)
        nc.sync.dma_start(w2_word[:].bitcast(I32), w2_words[0].bitcast(I32))
        for q in range(QUADRANTS):
            nc.sync.dma_start(w2_scale[32 * q : 32 * q + 4, :].bitcast(I32), w2_scales[0, 4 * q : 4 * q + 4, :].bitcast(I32))
        pos_tiles = [load_list(f"pos{d + 1}_tile", src) for d, src in enumerate((pos1, pos2, pos3))]
        gate_tile = keep.tile([P, gate.shape[0], V], F32, name="gate_tile")
        nc.sync.dma_start(gate_tile[:], gate.rearrange("d p v -> p d v"))
        cen_tile = load_list("cen_tile", cen)
        nxt_tiles = [load_list(f"nxt{d + 1}_tile", src) for d, src in enumerate((nxt1, nxt2, nxt3))]
        root_tile = load_list("root_tile", root)
        gate2_tile = keep.tile([P, gate2.shape[0], U], F32, name="gate2_tile")
        nc.sync.dma_start(gate2_tile[:], gate2.rearrange("d p v -> p d v"))

        early_nodes = EARLY_BATCHES * BATCH

        def gather_scales(tile, first):
            count = tile.shape[1]
            nc.vector.tensor_copy(tile[:], x_scale_table[:].indirect(entries(offs_tile, first, count)))
            return [tile[:, n0 : n0 + BATCH] for n0 in range(0, count, BATCH)]

        scale_early = keep.tile([P, early_nodes], U8, name="scale_early", align_bytes=64)
        scale_batches = gather_scales(scale_early, 0)

        def gather_words(g, dst, first, count):
            nc.vector.tensor_copy(dst, x_table[g][:].bitcast(U32).indirect(entries(offs_tile, first, count)))

        w1_word = {}
        w1_scale = {}

        def round_w1(g):
            rounded = keep.tile([P, PACK, P, PACK], BF16, name=f"w1_rounded{g}", align_bytes=64)
            src = w1_raw[g][:].rearrange("p j (m t) -> p m j t", t=PACK)
            dst = rounded[:].rearrange("p t m j -> p m j t")
            split = SCALAR_GROUPS[g]
            nc.scalar.copy(dst[:, 0:split, :, :], src[:, 0:split, :, :])
            if g == 0:
                nc.scalar.copy(dst[:, split:P, :, :], src[:, split:P, :, :])
            else:
                pairs = "p m j (u e) -> p u m j e"
                nc.vector.tensor_copy(dst[:, split:P, :, :].rearrange(pairs, e=2), src[:, split:P, :, :].rearrange(pairs, e=2))
            return rounded

        def quantise_w1(g, rounded, t0):
            words = keep.tile([P, 2 * P], U32, name=f"w1_word{g}{t0}", align_bytes=64)
            scales = keep.tile([P, 2 * P], U8, name=f"w1_scale{g}{t0}", align_bytes=64)
            nc.vector.quantize_mx(out=words[:].bitcast(FP8X4), scales=scales[:], in_=rounded[:, t0 : t0 + 2, :, :].rearrange("p t m j -> p (t m j)"))
            for u in range(2):
                w1_word[(g, t0 + u)] = words[:, u * P : (u + 1) * P]
                w1_scale[(g, t0 + u)] = scales[:, u * P : (u + 1) * P]

        def first_layer_pass(g, bank, words, scales, opens, t0=0):
            tiles = bank.shape[1]
            for t in range(t0, t0 + tiles):
                nc.tensor.matmul_mx(
                    out=bank[:, t - t0, :],
                    lhsT=w1_word[(g, t)].bitcast(FP8X4),
                    lhsT_scale=w1_scale[(g, t)],
                    rhs=words.bitcast(FP8X4),
                    rhs_scale=scales[4 * g : P, :],
                    start=(opens and t == t0),
                    stop=(not opens and t == t0 + tiles - 1),
                )

        last_batch = S // BATCH - 1
        half_banks = [bank_tile(b, [P, 2, BATCH]) for b in (0, last_batch)]
        h_banks = {b: bank_tile(b, [P, PACK, BATCH]) for b in range(1, last_batch)}
        x0_batches = []

        x0_word = keep.tile([P, early_nodes], U32, name="x0_word", tag="w1_raw0", align_bytes=64)
        rounded = round_w1(0)
        quantise_w1(0, rounded, 0)
        x0_first = keep.tile([P, BATCH], U32, name="x0_first", tag="x0_first", align_bytes=64)
        gather_words(0, x0_first[:], 0, BATCH)
        quantise_w1(0, rounded, 2)
        gather_words(0, x0_word[:, BATCH:SLICE], BATCH, BATCH)
        for first in range(SLICE, early_nodes, SLICE):
            gather_words(0, x0_word[:, first : first + SLICE], first, SLICE)
        x0_batches.append(x0_first[:])
        x0_batches.extend([x0_word[:, n0 : n0 + BATCH] for n0 in range(BATCH, early_nodes, BATCH)])
        for u in range(2):
            first_layer_pass(0, half_banks[u], x0_batches[0], scale_batches[0], True, 2 * u)
        scale_late = keep.tile([P, S - early_nodes], U8, name="scale_late", tag="x0_first", align_bytes=64)
        scale_batches.extend(gather_scales(scale_late, early_nodes))
        for b in range(1, EARLY_BATCHES):
            first_layer_pass(0, h_banks[b], x0_batches[b], scale_batches[b], True)
        rounded = round_w1(1)
        for t0 in range(0, PACK, 2):
            quantise_w1(1, rounded, t0)

        y_near = keep.tile([P, S], F32, name="y_near")
        x1_batches = []
        slice_firsts = [sum(LAST_SLICES[:i]) for i in range(len(LAST_SLICES))]
        for first, count in zip(slice_firsts, LAST_SLICES):
            tile = keep.tile([P, count], U32, name=f"x1_word{first}", tag=f"x1_word{first}", align_bytes=64)
            gather_words(1, tile[:], first, count)
            x1_batches.extend([tile[:, n0 : n0 + BATCH] for n0 in range(0, count, BATCH)])

        def first_batch(h_rounded):
            halves = keep.tile([P, 2, BATCH, 2], BF16, name="h_halves", align_bytes=64)
            for u in range(2):
                first_layer_pass(1, half_banks[u], x1_batches[0], scale_batches[0], False, 2 * u)
                nc.scalar.activation(halves[:, u, :, :], half_banks[u][:].rearrange("p t n -> p n t"), GELU)
            pairs_in = halves[:].rearrange("p u n e -> p (u n e)").bitcast(I32).rearrange("p (u n) -> p n u", u=2)
            pairs_out = h_rounded.rearrange("p n t -> p (n t)").bitcast(I32).rearrange("p (n u) -> p n u", u=2)
            nc.vector.tensor_copy(pairs_out, pairs_in)

        def whole_batch(b, h_rounded):
            if b == last_batch:
                h_banks[b] = bank_tile(b, [P, PACK, BATCH])
            late = b >= EARLY_BATCHES
            first_layer_pass(1, h_banks[b], x1_batches[b], scale_batches[b], late)
            if late:
                first_layer_pass(0, h_banks[b], x0_batches[b], scale_batches[b], False)
            nc.scalar.activation(h_rounded, h_banks[b][:].rearrange("p t n -> p n t"), GELU)

        def first_layer(first, width):
            h_rounded = keep.tile([P, width, PACK], BF16, name=f"h_rounded{first}", align_bytes=64)
            for b0 in range(0, width, BATCH):
                b = (first + b0) // BATCH
                if b == 0:
                    first_batch(h_rounded[:, b0 : b0 + BATCH, :])
                else:
                    whole_batch(b, h_rounded[:, b0 : b0 + BATCH, :])
            return h_rounded

        def second_layer(index, first, width, h_rounded):
            h_word = keep.tile([P, width], U32, name=f"h_word{first}", align_bytes=64)
            h_scale = keep.tile([P, width], U8, name=f"h_scale{first}", align_bytes=64)
            nc.vector.quantize_mx(out=h_word[:].bitcast(FP8X4), scales=h_scale[:], in_=h_rounded[:].rearrange("p n t -> p (n t)"))
            bank = bank_tile(index, [P, width])
            nc.tensor.matmul_mx(
                out=bank[:],
                lhsT=w2_word[:].bitcast(FP4X4),
                lhsT_scale=w2_scale[:],
                rhs=h_word[:].bitcast(FP8X4),
                rhs_scale=h_scale[:],
                start=True,
                stop=True,
            )
            if index == len(STRETCHES) - 1:
                nc.vector.tensor_scalar(y_near[:, first : first + width], bank[:], NEAR, None, MULT)
            else:
                nc.scalar.activation(y_near[:, first : first + width], bank[:], COPY, scale=NEAR)

        firsts = [sum(STRETCHES[:i]) for i in range(len(STRETCHES))]
        early_stretches = len([f for f, w in zip(firsts, STRETCHES) if f + w <= early_nodes])
        hidden = [first_layer(first, width) for first, width in zip(firsts[:early_stretches], STRETCHES[:early_stretches])]
        for first, freed in zip(range(early_nodes, S, BATCH), slice_firsts):
            tile = keep.tile([P, BATCH], U32, name=f"x0_word{first}", tag=f"x1_word{freed}", align_bytes=64)
            gather_words(0, tile[:], first, BATCH)
            x0_batches.append(tile[:])
        hidden.extend([first_layer(first, width) for first, width in zip(firsts[early_stretches:], STRETCHES[early_stretches:])])
        for index in range(len(STRETCHES)):
            second_layer(index, firsts[index], STRETCHES[index], hidden[index])

        def fresh(name, width):
            return keep.tile([P, width], F32, name=name)

        def pick(name, table, list_tile, first, count, factor=1.0):
            tile = fresh(name, count)
            nc.scalar.activation(tile[:], table[:].indirect(entries(list_tile, first, count)), COPY, scale=factor)
            return tile[:]

        def pick_gated(dst, table, list_tile, first, gates):
            count = dst.shape[1]
            nc.vector.tensor_tensor(dst, table[:].indirect(entries(list_tile, first, count)), gates[:, first : first + count], MULT)
            return dst

        def combine(dst, a, b, op):
            nc.vector.tensor_tensor(dst, a, b, op)
            return dst

        z_half = V // 2
        z_starts = (0, z_half)
        second = [pick(f"picked1_{c0}", y_near, pos_tiles[1], c0, z_half) for c0 in z_starts]
        third = [pick(f"picked2_{c0}", y_near, pos_tiles[2], c0, z_half) for c0 in z_starts]
        own = [pick(f"cen{c0}", y_near, cen_tile, c0, width, CEN_OVER_NEAR) for c0, width in OWN_PIECES]
        root_term = pick("root_term", y_near, root_tile, 0, U, ROOT_OVER_NEAR)
        near0 = pick_gated(fresh("near0", V)[:], y_near, pos_tiles[0], 0, gate_tile[:, 0, :])
        near1 = [combine(fresh(f"near1_{c0}", z_half)[:], src, gate_tile[:, 1, c0 : c0 + z_half], MULT) for c0, src in zip(z_starts, second)]
        first_two = []
        near2 = []
        for c0, a, src in zip(z_starts, near1, third):
            first_two.append(combine(fresh(f"sum1_{c0}", z_half)[:], near0[:, c0 : c0 + z_half], a, ADD))
            near2.append(combine(fresh(f"near2_{c0}", z_half)[:], src, gate_tile[:, 2, c0 : c0 + z_half], MULT))
        neighbours = fresh("neighbours", V)
        for c0, a, b in zip(z_starts, first_two, near2):
            combine(neighbours[:, c0 : c0 + z_half], a, b, ADD)
        z_near = fresh("z_near", V)
        for (c0, width), term in zip(OWN_PIECES, own):
            combine(z_near[:, c0 : c0 + width], neighbours[:, c0 : c0 + width], term, ADD)

        out_half = U // 2
        out_starts = (0, out_half)
        onward = [[pick(f"onward{d}_{c0}", z_near, nxt_tiles[d], c0, out_half) for c0 in out_starts] for d in (1, 2)]
        total = [pick_gated(fresh(f"onward0_{c0}", out_half)[:], z_near, nxt_tiles[0], c0, gate2_tile[:, 0, :]) for c0 in out_starts]
        total = [combine(fresh(f"with_root{c0}", out_half)[:], a, root_term[:, c0 : c0 + out_half], ADD) for c0, a in zip(out_starts, total)]
        result = fresh("result", U)
        for d in (1, 2):
            terms = [combine(fresh(f"far{d}_{c0}", out_half)[:], src, gate2_tile[:, d, c0 : c0 + out_half], MULT) for c0, src in zip(out_starts, onward[d - 1])]
            total = [combine(result[:, c0 : c0 + out_half] if d == 2 else fresh(f"far_sum{c0}", out_half)[:], a, b, ADD) for c0, a, b in zip(out_starts, total, terms)]
        for c0 in out_starts:
            nc.sync.dma_start(out[:, c0 : c0 + out_half], result[:, c0 : c0 + out_half])
